import numpy as np
import ml_dtypes


def mxq(x, axis, fmt="e4m3"):
    dtype, down = {"e4m3": (ml_dtypes.float8_e4m3fn, 7), "e5m2": (ml_dtypes.float8_e5m2, 14)}[fmt]
    v = np.moveaxis(np.asarray(x, np.float32).astype(ml_dtypes.bfloat16).astype(np.float64), axis, -1)
    blocks = v.reshape(v.shape[:-1] + (-1, 32))
    amax = np.abs(blocks).max(-1, keepdims=True)
    byte = np.maximum(np.where(amax > 0, np.frexp(amax)[1] - 1 + 127, 0) - down, 1)
    scale = np.exp2(byte - 127.0)
    codes = (blocks / scale).astype(np.float32).astype(dtype).astype(np.float64)
    return np.moveaxis((codes * scale).reshape(v.shape), -1, axis)


WIDE = False


def mx_kscale(k):
    if not WIDE:
        return np.ones(k)
    levels = np.array([10, -10, 5, -5, 0])
    if k % 512:
        return np.exp2(np.random.permutation(np.resize(levels, k // 32))).repeat(32)
    a = np.empty((k // 512, 16))
    for p in range(k // 512):
        a[p, :8] = np.random.permutation(np.resize(levels, 8))
        for g in range(8):
            far = levels[np.abs(levels - a[p, g]) >= 10]
            a[p, g + 8] = far[np.random.randint(len(far))]
    return np.exp2(a.ravel()).repeat(32)


def f64(x):
    return np.asarray(x).astype(np.float64)


def striped(idx):
    return np.tile(idx.reshape(-1, 16).T, (8, 1)).astype(np.uint16)


def unstriped(offs):
    return offs[:16].T.reshape(-1).astype(np.int64)


def striped8(idx):
    return np.concatenate([x.reshape(-1, 16).T for x in idx]).astype(np.uint16)


def runs(offs, k):
    lists = np.stack([offs[16 * r : 16 * r + 16].T.reshape(-1) for r in range(8)]).astype(np.int64)
    return lists[np.arange(k) % 512 // 64]


def pack_weight(w):
    k, n = w.shape
    w = f64(np.asarray(w, np.float32).astype(ml_dtypes.bfloat16)).reshape(k // 32, 32, n)
    amax = np.abs(w).max(1)
    byte = np.clip(np.where(amax > 0, np.frexp(amax)[1] - 1 + 127 - 7, 1), 1, 254)
    scaled = (w * np.exp2(127.0 - byte)[:, None, :]).reshape(k, n).astype(np.float32)
    words = np.ascontiguousarray(scaled.reshape(k // 512, 128, 4, n).transpose(0, 1, 3, 2)).astype(ml_dtypes.float8_e4m3fn).view(np.uint8)
    return words, np.ascontiguousarray(byte.astype(np.uint8).reshape(k // 512, 16, n))


def unpack_weight(words, scales):
    g, p, n, _ = words.shape
    vals = np.ascontiguousarray(words).view(ml_dtypes.float8_e4m3fn).astype(np.float64) * np.repeat(np.exp2(scales.astype(np.float64) - 127.0), 8, axis=1)[..., None]
    return vals.transpose(0, 1, 3, 2).reshape(g * 512, n)


E2M1 = np.array([0.0, 0.5, 1.0, 1.5, 2.0, 3.0, 4.0, 6.0, -0.0, -0.5, -1.0, -1.5, -2.0, -3.0, -4.0, -6.0])


def pack_fp4(w):
    k, n = w.shape
    w = f64(np.asarray(w, np.float32).astype(ml_dtypes.bfloat16)).reshape(k // 32, 32, n)
    amax = np.abs(w).max(1)
    mant, ex = np.frexp(amax / 6.0)
    byte = np.clip(np.where(amax > 0, np.where(mant > 0.5, ex, ex - 1) + 127, 1), 1, 254)
    scaled = (w * np.exp2(127.0 - byte)[:, None, :]).reshape(k, n).astype(np.float32)
    c = np.ascontiguousarray(scaled.reshape(k // 512, 128, 4, n).transpose(0, 1, 3, 2)).astype(ml_dtypes.float4_e2m1fn).view(np.uint8) & 0xF
    words = (c[..., 0::2] | (c[..., 1::2] << 4)).reshape(k // 512, 128, 2 * n)
    return np.ascontiguousarray(words), np.ascontiguousarray(byte.astype(np.uint8).reshape(k // 512, 16, n))


def unpack_fp4(words, scales):
    g, _, n = scales.shape
    words = np.ascontiguousarray(words).reshape(g, 128, n, 2)
    nib = np.empty((g, 128, n, 4), np.uint8)
    nib[..., 0::2] = words & 0xF
    nib[..., 1::2] = words >> 4
    vals = E2M1[nib] * np.repeat(np.exp2(scales.astype(np.float64) - 127.0), 8, axis=1)[..., None]
    return vals.transpose(0, 1, 3, 2).reshape(g * 512, n)


def planes(y):
    n, m = y.shape
    v = y.astype(np.float32).astype(ml_dtypes.bfloat16).astype(np.float64).reshape(n // 32, 32, m)
    top = np.abs(v).max(1)
    byte = np.clip(np.where(top > 0, np.frexp(top)[1] - 1 + 127 - 7, 1), 1, 254)
    codes = (v * np.exp2(127.0 - byte)[:, None, :]).reshape(n, m).astype(np.float32).astype(ml_dtypes.float8_e4m3fn).view(np.uint8)
    words = codes.reshape(n // 512, 128, 4, m).transpose(0, 1, 3, 2)
    return np.ascontiguousarray(words), np.ascontiguousarray(byte.astype(np.uint8).reshape(n // 512, 16, m))


K, T, S, V, N, H = 512, 2048, 512, 256, 512, 512


def setup_inputs():
    n = np.random.standard_normal
    s = mx_kscale(K)[:, None]
    u = mx_kscale(H)
    packed_xT = pack_weight(n((K, T)) * s)
    packed_w2 = pack_fp4(n((H, N)) / np.sqrt(H) / u[:, None])
    return {
        "x_words": packed_xT[0],
        "x_scales": packed_xT[1],
        "w1": (n((K, H)) / np.sqrt(K) / s * u).astype(np.float32),
        "ln": (np.repeat(np.random.uniform(0.1, 1.0, (8, V)), 64, axis=0) * u[:, None]).astype(np.float32),
        "w2_words": packed_w2[0],
        "w2_scales": packed_w2[1],
        "offs": striped(np.random.permutation(T)[:S]),
        "src": striped8(np.stack([np.random.permutation(S)[:V] for _ in range(8)])),
        "dst": striped8(np.stack([np.random.permutation(S)[:V] for _ in range(8)])),
    }


def reference(x_words, x_scales, w1, ln, w2_words, w2_scales, offs, src, dst):
    xq = unpack_weight(x_words, x_scales)[:, unstriped(offs)]
    y = mxq(f64(w1), 0, "e4m3").T @ xq
    m1 = np.minimum(y[np.arange(H)[:, None], runs(dst, H)], y[np.arange(H)[:, None], runs(src, H)] + f64(ln))
    z = y.copy()
    z[np.arange(H)[:, None], runs(dst, H)] = m1
    out_0 = unpack_fp4(w2_words, w2_scales).T @ mxq(z, 0, "e4m3")
    return (out_0,) + planes(out_0)

@@ -1,0 +1,186 @@
+from contextlib import ExitStack
+
+import concourse.mybir as mybir
+
+K, T, S, V, H, N = 512, 2048, 512, 256, 512, 512
+FLOPS = 2 * K * H * S + 2 * H * N * S
+
+F32 = mybir.dt.float32
+BF16 = mybir.dt.bfloat16
+I32 = mybir.dt.int32
+U32 = mybir.dt.uint32
+U16 = mybir.dt.uint16
+U8 = mybir.dt.uint8
+FP8X4 = mybir.dt.float8_e4m3fn_x4
+FP4X4 = mybir.dt.float4_e2m1fn_x4
+ADD = mybir.AluOpType.add
+MIN = mybir.AluOpType.min
+
+P = 128
+PACK = 4
+QUADS = 4
+M = 128
+CHUNKS = 4
+C = S // CHUNKS
+
+
+def tile_picked_bellman_none_po_kernel(
+    tc, x_words, x_scales, w1, ln, w2_words, w2_scales, offs, src, dst, out_0, out_1, out_2
+):
+    nc = tc.nc
+    with ExitStack() as ctx:
+        lists = ctx.enter_context(tc.tile_pool(name="lists", bufs=1))
+        sb = ctx.enter_context(tc.tile_pool(name="sb", bufs=1))
+        ps = ctx.enter_context(tc.psum_pool(name="ps", bufs=1))
+
+        offs_t = lists.tile([P, S // 16], U16, name="offs_t")
+        src_t = lists.tile([P, V // 16], U16, name="src_t")
+        dst_t = lists.tile([P, V // 16], U16, name="dst_t")
+
+        x_codes = sb.tile([P, T], I32, name="x_codes", align_bytes=64)
+        x_bytes = sb.tile([P, T], U8, name="x_bytes", align_bytes=64)
+        w1_raw = sb.tile([P, PACK, H], F32, name="w1_raw", align_bytes=64)
+        ln_t = sb.tile([P, PACK, V], F32, name="ln_t", align_bytes=64)
+        w2_raw = sb.tile([P, 2 * N], U8, name="w2_raw", align_bytes=64)
+        w2_bytes = sb.tile([P, N], U8, name="w2_bytes", align_bytes=64)
+
+        nc.vector.memset(x_bytes[:].bitcast(I32), 0)
+        nc.gpsimd.memset(w2_bytes[:].bitcast(I32), 0)
+        nc.sync.dma_start(offs_t[:], offs)
+        nc.sync.dma_start(w1_raw[:], w1.rearrange("(p j) c -> p j c", j=PACK))
+        for q in range(QUADS):
+            nc.scalar.dma_start(
+                x_bytes[32 * q : 32 * q + 4, :].bitcast(I32), x_scales[0, 4 * q : 4 * q + 4, :].bitcast(I32)
+            )
+        nc.sync.dma_start(src_t[:], src)
+        nc.sync.dma_start(dst_t[:], dst)
+        nc.sync.dma_start(x_codes[:], x_words[0].rearrange("p n t -> p (n t)").bitcast(I32))
+        nc.sync.dma_start(w2_raw[:].bitcast(I32), w2_words[0].bitcast(I32))
+        nc.sync.dma_start(ln_t[:], ln.rearrange("(p t) v -> p t v", t=PACK))
+        for q in range(QUADS):
+            nc.gpsimd.dma_start(
+                w2_bytes[32 * q : 32 * q + 4, :].bitcast(I32), w2_scales[0, 4 * q : 4 * q + 4, :].bitcast(I32)
+            )
+
+        picked_bytes = sb.tile([P, S], U8, name="picked_bytes", align_bytes=64)
+        nc.vector.tensor_copy(picked_bytes[:], x_bytes[:].indirect(offs_t[:]))
+
+        w1_cols = w1_raw[:].rearrange("p j (m t) -> p m j t", t=PACK)
+        w1_bf, w1_codes, w1_scale = [], [], []
+        for u in range(2):
+            w1_bf.append(sb.tile([P, 2 * M * PACK], BF16, name=f"w1_bf{u}", align_bytes=64))
+            w1_codes.append(sb.tile([P, 2 * M], U32, name=f"w1_codes{u}", align_bytes=64))
+            w1_scale.append(sb.tile([P, 2 * M], U8, name=f"w1_scale{u}", align_bytes=64))
+        dealt = [w1_bf[u][:].rearrange("p (t m j) -> p m j t", t=2, j=PACK) for u in range(2)]
+        nc.vector.tensor_copy(dealt[0], w1_cols[:, :, :, 0:2])
+        nc.scalar.copy(dealt[1], w1_cols[:, :, :, 2:4])
+        for u in range(2):
+            nc.vector.quantize_mx(out=w1_codes[u][:].bitcast(FP8X4), scales=w1_scale[u][:], in_=w1_bf[u][:])
+
+        picked_codes = sb.tile([P, S], U32, name="picked_codes", align_bytes=64)
+        half = S // 2
+        for h in range(2):
+            nc.vector.tensor_copy(
+                picked_codes[:, h * half : (h + 1) * half],
+                x_codes[:].bitcast(U32).indirect(offs_t[:, h * half // 16 : (h + 1) * half // 16]),
+            )
+
+        y = [sb.tile([P, S], F32, name=f"y{t}", align_bytes=64) for t in range(PACK)]
+        pieces = [(0, 0, half), (0, half, S)] + [(t, 0, S) for t in range(1, PACK)]
+        for b, (t, c0, c1) in enumerate(pieces):
+            acc = ps.tile([M, c1 - c0], F32, name=f"acc{b}", tag=f"bank{b}")
+            cols = slice((t % 2) * M, (t % 2 + 1) * M)
+            nc.tensor.matmul_mx(
+                out=acc[:],
+                lhsT=w1_codes[t // 2][:, cols].bitcast(FP8X4),
+                lhsT_scale=w1_scale[t // 2][:, cols],
+                rhs=picked_codes[:, c0:c1].bitcast(FP8X4),
+                rhs_scale=picked_bytes[:, c0:c1],
+                start=True,
+                stop=True,
+            )
+            nc.scalar.copy(y[t][:, c0:c1], acc[:])
+
+        w2_codes = sb.tile([P, 2 * N], U8, name="w2_codes", align_bytes=64)
+        w2_scale = sb.tile([P, N], U8, name="w2_scale", align_bytes=64)
+        nc.vector.tensor_copy(
+            w2_scale[:].rearrange("p (t m) -> p m t", t=PACK), w2_bytes[:].rearrange("p (m t) -> p m t", t=PACK)
+        )
+        nc.vector.tensor_copy(
+            w2_codes[:].rearrange("p (t m b) -> p m t b", t=PACK, b=2),
+            w2_raw[:].rearrange("p (m t b) -> p m t b", t=PACK, b=2),
+        )
+
+        old = sb.tile([P, PACK, V], F32, name="old", align_bytes=64)
+        new = sb.tile([P, PACK, V], F32, name="new", align_bytes=64)
+
+        def fetch_old(t):
+            nc.vector.tensor_copy(old[:, t, :], y[t][:].indirect(dst_t[:]))
+
+        def fetch_new(t):
+            nc.vector.tensor_tensor(new[:, t, :], y[t][:].indirect(src_t[:]), ln_t[:, t, :], ADD)
+
+        for t in range(PACK - 1):
+            fetch_old(t)
+            fetch_new(t)
+        fetch_new(PACK - 1)
+        fetch_old(PACK - 1)
+        nc.vector.tensor_tensor(ln_t[:, 2:4, :], old[:, 0:2, :], new[:, 0:2, :], MIN)
+        nc.vector.tensor_tensor(ln_t[:, 0:2, :], old[:, 2:4, :], new[:, 2:4, :], MIN)
+
+        z_bf = sb.tile([P, S, PACK], BF16, name="z_bf", align_bytes=64)
+        for t in range(PACK):
+            nc.vector.tensor_copy(y[t][:].indirect(dst_t[:]), ln_t[:, (t + 2) % PACK, :])
+            if t < PACK - 1:
+                nc.scalar.copy(z_bf[:, :, t], y[t][:])
+
+        z_codes = sb.tile([P, S], U32, name="z_codes", align_bytes=64)
+        z_scale = sb.tile([P, S], U8, name="z_scale", align_bytes=64)
+        out_codes = sb.tile([P, S], I32, name="out_codes", align_bytes=64)
+        out_scale = sb.tile([P, S], U8, name="out_scale", align_bytes=64)
+        z_flat = z_bf[:].rearrange("p c t -> p (c t)")
+        out_rows = out_0.rearrange("(p t) c -> p t c", t=PACK)
+        out_words = out_1[0].rearrange("p n t -> p (n t)").bitcast(I32)
+
+        accs = []
+        for i in range(CHUNKS):
+            cols = slice(i * C, (i + 1) * C)
+            nc.scalar.copy(z_bf[:, cols, PACK - 1], y[PACK - 1][:, cols])
+            nc.vector.quantize_mx(
+                out=z_codes[:, cols].bitcast(FP8X4),
+                scales=z_scale[:, cols],
+                in_=z_flat[:, i * C * PACK : (i + 1) * C * PACK],
+            )
+            acc = ps.tile([M, PACK, C], F32, name=f"out_acc{i}", tag=f"bank{(5 + i) % 8}")
+            accs.append(acc)
+            for t in range(PACK):
+                nc.tensor.matmul_mx(
+                    out=acc[:, t, :],
+                    lhsT=w2_codes[:, 2 * M * t : 2 * M * (t + 1)].bitcast(FP4X4),
+                    lhsT_scale=w2_scale[:, M * t : M * (t + 1)],
+                    rhs=z_codes[:, cols].bitcast(FP8X4),
+                    rhs_scale=z_scale[:, cols],
+                    start=True,
+                    stop=True,
+                )
+
+        for i in range(CHUNKS):
+            cols = slice(i * C, (i + 1) * C)
+            res = sb.tile([P, PACK, C], F32, name=f"res{i}", align_bytes=64)
+            nc.scalar.copy(res[:], accs[i][:])
+            nc.sync.dma_start(out_rows[:, :, cols], res[:])
+            res_bf = sb.tile([P, C, PACK], BF16, name=f"res_bf{i}", align_bytes=64)
+            nc.vector.tensor_copy(
+                res_bf[:].rearrange("p (c i) t -> p c t i", i=4), res[:].rearrange("p t (c i) -> p c t i", i=4)
+            )
+            nc.vector.quantize_mx(
+                out=out_codes[:, cols].bitcast(FP8X4),
+                scales=out_scale[:, cols],
+                in_=res_bf[:].rearrange("p c t -> p (c t)"),
+            )
+            if i == CHUNKS - 2:
+                nc.sync.dma_start(out_words[:, : (i + 1) * C], out_codes[:, : (i + 1) * C])
+        nc.sync.dma_start(out_words[:, S - C :], out_codes[:, S - C :])
+        for q in range(QUADS):
+            eng = nc.scalar if q % 2 else nc.sync
+            eng.dma_start(out_2[0, 4 * q : 4 * q + 4, :].bitcast(I32), out_scale[32 * q : 32 * q + 4, :].bitcast(I32))

@@ -38,44 +38,42 @@ def tile_picked_bellman_none_po_kernel(
         dst_t = lists.tile([P, V // 16], U16, name="dst_t")
 
         x_codes = sb.tile([P, T], I32, name="x_codes", align_bytes=64)
-        x_bytes = sb.tile([P, T], U8, name="x_bytes", align_bytes=64)
+        x_bytes = sb.tile([P, T], U8, name="x_bytes", tag="x_bytes", align_bytes=64)
         w1_raw = sb.tile([P, PACK, H], F32, name="w1_raw", align_bytes=64)
         ln_t = sb.tile([P, PACK, V], F32, name="ln_t", align_bytes=64)
         w2_raw = sb.tile([P, 2 * N], U8, name="w2_raw", align_bytes=64)
         w2_bytes = sb.tile([P, N], U8, name="w2_bytes", align_bytes=64)
 
-        nc.vector.memset(x_bytes[:].bitcast(I32), 0)
+        nc.gpsimd.memset(x_bytes[:].bitcast(I32), 0)
         nc.gpsimd.memset(w2_bytes[:].bitcast(I32), 0)
-        nc.sync.dma_start(offs_t[:], offs)
         nc.sync.dma_start(w1_raw[:], w1.rearrange("(p j) c -> p j c", j=PACK))
+        nc.sync.dma_start(offs_t[:], offs)
         for q in range(QUADS):
-            nc.scalar.dma_start(
+            nc.sync.dma_start(
                 x_bytes[32 * q : 32 * q + 4, :].bitcast(I32), x_scales[0, 4 * q : 4 * q + 4, :].bitcast(I32)
             )
-        nc.sync.dma_start(src_t[:], src)
         nc.sync.dma_start(dst_t[:], dst)
         nc.sync.dma_start(x_codes[:], x_words[0].rearrange("p n t -> p (n t)").bitcast(I32))
+        nc.sync.dma_start(src_t[:], src)
         nc.sync.dma_start(w2_raw[:].bitcast(I32), w2_words[0].bitcast(I32))
         nc.sync.dma_start(ln_t[:], ln.rearrange("(p t) v -> p t v", t=PACK))
         for q in range(QUADS):
-            nc.gpsimd.dma_start(
+            nc.sync.dma_start(
                 w2_bytes[32 * q : 32 * q + 4, :].bitcast(I32), w2_scales[0, 4 * q : 4 * q + 4, :].bitcast(I32)
             )
+
 
         picked_bytes = sb.tile([P, S], U8, name="picked_bytes", align_bytes=64)
         nc.vector.tensor_copy(picked_bytes[:], x_bytes[:].indirect(offs_t[:]))
 
+        w1_codes = sb.tile([P, H], U32, name="w1_codes", tag="x_bytes", align_bytes=64)
+        w1_scale = sb.tile([P, H], U8, name="w1_scale", align_bytes=64)
         w1_cols = w1_raw[:].rearrange("p j (m t) -> p m j t", t=PACK)
-        w1_bf, w1_codes, w1_scale = [], [], []
-        for u in range(2):
-            w1_bf.append(sb.tile([P, 2 * M * PACK], BF16, name=f"w1_bf{u}", align_bytes=64))
-            w1_codes.append(sb.tile([P, 2 * M], U32, name=f"w1_codes{u}", align_bytes=64))
-            w1_scale.append(sb.tile([P, 2 * M], U8, name=f"w1_scale{u}", align_bytes=64))
-        dealt = [w1_bf[u][:].rearrange("p (t m j) -> p m j t", t=2, j=PACK) for u in range(2)]
-        nc.vector.tensor_copy(dealt[0], w1_cols[:, :, :, 0:2])
-        nc.scalar.copy(dealt[1], w1_cols[:, :, :, 2:4])
-        for u in range(2):
-            nc.vector.quantize_mx(out=w1_codes[u][:].bitcast(FP8X4), scales=w1_scale[u][:], in_=w1_bf[u][:])
+        for u, copy in enumerate((nc.vector.tensor_copy, nc.scalar.copy)):
+            w1_bf = sb.tile([P, 2 * M * PACK], BF16, name=f"w1_bf{u}", align_bytes=64)
+            copy(w1_bf[:].rearrange("p (t m j) -> p m j t", t=2, j=PACK), w1_cols[:, :, :, 2 * u : 2 * u + 2])
+            cols = slice(2 * u * M, 2 * (u + 1) * M)
+            nc.vector.quantize_mx(out=w1_codes[:, cols].bitcast(FP8X4), scales=w1_scale[:, cols], in_=w1_bf[:])
 
         picked_codes = sb.tile([P, S], U32, name="picked_codes", align_bytes=64)
         half = S // 2
@@ -85,15 +83,16 @@ def tile_picked_bellman_none_po_kernel(
                 x_codes[:].bitcast(U32).indirect(offs_t[:, h * half // 16 : (h + 1) * half // 16]),
             )
 
-        y = [sb.tile([P, S], F32, name=f"y{t}", align_bytes=64) for t in range(PACK)]
-        pieces = [(0, 0, half), (0, half, S)] + [(t, 0, S) for t in range(1, PACK)]
+        order = (0, 2, 3, 1)
+        y = [sb.tile([P, S], F32, name=f"y{t}", tag=f"y{t}", align_bytes=64) for t in range(PACK)]
+        pieces = [(0, 0, half), (0, half, S)] + [(t, 0, S) for t in order[1:]]
         for b, (t, c0, c1) in enumerate(pieces):
             acc = ps.tile([M, c1 - c0], F32, name=f"acc{b}", tag=f"bank{b}")
-            cols = slice((t % 2) * M, (t % 2 + 1) * M)
+            cols = slice(t * M, (t + 1) * M)
             nc.tensor.matmul_mx(
                 out=acc[:],
-                lhsT=w1_codes[t // 2][:, cols].bitcast(FP8X4),
-                lhsT_scale=w1_scale[t // 2][:, cols],
+                lhsT=w1_codes[:, cols].bitcast(FP8X4),
+                lhsT_scale=w1_scale[:, cols],
                 rhs=picked_codes[:, c0:c1].bitcast(FP8X4),
                 rhs_scale=picked_bytes[:, c0:c1],
                 start=True,
@@ -102,37 +101,47 @@ def tile_picked_bellman_none_po_kernel(
             nc.scalar.copy(y[t][:, c0:c1], acc[:])
 
         w2_codes = sb.tile([P, 2 * N], U8, name="w2_codes", align_bytes=64)
-        w2_scale = sb.tile([P, N], U8, name="w2_scale", align_bytes=64)
-        nc.vector.tensor_copy(
-            w2_scale[:].rearrange("p (t m) -> p m t", t=PACK), w2_bytes[:].rearrange("p (m t) -> p m t", t=PACK)
-        )
         nc.vector.tensor_copy(
             w2_codes[:].rearrange("p (t m b) -> p m t b", t=PACK, b=2),
             w2_raw[:].rearrange("p (m t b) -> p m t b", t=PACK, b=2),
         )
 
+        w2_scale = sb.tile([P, N], U8, name="w2_scale", align_bytes=64)
+        nc.vector.tensor_copy(
+            w2_scale[:].rearrange("p (t m) -> p m t", t=PACK), w2_bytes[:].rearrange("p (m t) -> p m t", t=PACK)
+        )
+
         old = sb.tile([P, PACK, V], F32, name="old", align_bytes=64)
         new = sb.tile([P, PACK, V], F32, name="new", align_bytes=64)
 
-        def fetch_old(t):
-            nc.vector.tensor_copy(old[:, t, :], y[t][:].indirect(dst_t[:]))
+        def fetch_old(i):
+            nc.vector.tensor_copy(old[:, i, :], y[order[i]][:].indirect(dst_t[:]))
 
-        def fetch_new(t):
-            nc.vector.tensor_tensor(new[:, t, :], y[t][:].indirect(src_t[:]), ln_t[:, t, :], ADD)
+        def fetch_new(i):
+            nc.vector.tensor_tensor(new[:, i, :], y[order[i]][:].indirect(src_t[:]), ln_t[:, order[i], :], ADD)
 
-        for t in range(PACK - 1):
-            fetch_old(t)
-            fetch_new(t)
+        for i in range(PACK - 1):
+            fetch_old(i)
+            fetch_new(i)
         fetch_new(PACK - 1)
         fetch_old(PACK - 1)
-        nc.vector.tensor_tensor(ln_t[:, 2:4, :], old[:, 0:2, :], new[:, 0:2, :], MIN)
-        nc.vector.tensor_tensor(ln_t[:, 0:2, :], old[:, 2:4, :], new[:, 2:4, :], MIN)
+        nc.vector.tensor_tensor(ln_t[:, 1::2, :], old[:, 0:2, :], new[:, 0:2, :], MIN)
+        nc.vector.tensor_tensor(new[:, 2:4, :], old[:, 2:4, :], new[:, 2:4, :], MIN)
+        relaxed = [ln_t[:, 1, :], ln_t[:, 3, :], new[:, 2, :], new[:, 3, :]]
 
         z_bf = sb.tile([P, S, PACK], BF16, name="z_bf", align_bytes=64)
-        for t in range(PACK):
-            nc.vector.tensor_copy(y[t][:].indirect(dst_t[:]), ln_t[:, (t + 2) % PACK, :])
-            if t < PACK - 1:
-                nc.scalar.copy(z_bf[:, :, t], y[t][:])
+        last = order[PACK - 1]
+        for i in range(PACK - 1):
+            t = order[i]
+            nc.vector.tensor_copy(y[t][:].indirect(dst_t[:]), relaxed[i])
+            for h in range(2):
+                cols = slice(h * half, (h + 1) * half)
+                nc.scalar.copy(z_bf[:, cols, t], y[t][:, cols])
+            if i == 0:
+                z_last = sb.tile([P, S], F32, name="z_last", tag="y0", align_bytes=64)
+                nc.scalar.copy(z_last[:], y[last][:])
+
+        nc.vector.tensor_copy(z_last[:].indirect(dst_t[:]), relaxed[PACK - 1])
 
         z_codes = sb.tile([P, S], U32, name="z_codes", align_bytes=64)
         z_scale = sb.tile([P, S], U8, name="z_scale", align_bytes=64)
@@ -142,20 +151,26 @@ def tile_picked_bellman_none_po_kernel(
         out_rows = out_0.rearrange("(p t) c -> p t c", t=PACK)
         out_words = out_1[0].rearrange("p n t -> p (n t)").bitcast(I32)
 
-        accs = []
-        for i in range(CHUNKS):
-            cols = slice(i * C, (i + 1) * C)
-            nc.scalar.copy(z_bf[:, cols, PACK - 1], y[PACK - 1][:, cols])
+        def quantize(codes, scale, values, c0, c1):
             nc.vector.quantize_mx(
-                out=z_codes[:, cols].bitcast(FP8X4),
-                scales=z_scale[:, cols],
-                in_=z_flat[:, i * C * PACK : (i + 1) * C * PACK],
+                out=codes[:, c0:c1].bitcast(FP8X4), scales=scale[:, c0:c1], in_=values[:, c0 * PACK : c1 * PACK]
             )
-            acc = ps.tile([M, PACK, C], F32, name=f"out_acc{i}", tag=f"bank{(5 + i) % 8}")
-            accs.append(acc)
+
+        for h in range(2):
+            for c0 in (h * half, h * half + C):
+                nc.vector.tensor_copy(z_bf[:, c0 : c0 + C, last], z_last[:, c0 : c0 + C])
+            for c0 in (h * half, h * half + C):
+                quantize(z_codes, z_scale, z_flat, c0, c0 + C)
+
+        res_bf = sb.tile([P, S, PACK], BF16, name="res_bf", align_bytes=64)
+        res_flat = res_bf[:].rearrange("p c t -> p (c t)")
+        for h in range(2):
+            cols = slice(h * half, (h + 1) * half)
+            res = sb.tile([P, PACK, half], F32, name=f"res{h}", align_bytes=64)
             for t in range(PACK):
+                acc = ps.tile([M, half], F32, name=f"out_acc{h}{t}", tag=f"bank{h * PACK + t}")
                 nc.tensor.matmul_mx(
-                    out=acc[:, t, :],
+                    out=acc[:],
                     lhsT=w2_codes[:, 2 * M * t : 2 * M * (t + 1)].bitcast(FP4X4),
                     lhsT_scale=w2_scale[:, M * t : M * (t + 1)],
                     rhs=z_codes[:, cols].bitcast(FP8X4),
@@ -163,24 +178,20 @@ def tile_picked_bellman_none_po_kernel(
                     start=True,
                     stop=True,
                 )
-
-        for i in range(CHUNKS):
-            cols = slice(i * C, (i + 1) * C)
-            res = sb.tile([P, PACK, C], F32, name=f"res{i}", align_bytes=64)
-            nc.scalar.copy(res[:], accs[i][:])
-            nc.sync.dma_start(out_rows[:, :, cols], res[:])
-            res_bf = sb.tile([P, C, PACK], BF16, name=f"res_bf{i}", align_bytes=64)
-            nc.vector.tensor_copy(
-                res_bf[:].rearrange("p (c i) t -> p c t i", i=4), res[:].rearrange("p t (c i) -> p c t i", i=4)
-            )
-            nc.vector.quantize_mx(
-                out=out_codes[:, cols].bitcast(FP8X4),
-                scales=out_scale[:, cols],
-                in_=res_bf[:].rearrange("p c t -> p (c t)"),
-            )
-            if i == CHUNKS - 2:
-                nc.sync.dma_start(out_words[:, : (i + 1) * C], out_codes[:, : (i + 1) * C])
-        nc.sync.dma_start(out_words[:, S - C :], out_codes[:, S - C :])
+                if h == 0 and t % 2:
+                    nc.vector.tensor_copy(res[:, t, :], acc[:])
+                else:
+                    nc.scalar.copy(res[:, t, :], acc[:])
+                if t % 2:
+                    nc.sync.dma_start(out_rows[:, t - 1 : t + 1, cols], res[:, t - 1 : t + 1, :])
+            for i in range(2):
+                nc.vector.tensor_copy(
+                    res_bf[:, h * half + i * C : h * half + (i + 1) * C, :].rearrange("p (c i) t -> p c t i", i=4),
+                    res[:, :, i * C : (i + 1) * C].rearrange("p t (c i) -> p c t i", i=4),
+                )
+            for i in range(2):
+                quantize(out_codes, out_scale, res_flat, h * half + i * C, h * half + (i + 1) * C)
+            nc.sync.dma_start(out_words[:, cols], out_codes[:, cols])
         for q in range(QUADS):
-            eng = nc.scalar if q % 2 else nc.sync
+            eng = nc.sync if q % 2 else nc.scalar
             eng.dma_start(out_2[0, 4 * q : 4 * q + 4, :].bitcast(I32), out_scale[32 * q : 32 * q + 4, :].bitcast(I32))

@@ -20,8 +20,11 @@ P = 128
 PACK = 4
 QUADS = 4
 M = 128
-CHUNKS = 4
-C = S // CHUNKS
+GROUP = 16
+HALF = S // 2
+QUARTER = S // 4
+ORDER = (0, 2, 3, 1)
+WARM_PASSES = 2
 
 
 def tile_picked_bellman_none_po_kernel(
@@ -33,9 +36,9 @@ def tile_picked_bellman_none_po_kernel(
         sb = ctx.enter_context(tc.tile_pool(name="sb", bufs=1))
         ps = ctx.enter_context(tc.psum_pool(name="ps", bufs=1))
 
-        offs_t = lists.tile([P, S // 16], U16, name="offs_t")
-        src_t = lists.tile([P, V // 16], U16, name="src_t")
-        dst_t = lists.tile([P, V // 16], U16, name="dst_t")
+        offs_t = lists.tile([P, S // GROUP], U16, name="offs_t")
+        src_t = lists.tile([P, V // GROUP], U16, name="src_t")
+        dst_t = lists.tile([P, V // GROUP], U16, name="dst_t")
 
         x_codes = sb.tile([P, T], I32, name="x_codes", align_bytes=64)
         x_bytes = sb.tile([P, T], U8, name="x_bytes", tag="x_bytes", align_bytes=64)
@@ -62,7 +65,6 @@ def tile_picked_bellman_none_po_kernel(
                 w2_bytes[32 * q : 32 * q + 4, :].bitcast(I32), w2_scales[0, 4 * q : 4 * q + 4, :].bitcast(I32)
             )
 
-
         picked_bytes = sb.tile([P, S], U8, name="picked_bytes", align_bytes=64)
         nc.vector.tensor_copy(picked_bytes[:], x_bytes[:].indirect(offs_t[:]))
 
@@ -76,21 +78,23 @@ def tile_picked_bellman_none_po_kernel(
             nc.vector.quantize_mx(out=w1_codes[:, cols].bitcast(FP8X4), scales=w1_scale[:, cols], in_=w1_bf[:])
 
         picked_codes = sb.tile([P, S], U32, name="picked_codes", align_bytes=64)
-        half = S // 2
         for h in range(2):
             nc.vector.tensor_copy(
-                picked_codes[:, h * half : (h + 1) * half],
-                x_codes[:].bitcast(U32).indirect(offs_t[:, h * half // 16 : (h + 1) * half // 16]),
+                picked_codes[:, h * HALF : (h + 1) * HALF],
+                x_codes[:].bitcast(U32).indirect(offs_t[:, h * HALF // GROUP : (h + 1) * HALF // GROUP]),
             )
 
-        order = (0, 2, 3, 1)
         y = [sb.tile([P, S], F32, name=f"y{t}", tag=f"y{t}", align_bytes=64) for t in range(PACK)]
-        pieces = [(0, 0, half), (0, half, S)] + [(t, 0, S) for t in order[1:]]
-        for b, (t, c0, c1) in enumerate(pieces):
-            acc = ps.tile([M, c1 - c0], F32, name=f"acc{b}", tag=f"bank{b}")
+        first = ORDER[0]
+        vector_piece = (first, S - QUARTER, S)
+        pieces = [(first, 0, HALF), (first, HALF, S - QUARTER), vector_piece] + [(t, 0, S) for t in ORDER[1:]]
+        y_acc = {}
+        for b, piece in enumerate(pieces):
+            t, c0, c1 = piece
+            y_acc[piece] = ps.tile([M, c1 - c0], F32, name=f"y_acc{b}", tag=f"bank{b}")
             cols = slice(t * M, (t + 1) * M)
             nc.tensor.matmul_mx(
-                out=acc[:],
+                out=y_acc[piece][:],
                 lhsT=w1_codes[:, cols].bitcast(FP8X4),
                 lhsT_scale=w1_scale[:, cols],
                 rhs=picked_codes[:, c0:c1].bitcast(FP8X4),
@@ -98,27 +102,28 @@ def tile_picked_bellman_none_po_kernel(
                 start=True,
                 stop=True,
             )
-            nc.scalar.copy(y[t][:, c0:c1], acc[:])
+            if piece != vector_piece:
+                nc.scalar.copy(y[t][:, c0:c1], y_acc[piece][:])
 
         w2_codes = sb.tile([P, 2 * N], U8, name="w2_codes", align_bytes=64)
         nc.vector.tensor_copy(
             w2_codes[:].rearrange("p (t m b) -> p m t b", t=PACK, b=2),
             w2_raw[:].rearrange("p (m t b) -> p m t b", t=PACK, b=2),
         )
+        w2_scale_head = sb.tile([P, (PACK - 1) * M], U8, name="w2_scale_head", align_bytes=64)
+        w2_byte_cols = w2_bytes[:].rearrange("p (m t) -> p m t", t=PACK)
+        nc.vector.tensor_copy(w2_scale_head[:].rearrange("p (t m) -> p m t", m=M), w2_byte_cols[:, :, : PACK - 1])
 
-        w2_scale = sb.tile([P, N], U8, name="w2_scale", align_bytes=64)
-        nc.vector.tensor_copy(
-            w2_scale[:].rearrange("p (t m) -> p m t", t=PACK), w2_bytes[:].rearrange("p (m t) -> p m t", t=PACK)
-        )
+        nc.vector.tensor_copy(y[first][:, S - QUARTER :], y_acc[vector_piece][:])
 
-        old = sb.tile([P, PACK, V], F32, name="old", align_bytes=64)
+        old = sb.tile([P, PACK, V], F32, name="old", tag="old", align_bytes=64)
         new = sb.tile([P, PACK, V], F32, name="new", align_bytes=64)
 
         def fetch_old(i):
-            nc.vector.tensor_copy(old[:, i, :], y[order[i]][:].indirect(dst_t[:]))
+            nc.vector.tensor_copy(old[:, i, :], y[ORDER[i]][:].indirect(dst_t[:]))
 
         def fetch_new(i):
-            nc.vector.tensor_tensor(new[:, i, :], y[order[i]][:].indirect(src_t[:]), ln_t[:, order[i], :], ADD)
+            nc.vector.tensor_tensor(new[:, i, :], y[ORDER[i]][:].indirect(src_t[:]), ln_t[:, ORDER[i], :], ADD)
 
         for i in range(PACK - 1):
             fetch_old(i)
@@ -130,17 +135,32 @@ def tile_picked_bellman_none_po_kernel(
         relaxed = [ln_t[:, 1, :], ln_t[:, 3, :], new[:, 2, :], new[:, 3, :]]
 
         z_bf = sb.tile([P, S, PACK], BF16, name="z_bf", align_bytes=64)
-        last = order[PACK - 1]
+        last = ORDER[PACK - 1]
         for i in range(PACK - 1):
-            t = order[i]
+            t = ORDER[i]
             nc.vector.tensor_copy(y[t][:].indirect(dst_t[:]), relaxed[i])
             for h in range(2):
-                cols = slice(h * half, (h + 1) * half)
+                cols = slice(h * HALF, (h + 1) * HALF)
                 nc.scalar.copy(z_bf[:, cols, t], y[t][:, cols])
-            if i == 0:
-                z_last = sb.tile([P, S], F32, name="z_last", tag="y0", align_bytes=64)
+            if t == first:
+                z_last = sb.tile([P, S], F32, name="z_last", tag=f"y{first}", align_bytes=64)
                 nc.scalar.copy(z_last[:], y[last][:])
 
+        w2_scale_tail = sb.tile([P, M], U8, name="w2_scale_tail", tag="old", align_bytes=64)
+        nc.vector.tensor_copy(w2_scale_tail[:], w2_byte_cols[:, :, PACK - 1])
+        w2_scale = [w2_scale_head[:, t * M : (t + 1) * M] for t in range(PACK - 1)] + [w2_scale_tail[:]]
+
+        warm = ps.tile([M, S], F32, name="warm", tag="bank7")
+        for rep in range(WARM_PASSES):
+            nc.tensor.matmul_mx(
+                out=warm[:],
+                lhsT=w2_codes[:, 2 * M * (PACK - 1) :].bitcast(FP4X4),
+                lhsT_scale=w2_scale[PACK - 1],
+                rhs=picked_codes[:].bitcast(FP8X4),
+                rhs_scale=picked_bytes[:],
+                start=True,
+                stop=True,
+            )
         nc.vector.tensor_copy(z_last[:].indirect(dst_t[:]), relaxed[PACK - 1])
 
         z_codes = sb.tile([P, S], U32, name="z_codes", align_bytes=64)
@@ -151,47 +171,50 @@ def tile_picked_bellman_none_po_kernel(
         out_rows = out_0.rearrange("(p t) c -> p t c", t=PACK)
         out_words = out_1[0].rearrange("p n t -> p (n t)").bitcast(I32)
 
-        def quantize(codes, scale, values, c0, c1):
+        def quantize(codes, scale, values, c0):
+            c1 = c0 + QUARTER
             nc.vector.quantize_mx(
                 out=codes[:, c0:c1].bitcast(FP8X4), scales=scale[:, c0:c1], in_=values[:, c0 * PACK : c1 * PACK]
             )
 
         for h in range(2):
-            for c0 in (h * half, h * half + C):
-                nc.vector.tensor_copy(z_bf[:, c0 : c0 + C, last], z_last[:, c0 : c0 + C])
-            for c0 in (h * half, h * half + C):
-                quantize(z_codes, z_scale, z_flat, c0, c0 + C)
+            for c0 in (h * HALF, h * HALF + QUARTER):
+                nc.vector.tensor_copy(z_bf[:, c0 : c0 + QUARTER, last], z_last[:, c0 : c0 + QUARTER])
+            for c0 in (h * HALF, h * HALF + QUARTER):
+                quantize(z_codes, z_scale, z_flat, c0)
 
         res_bf = sb.tile([P, S, PACK], BF16, name="res_bf", align_bytes=64)
         res_flat = res_bf[:].rearrange("p c t -> p (c t)")
         for h in range(2):
-            cols = slice(h * half, (h + 1) * half)
-            res = sb.tile([P, PACK, half], F32, name=f"res{h}", align_bytes=64)
+            cols = slice(h * HALF, (h + 1) * HALF)
+            res = sb.tile([P, PACK, HALF], F32, name=f"res{h}", align_bytes=64)
             for t in range(PACK):
-                acc = ps.tile([M, half], F32, name=f"out_acc{h}{t}", tag=f"bank{h * PACK + t}")
+                out_acc = ps.tile([M, HALF], F32, name=f"out_acc{h}{t}", tag=f"bank{h * PACK + t}")
                 nc.tensor.matmul_mx(
-                    out=acc[:],
+                    out=out_acc[:],
                     lhsT=w2_codes[:, 2 * M * t : 2 * M * (t + 1)].bitcast(FP4X4),
-                    lhsT_scale=w2_scale[:, M * t : M * (t + 1)],
+                    lhsT_scale=w2_scale[t],
                     rhs=z_codes[:, cols].bitcast(FP8X4),
                     rhs_scale=z_scale[:, cols],
                     start=True,
                     stop=True,
                 )
-                if h == 0 and t % 2:
-                    nc.vector.tensor_copy(res[:, t, :], acc[:])
+                if h == 0 and t % 2 == 0:
+                    nc.vector.tensor_copy(res[:, t, :], out_acc[:])
                 else:
-                    nc.scalar.copy(res[:, t, :], acc[:])
+                    nc.scalar.copy(res[:, t, :], out_acc[:])
                 if t % 2:
                     nc.sync.dma_start(out_rows[:, t - 1 : t + 1, cols], res[:, t - 1 : t + 1, :])
-            for i in range(2):
+            for c0 in (0, QUARTER):
                 nc.vector.tensor_copy(
-                    res_bf[:, h * half + i * C : h * half + (i + 1) * C, :].rearrange("p (c i) t -> p c t i", i=4),
-                    res[:, :, i * C : (i + 1) * C].rearrange("p t (c i) -> p c t i", i=4),
+                    res_bf[:, h * HALF + c0 : h * HALF + c0 + QUARTER, :].rearrange("p (c i) t -> p c t i", i=4),
+                    res[:, :, c0 : c0 + QUARTER].rearrange("p t (c i) -> p c t i", i=4),
                 )
-            for i in range(2):
-                quantize(out_codes, out_scale, res_flat, h * half + i * C, h * half + (i + 1) * C)
+            for c0 in (0, QUARTER):
+                quantize(out_codes, out_scale, res_flat, h * HALF + c0)
             nc.sync.dma_start(out_words[:, cols], out_codes[:, cols])
         for q in range(QUADS):
-            eng = nc.sync if q % 2 else nc.scalar
-            eng.dma_start(out_2[0, 4 * q : 4 * q + 4, :].bitcast(I32), out_scale[32 * q : 32 * q + 4, :].bitcast(I32))
+            queue = nc.sync if q % 2 else nc.scalar
+            queue.dma_start(
+                out_2[0, 4 * q : 4 * q + 4, :].bitcast(I32), out_scale[32 * q : 32 * q + 4, :].bitcast(I32)
+            )

@@ -86,8 +86,7 @@ def tile_picked_bellman_none_po_kernel(
 
         y = [sb.tile([P, S], F32, name=f"y{t}", tag=f"y{t}", align_bytes=64) for t in range(PACK)]
         first = ORDER[0]
-        vector_piece = (first, S - QUARTER, S)
-        pieces = [(first, 0, HALF), (first, HALF, S - QUARTER), vector_piece] + [(t, 0, S) for t in ORDER[1:]]
+        pieces = [(first, 0, HALF), (first, HALF, S)] + [(t, 0, S) for t in ORDER[1:]]
         y_acc = {}
         for b, piece in enumerate(pieces):
             t, c0, c1 = piece
@@ -102,8 +101,7 @@ def tile_picked_bellman_none_po_kernel(
                 start=True,
                 stop=True,
             )
-            if piece != vector_piece:
-                nc.scalar.copy(y[t][:, c0:c1], y_acc[piece][:])
+            nc.scalar.copy(y[t][:, c0:c1], y_acc[piece][:])
 
         w2_codes = sb.tile([P, 2 * N], U8, name="w2_codes", align_bytes=64)
         nc.vector.tensor_copy(
@@ -114,7 +112,6 @@ def tile_picked_bellman_none_po_kernel(
         w2_byte_cols = w2_bytes[:].rearrange("p (m t) -> p m t", t=PACK)
         nc.vector.tensor_copy(w2_scale_head[:].rearrange("p (t m) -> p m t", m=M), w2_byte_cols[:, :, : PACK - 1])
 
-        nc.vector.tensor_copy(y[first][:, S - QUARTER :], y_acc[vector_piece][:])
 
         old = sb.tile([P, PACK, V], F32, name="old", tag="old", align_bytes=64)
         new = sb.tile([P, PACK, V], F32, name="new", align_bytes=64)
@@ -125,26 +122,32 @@ def tile_picked_bellman_none_po_kernel(
         def fetch_new(i):
             nc.vector.tensor_tensor(new[:, i, :], y[ORDER[i]][:].indirect(src_t[:]), ln_t[:, ORDER[i], :], ADD)
 
-        for i in range(PACK - 1):
-            fetch_old(i)
-            fetch_new(i)
-        fetch_new(PACK - 1)
-        fetch_old(PACK - 1)
-        nc.vector.tensor_tensor(ln_t[:, 1::2, :], old[:, 0:2, :], new[:, 0:2, :], MIN)
-        nc.vector.tensor_tensor(new[:, 2:4, :], old[:, 2:4, :], new[:, 2:4, :], MIN)
-        relaxed = [ln_t[:, 1, :], ln_t[:, 3, :], new[:, 2, :], new[:, 3, :]]
-
         z_bf = sb.tile([P, S, PACK], BF16, name="z_bf", align_bytes=64)
         last = ORDER[PACK - 1]
-        for i in range(PACK - 1):
+        relaxed = [ln_t[:, 0, :], ln_t[:, 3, :], new[:, 2, :], new[:, 3, :]]
+
+        def put_back(i):
             t = ORDER[i]
             nc.vector.tensor_copy(y[t][:].indirect(dst_t[:]), relaxed[i])
             for h in range(2):
                 cols = slice(h * HALF, (h + 1) * HALF)
                 nc.scalar.copy(z_bf[:, cols, t], y[t][:, cols])
-            if t == first:
-                z_last = sb.tile([P, S], F32, name="z_last", tag=f"y{first}", align_bytes=64)
-                nc.scalar.copy(z_last[:], y[last][:])
+
+        for i in range(2):
+            fetch_old(i)
+            fetch_new(i)
+        fetch_new(2)
+        nc.vector.tensor_tensor(ln_t[:, 0::3, :], old[:, 0:2, :], new[:, 0:2, :], MIN)
+        fetch_old(2)
+        put_back(0)
+        z_last = sb.tile([P, S], F32, name="z_last", tag=f"y{first}", align_bytes=64)
+        nc.scalar.copy(z_last[:], y[last][:])
+        fetch_old(3)
+        fetch_new(3)
+        nc.vector.tensor_tensor(new[:, 2, :], old[:, 2, :], new[:, 2, :], MIN)
+        put_back(1)
+        nc.vector.tensor_tensor(new[:, 3, :], old[:, 3, :], new[:, 3, :], MIN)
+        put_back(2)
 
         w2_scale_tail = sb.tile([P, M], U8, name="w2_scale_tail", tag="old", align_bytes=64)
         nc.vector.tensor_copy(w2_scale_tail[:], w2_byte_cols[:, :, PACK - 1])
@@ -177,11 +180,11 @@ def tile_picked_bellman_none_po_kernel(
                 out=codes[:, c0:c1].bitcast(FP8X4), scales=scale[:, c0:c1], in_=values[:, c0 * PACK : c1 * PACK]
             )
 
-        for h in range(2):
-            for c0 in (h * HALF, h * HALF + QUARTER):
-                nc.vector.tensor_copy(z_bf[:, c0 : c0 + QUARTER, last], z_last[:, c0 : c0 + QUARTER])
-            for c0 in (h * HALF, h * HALF + QUARTER):
-                quantize(z_codes, z_scale, z_flat, c0)
+        for c0 in range(0, S, QUARTER):
+            copy = nc.vector.tensor_copy if c0 < HALF else nc.scalar.copy
+            copy(z_bf[:, c0 : c0 + QUARTER, last], z_last[:, c0 : c0 + QUARTER])
+        for c0 in range(0, S, QUARTER):
+            quantize(z_codes, z_scale, z_flat, c0)
 
         res_bf = sb.tile([P, S, PACK], BF16, name="res_bf", align_bytes=64)
         res_flat = res_bf[:].rearrange("p c t -> p (c t)")
@@ -190,20 +193,24 @@ def tile_picked_bellman_none_po_kernel(
             res = sb.tile([P, PACK, HALF], F32, name=f"res{h}", align_bytes=64)
             for t in range(PACK):
                 out_acc = ps.tile([M, HALF], F32, name=f"out_acc{h}{t}", tag=f"bank{h * PACK + t}")
-                nc.tensor.matmul_mx(
-                    out=out_acc[:],
-                    lhsT=w2_codes[:, 2 * M * t : 2 * M * (t + 1)].bitcast(FP4X4),
-                    lhsT_scale=w2_scale[t],
-                    rhs=z_codes[:, cols].bitcast(FP8X4),
-                    rhs_scale=z_scale[:, cols],
-                    start=True,
-                    stop=True,
-                )
+                for c0 in (0, QUARTER):
+                    part = slice(h * HALF + c0, h * HALF + c0 + QUARTER)
+                    nc.tensor.matmul_mx(
+                        out=out_acc[:, c0 : c0 + QUARTER],
+                        lhsT=w2_codes[:, 2 * M * t : 2 * M * (t + 1)].bitcast(FP4X4),
+                        lhsT_scale=w2_scale[t],
+                        rhs=z_codes[:, part].bitcast(FP8X4),
+                        rhs_scale=z_scale[:, part],
+                        start=True,
+                        stop=True,
+                    )
                 if h == 0 and t % 2 == 0:
                     nc.vector.tensor_copy(res[:, t, :], out_acc[:])
                 else:
                     nc.scalar.copy(res[:, t, :], out_acc[:])
-                if t % 2:
+                if h == 0 and t < 2:
+                    nc.sync.dma_start(out_rows[:, t, cols], res[:, t, :])
+                elif t % 2:
                     nc.sync.dma_start(out_rows[:, t - 1 : t + 1, cols], res[:, t - 1 : t + 1, :])
             for c0 in (0, QUARTER):
                 nc.vector.tensor_copy(

@@ -105,8 +105,8 @@ def tile_picked_bellman_none_po_kernel(
 
         w2_codes = sb.tile([P, 2 * N], U8, name="w2_codes", align_bytes=64)
         nc.vector.tensor_copy(
-            w2_codes[:].rearrange("p (t m b) -> p m t b", t=PACK, b=2),
-            w2_raw[:].rearrange("p (m t b) -> p m t b", t=PACK, b=2),
+            w2_codes[:].bitcast(U16).rearrange("p (t m) -> p m t", t=PACK),
+            w2_raw[:].bitcast(U16).rearrange("p (m t) -> p m t", t=PACK),
         )
         w2_scale_head = sb.tile([P, (PACK - 1) * M], U8, name="w2_scale_head", align_bytes=64)
         w2_byte_cols = w2_bytes[:].rearrange("p (m t) -> p m t", t=PACK)
@@ -188,38 +188,52 @@ def tile_picked_bellman_none_po_kernel(
 
         res_bf = sb.tile([P, S, PACK], BF16, name="res_bf", align_bytes=64)
         res_flat = res_bf[:].rearrange("p c t -> p (c t)")
-        for h in range(2):
-            cols = slice(h * HALF, (h + 1) * HALF)
-            res = sb.tile([P, PACK, HALF], F32, name=f"res{h}", align_bytes=64)
-            for t in range(PACK):
-                out_acc = ps.tile([M, HALF], F32, name=f"out_acc{h}{t}", tag=f"bank{h * PACK + t}")
-                for c0 in (0, QUARTER):
-                    part = slice(h * HALF + c0, h * HALF + c0 + QUARTER)
-                    nc.tensor.matmul_mx(
-                        out=out_acc[:, c0 : c0 + QUARTER],
-                        lhsT=w2_codes[:, 2 * M * t : 2 * M * (t + 1)].bitcast(FP4X4),
-                        lhsT_scale=w2_scale[t],
-                        rhs=z_codes[:, part].bitcast(FP8X4),
-                        rhs_scale=z_scale[:, part],
-                        start=True,
-                        stop=True,
-                    )
-                if h == 0 and t % 2 == 0:
-                    nc.vector.tensor_copy(res[:, t, :], out_acc[:])
-                else:
-                    nc.scalar.copy(res[:, t, :], out_acc[:])
-                if h == 0 and t < 2:
-                    nc.sync.dma_start(out_rows[:, t, cols], res[:, t, :])
-                elif t % 2:
-                    nc.sync.dma_start(out_rows[:, t - 1 : t + 1, cols], res[:, t - 1 : t + 1, :])
-            for c0 in (0, QUARTER):
-                nc.vector.tensor_copy(
-                    res_bf[:, h * HALF + c0 : h * HALF + c0 + QUARTER, :].rearrange("p (c i) t -> p c t i", i=4),
-                    res[:, :, c0 : c0 + QUARTER].rearrange("p t (c i) -> p c t i", i=4),
-                )
-            for c0 in (0, QUARTER):
-                quantize(out_codes, out_scale, res_flat, h * HALF + c0)
-            nc.sync.dma_start(out_words[:, cols], out_codes[:, cols])
+
+        def product(acc, t, c0, c1):
+            nc.tensor.matmul_mx(
+                out=acc,
+                lhsT=w2_codes[:, 2 * M * t : 2 * M * (t + 1)].bitcast(FP4X4),
+                lhsT_scale=w2_scale[t],
+                rhs=z_codes[:, c0:c1].bitcast(FP8X4),
+                rhs_scale=z_scale[:, c0:c1],
+                start=True,
+                stop=True,
+            )
+
+        def interleave(copy, res, r0, c0):
+            copy(
+                res_bf[:, c0 : c0 + QUARTER, :].rearrange("p (c i) t -> p c t i", i=4),
+                res[:, :, r0 : r0 + QUARTER].rearrange("p t (c i) -> p c t i", i=4),
+            )
+
+        vector_banks = ((0, 1), (3, 1))
+        res = []
+        for q in range(4):
+            c0 = q * QUARTER
+            cols = slice(c0, c0 + QUARTER)
+            res.append(sb.tile([P, PACK, QUARTER], F32, name=f"res{q}", align_bytes=64))
+            for u in range(2):
+                acc = ps.tile([M, 2, QUARTER], F32, name=f"out_acc{q}{u}", tag=f"bank{2 * q + u}")
+                for e in range(2):
+                    product(acc[:, e, :], 2 * u + e, c0, c0 + QUARTER)
+                copy = nc.vector.tensor_copy if (q, u) in vector_banks else nc.scalar.copy
+                copy(res[q][:, 2 * u : 2 * u + 2, :], acc[:])
+                if q == 0:
+                    nc.sync.dma_start(out_rows[:, 2 * u : 2 * u + 2, cols], res[q][:, 2 * u : 2 * u + 2, :])
+            if q:
+                nc.sync.dma_start(out_rows[:, :, cols], res[q][:])
+            if q == 1:
+                for e in range(2):
+                    interleave(nc.vector.tensor_copy, res[e], 0, e * QUARTER)
+        interleave(nc.vector.tensor_copy, res[2], 0, HALF)
+        interleave(nc.scalar.copy, res[3], 0, HALF + QUARTER)
+        nc.vector.quantize_mx(
+            out=out_codes[:, :HALF].bitcast(FP8X4), scales=out_scale[:, :HALF], in_=res_flat[:, : HALF * PACK]
+        )
+        nc.sync.dma_start(out_words[:, :HALF], out_codes[:, :HALF])
+        for c0 in (HALF, HALF + QUARTER):
+            quantize(out_codes, out_scale, res_flat, c0)
+        nc.sync.dma_start(out_words[:, HALF:], out_codes[:, HALF:])
         for q in range(QUADS):
             queue = nc.sync if q % 2 else nc.scalar
             queue.dma_start(

@@ -24,6 +24,7 @@ GROUP = 16
 HALF = S // 2
 QUARTER = S // 4
 ORDER = (0, 2, 3, 1)
+SPLIT = 96
 WARM_PASSES = 2
 
 
@@ -49,39 +50,41 @@ def tile_picked_bellman_none_po_kernel(
 
         nc.gpsimd.memset(x_bytes[:].bitcast(I32), 0)
         nc.gpsimd.memset(w2_bytes[:].bitcast(I32), 0)
-        nc.sync.dma_start(w1_raw[:], w1.rearrange("(p j) c -> p j c", j=PACK))
         nc.sync.dma_start(offs_t[:], offs)
+        nc.sync.dma_start(x_codes[:], x_words[0].rearrange("p n t -> p (n t)").bitcast(I32))
         for q in range(QUADS):
             nc.sync.dma_start(
                 x_bytes[32 * q : 32 * q + 4, :].bitcast(I32), x_scales[0, 4 * q : 4 * q + 4, :].bitcast(I32)
             )
-        nc.sync.dma_start(dst_t[:], dst)
-        nc.sync.dma_start(x_codes[:], x_words[0].rearrange("p n t -> p (n t)").bitcast(I32))
-        nc.sync.dma_start(src_t[:], src)
+        nc.sync.dma_start(w1_raw[:], w1.rearrange("(p j) c -> p j c", j=PACK))
         nc.sync.dma_start(w2_raw[:].bitcast(I32), w2_words[0].bitcast(I32))
-        nc.sync.dma_start(ln_t[:], ln.rearrange("(p t) v -> p t v", t=PACK))
+        nc.sync.dma_start(dst_t[:], dst)
         for q in range(QUADS):
             nc.sync.dma_start(
                 w2_bytes[32 * q : 32 * q + 4, :].bitcast(I32), w2_scales[0, 4 * q : 4 * q + 4, :].bitcast(I32)
             )
+        nc.sync.dma_start(ln_t[:], ln.rearrange("(p t) v -> p t v", t=PACK))
+        nc.sync.dma_start(src_t[:], src)
 
+        picked_codes = sb.tile([P, S], U32, name="picked_codes", align_bytes=64)
+        nc.vector.tensor_copy(picked_codes[:], x_codes[:].bitcast(U32).indirect(offs_t[:]))
         picked_bytes = sb.tile([P, S], U8, name="picked_bytes", align_bytes=64)
         nc.vector.tensor_copy(picked_bytes[:], x_bytes[:].indirect(offs_t[:]))
 
-        w1_codes = sb.tile([P, H], U32, name="w1_codes", tag="x_bytes", align_bytes=64)
+        w1_codes = sb.tile([P, H], U32, name="w1_codes", align_bytes=64)
         w1_scale = sb.tile([P, H], U8, name="w1_scale", align_bytes=64)
         w1_cols = w1_raw[:].rearrange("p j (m t) -> p m j t", t=PACK)
-        for u, copy in enumerate((nc.vector.tensor_copy, nc.scalar.copy)):
-            w1_bf = sb.tile([P, 2 * M * PACK], BF16, name=f"w1_bf{u}", align_bytes=64)
-            copy(w1_bf[:].rearrange("p (t m j) -> p m j t", t=2, j=PACK), w1_cols[:, :, :, 2 * u : 2 * u + 2])
-            cols = slice(2 * u * M, 2 * (u + 1) * M)
-            nc.vector.quantize_mx(out=w1_codes[:, cols].bitcast(FP8X4), scales=w1_scale[:, cols], in_=w1_bf[:])
-
-        picked_codes = sb.tile([P, S], U32, name="picked_codes", align_bytes=64)
-        for h in range(2):
-            nc.vector.tensor_copy(
-                picked_codes[:, h * HALF : (h + 1) * HALF],
-                x_codes[:].bitcast(U32).indirect(offs_t[:, h * HALF // GROUP : (h + 1) * HALF // GROUP]),
+        w1_bf = [sb.tile([P, 2 * M * PACK], BF16, name=f"w1_bf{u}", align_bytes=64) for u in range(2)]
+        w1_dealt = [w1_bf[u][:].rearrange("p (t m j) -> p m j t", t=2, j=PACK) for u in range(2)]
+        nc.vector.tensor_copy(w1_dealt[0][:, :SPLIT], w1_cols[:, :SPLIT, :, 0:2])
+        nc.scalar.copy(w1_dealt[0][:, SPLIT:], w1_cols[:, SPLIT:, :, 0:2])
+        nc.scalar.copy(w1_dealt[1], w1_cols[:, :, :, 2:4])
+        for c0, c1 in ((0, M), (M, 2 * M), (2 * M, 4 * M)):
+            u, r0 = divmod(c0, 2 * M)
+            nc.vector.quantize_mx(
+                out=w1_codes[:, c0:c1].bitcast(FP8X4),
+                scales=w1_scale[:, c0:c1],
+                in_=w1_bf[u][:, r0 * PACK : (r0 + c1 - c0) * PACK],
             )
 
         y = [sb.tile([P, S], F32, name=f"y{t}", tag=f"y{t}", align_bytes=64) for t in range(PACK)]

@@ -23,8 +23,9 @@ M = 128
 GROUP = 16
 HALF = S // 2
 QUARTER = S // 4
+PAIR = 2
 ORDER = (0, 2, 3, 1)
-SPLIT = 96
+VECTOR_BANKS = ((0, 1), (3, 1))
 WARM_PASSES = 2
 
 
@@ -42,7 +43,7 @@ def tile_picked_bellman_none_po_kernel(
         dst_t = lists.tile([P, V // GROUP], U16, name="dst_t")
 
         x_codes = sb.tile([P, T], I32, name="x_codes", align_bytes=64)
-        x_bytes = sb.tile([P, T], U8, name="x_bytes", tag="x_bytes", align_bytes=64)
+        x_bytes = sb.tile([P, T], U8, name="x_bytes", align_bytes=64)
         w1_raw = sb.tile([P, PACK, H], F32, name="w1_raw", align_bytes=64)
         ln_t = sb.tile([P, PACK, V], F32, name="ln_t", align_bytes=64)
         w2_raw = sb.tile([P, 2 * N], U8, name="w2_raw", align_bytes=64)
@@ -74,29 +75,28 @@ def tile_picked_bellman_none_po_kernel(
         w1_codes = sb.tile([P, H], U32, name="w1_codes", align_bytes=64)
         w1_scale = sb.tile([P, H], U8, name="w1_scale", align_bytes=64)
         w1_cols = w1_raw[:].rearrange("p j (m t) -> p m j t", t=PACK)
-        w1_bf = [sb.tile([P, 2 * M * PACK], BF16, name=f"w1_bf{u}", align_bytes=64) for u in range(2)]
-        w1_dealt = [w1_bf[u][:].rearrange("p (t m j) -> p m j t", t=2, j=PACK) for u in range(2)]
-        nc.vector.tensor_copy(w1_dealt[0][:, :SPLIT], w1_cols[:, :SPLIT, :, 0:2])
-        nc.scalar.copy(w1_dealt[0][:, SPLIT:], w1_cols[:, SPLIT:, :, 0:2])
-        nc.scalar.copy(w1_dealt[1], w1_cols[:, :, :, 2:4])
-        for c0, c1 in ((0, M), (M, 2 * M), (2 * M, 4 * M)):
-            u, r0 = divmod(c0, 2 * M)
+        w1_bf = [sb.tile([P, PAIR * M * PACK], BF16, name=f"w1_bf{u}", align_bytes=64) for u in range(2)]
+        for u, copy in enumerate((nc.vector.tensor_copy, nc.scalar.copy)):
+            copy(
+                w1_bf[u][:].rearrange("p (t m j) -> p m j t", t=PAIR, j=PACK),
+                w1_cols[:, :, :, PAIR * u : PAIR * (u + 1)],
+            )
+        for t0, t1 in ((0, 1), (1, 2), (2, 4)):
+            u, inner = divmod(t0, PAIR)
             nc.vector.quantize_mx(
-                out=w1_codes[:, c0:c1].bitcast(FP8X4),
-                scales=w1_scale[:, c0:c1],
-                in_=w1_bf[u][:, r0 * PACK : (r0 + c1 - c0) * PACK],
+                out=w1_codes[:, t0 * M : t1 * M].bitcast(FP8X4),
+                scales=w1_scale[:, t0 * M : t1 * M],
+                in_=w1_bf[u][:, inner * M * PACK : (inner + t1 - t0) * M * PACK],
             )
 
         y = [sb.tile([P, S], F32, name=f"y{t}", tag=f"y{t}", align_bytes=64) for t in range(PACK)]
         first = ORDER[0]
         pieces = [(first, 0, HALF), (first, HALF, S)] + [(t, 0, S) for t in ORDER[1:]]
-        y_acc = {}
-        for b, piece in enumerate(pieces):
-            t, c0, c1 = piece
-            y_acc[piece] = ps.tile([M, c1 - c0], F32, name=f"y_acc{b}", tag=f"bank{b}")
+        for b, (t, c0, c1) in enumerate(pieces):
+            y_acc = ps.tile([M, c1 - c0], F32, name=f"y_acc{b}", tag=f"bank{b}")
             cols = slice(t * M, (t + 1) * M)
             nc.tensor.matmul_mx(
-                out=y_acc[piece][:],
+                out=y_acc[:],
                 lhsT=w1_codes[:, cols].bitcast(FP8X4),
                 lhsT_scale=w1_scale[:, cols],
                 rhs=picked_codes[:, c0:c1].bitcast(FP8X4),
@@ -104,7 +104,7 @@ def tile_picked_bellman_none_po_kernel(
                 start=True,
                 stop=True,
             )
-            nc.scalar.copy(y[t][:, c0:c1], y_acc[piece][:])
+            nc.scalar.copy(y[t][:, c0:c1], y_acc[:])
 
         w2_codes = sb.tile([P, 2 * N], U8, name="w2_codes", align_bytes=64)
         nc.vector.tensor_copy(
@@ -114,7 +114,6 @@ def tile_picked_bellman_none_po_kernel(
         w2_scale_head = sb.tile([P, (PACK - 1) * M], U8, name="w2_scale_head", align_bytes=64)
         w2_byte_cols = w2_bytes[:].rearrange("p (m t) -> p m t", t=PACK)
         nc.vector.tensor_copy(w2_scale_head[:].rearrange("p (t m) -> p m t", m=M), w2_byte_cols[:, :, : PACK - 1])
-
 
         old = sb.tile([P, PACK, V], F32, name="old", tag="old", align_bytes=64)
         new = sb.tile([P, PACK, V], F32, name="new", align_bytes=64)
@@ -177,8 +176,7 @@ def tile_picked_bellman_none_po_kernel(
         out_rows = out_0.rearrange("(p t) c -> p t c", t=PACK)
         out_words = out_1[0].rearrange("p n t -> p (n t)").bitcast(I32)
 
-        def quantize(codes, scale, values, c0):
-            c1 = c0 + QUARTER
+        def quantize(codes, scale, values, c0, c1):
             nc.vector.quantize_mx(
                 out=codes[:, c0:c1].bitcast(FP8X4), scales=scale[:, c0:c1], in_=values[:, c0 * PACK : c1 * PACK]
             )
@@ -187,56 +185,51 @@ def tile_picked_bellman_none_po_kernel(
             copy = nc.vector.tensor_copy if c0 < HALF else nc.scalar.copy
             copy(z_bf[:, c0 : c0 + QUARTER, last], z_last[:, c0 : c0 + QUARTER])
         for c0 in range(0, S, QUARTER):
-            quantize(z_codes, z_scale, z_flat, c0)
+            quantize(z_codes, z_scale, z_flat, c0, c0 + QUARTER)
 
         res_bf = sb.tile([P, S, PACK], BF16, name="res_bf", align_bytes=64)
         res_flat = res_bf[:].rearrange("p c t -> p (c t)")
-
-        def product(acc, t, c0, c1):
-            nc.tensor.matmul_mx(
-                out=acc,
-                lhsT=w2_codes[:, 2 * M * t : 2 * M * (t + 1)].bitcast(FP4X4),
-                lhsT_scale=w2_scale[t],
-                rhs=z_codes[:, c0:c1].bitcast(FP8X4),
-                rhs_scale=z_scale[:, c0:c1],
-                start=True,
-                stop=True,
-            )
-
-        def interleave(copy, res, r0, c0):
-            copy(
-                res_bf[:, c0 : c0 + QUARTER, :].rearrange("p (c i) t -> p c t i", i=4),
-                res[:, :, r0 : r0 + QUARTER].rearrange("p t (c i) -> p c t i", i=4),
-            )
-
-        vector_banks = ((0, 1), (3, 1))
         res = []
-        for q in range(4):
-            c0 = q * QUARTER
-            cols = slice(c0, c0 + QUARTER)
+
+        def interleave(copy, q):
+            copy(
+                res_bf[:, q * QUARTER : (q + 1) * QUARTER, :].rearrange("p (c i) t -> p c t i", i=4),
+                res[q][:].rearrange("p t (c i) -> p c t i", i=4),
+            )
+
+        for q in range(S // QUARTER):
+            cols = slice(q * QUARTER, (q + 1) * QUARTER)
             res.append(sb.tile([P, PACK, QUARTER], F32, name=f"res{q}", align_bytes=64))
-            for u in range(2):
-                acc = ps.tile([M, 2, QUARTER], F32, name=f"out_acc{q}{u}", tag=f"bank{2 * q + u}")
-                for e in range(2):
-                    product(acc[:, e, :], 2 * u + e, c0, c0 + QUARTER)
-                copy = nc.vector.tensor_copy if (q, u) in vector_banks else nc.scalar.copy
-                copy(res[q][:, 2 * u : 2 * u + 2, :], acc[:])
+            for u in range(PACK // PAIR):
+                planes = slice(PAIR * u, PAIR * (u + 1))
+                out_acc = ps.tile([M, PAIR, QUARTER], F32, name=f"out_acc{q}{u}", tag=f"bank{PAIR * q + u}")
+                for inner in range(PAIR):
+                    t = PAIR * u + inner
+                    nc.tensor.matmul_mx(
+                        out=out_acc[:, inner, :],
+                        lhsT=w2_codes[:, 2 * M * t : 2 * M * (t + 1)].bitcast(FP4X4),
+                        lhsT_scale=w2_scale[t],
+                        rhs=z_codes[:, cols].bitcast(FP8X4),
+                        rhs_scale=z_scale[:, cols],
+                        start=True,
+                        stop=True,
+                    )
+                copy = nc.vector.tensor_copy if (q, u) in VECTOR_BANKS else nc.scalar.copy
+                copy(res[q][:, planes, :], out_acc[:])
                 if q == 0:
-                    nc.sync.dma_start(out_rows[:, 2 * u : 2 * u + 2, cols], res[q][:, 2 * u : 2 * u + 2, :])
-            if q:
+                    nc.sync.dma_start(out_rows[:, planes, cols], res[q][:, planes, :])
+            if q > 0:
                 nc.sync.dma_start(out_rows[:, :, cols], res[q][:])
             if q == 1:
-                for e in range(2):
-                    interleave(nc.vector.tensor_copy, res[e], 0, e * QUARTER)
-        interleave(nc.vector.tensor_copy, res[2], 0, HALF)
-        interleave(nc.scalar.copy, res[3], 0, HALF + QUARTER)
-        nc.vector.quantize_mx(
-            out=out_codes[:, :HALF].bitcast(FP8X4), scales=out_scale[:, :HALF], in_=res_flat[:, : HALF * PACK]
-        )
-        nc.sync.dma_start(out_words[:, :HALF], out_codes[:, :HALF])
-        for c0 in (HALF, HALF + QUARTER):
-            quantize(out_codes, out_scale, res_flat, c0)
-        nc.sync.dma_start(out_words[:, HALF:], out_codes[:, HALF:])
+                interleave(nc.vector.tensor_copy, 0)
+                interleave(nc.vector.tensor_copy, 1)
+        interleave(nc.vector.tensor_copy, 2)
+        interleave(nc.scalar.copy, 3)
+        quantize(out_codes, out_scale, res_flat, 0, HALF)
+        quantize(out_codes, out_scale, res_flat, HALF, S - QUARTER)
+        nc.sync.dma_start(out_words[:, : S - QUARTER], out_codes[:, : S - QUARTER])
+        quantize(out_codes, out_scale, res_flat, S - QUARTER, S)
+        nc.sync.dma_start(out_words[:, S - QUARTER :], out_codes[:, S - QUARTER :])
         for q in range(QUADS):
             queue = nc.sync if q % 2 else nc.scalar
             queue.dma_start(

@@ -22,6 +22,7 @@ QUADS = 4
 M = 128
 GROUP = 16
 HALF = S // 2
+SPREAD = P - 16
 QUARTER = S // 4
 PAIR = 2
 ORDER = (0, 2, 3, 1)
@@ -42,56 +43,61 @@ def tile_picked_bellman_none_po_kernel(
         src_t = lists.tile([P, V // GROUP], U16, name="src_t")
         dst_t = lists.tile([P, V // GROUP], U16, name="dst_t")
 
-        x_codes = sb.tile([P, T], I32, name="x_codes", align_bytes=64)
+        x_codes = sb.tile([P, T], I32, name="x_codes", tag="x_codes", align_bytes=64)
         x_bytes = sb.tile([P, T], U8, name="x_bytes", align_bytes=64)
         w1_raw = sb.tile([P, PACK, H], F32, name="w1_raw", align_bytes=64)
         ln_t = sb.tile([P, PACK, V], F32, name="ln_t", align_bytes=64)
-        w2_raw = sb.tile([P, 2 * N], U8, name="w2_raw", align_bytes=64)
         w2_bytes = sb.tile([P, N], U8, name="w2_bytes", align_bytes=64)
 
-        nc.gpsimd.memset(x_bytes[:].bitcast(I32), 0)
         nc.gpsimd.memset(w2_bytes[:].bitcast(I32), 0)
+        nc.gpsimd.memset(x_bytes[:SPREAD, :].bitcast(I32), 0)
+        picked_bytes = sb.tile([P, S], U8, name="picked_bytes", align_bytes=64)
+        nc.gpsimd.memset(picked_bytes[:].bitcast(I32), 0)
         nc.sync.dma_start(offs_t[:], offs)
-        nc.sync.dma_start(x_codes[:], x_words[0].rearrange("p n t -> p (n t)").bitcast(I32))
-        for q in range(QUADS):
-            nc.sync.dma_start(
-                x_bytes[32 * q : 32 * q + 4, :].bitcast(I32), x_scales[0, 4 * q : 4 * q + 4, :].bitcast(I32)
-            )
-        nc.sync.dma_start(w1_raw[:], w1.rearrange("(p j) c -> p j c", j=PACK))
-        nc.sync.dma_start(w2_raw[:].bitcast(I32), w2_words[0].bitcast(I32))
+        nc.scalar.dma_start(x_bytes[SPREAD:, :].bitcast(I32), x_scales[0].bitcast(I32))
         nc.sync.dma_start(dst_t[:], dst)
+        nc.sync.dma_start(w1_raw[:], w1.rearrange("(p j) c -> p j c", j=PACK))
+        nc.sync.dma_start(x_codes[:], x_words[0].rearrange("p n t -> p (n t)").bitcast(I32))
+        w2_raw = sb.tile([P, 2 * N], U8, name="w2_raw", align_bytes=64)
+        nc.sync.dma_start(w2_raw[:].bitcast(I32), w2_words[0].bitcast(I32))
+        nc.sync.dma_start(src_t[:], src)
+        nc.sync.dma_start(ln_t[:], ln.rearrange("(p t) v -> p t v", t=PACK))
         for q in range(QUADS):
-            nc.sync.dma_start(
+            nc.gpsimd.dma_start(
                 w2_bytes[32 * q : 32 * q + 4, :].bitcast(I32), w2_scales[0, 4 * q : 4 * q + 4, :].bitcast(I32)
             )
-        nc.sync.dma_start(ln_t[:], ln.rearrange("(p t) v -> p t v", t=PACK))
-        nc.sync.dma_start(src_t[:], src)
 
-        picked_codes = sb.tile([P, S], U32, name="picked_codes", align_bytes=64)
-        nc.vector.tensor_copy(picked_codes[:], x_codes[:].bitcast(U32).indirect(offs_t[:]))
-        picked_bytes = sb.tile([P, S], U8, name="picked_bytes", align_bytes=64)
-        nc.vector.tensor_copy(picked_bytes[:], x_bytes[:].indirect(offs_t[:]))
+        spread_bytes = sb.tile([P, S], U8, name="spread_bytes", align_bytes=64)
+        nc.vector.tensor_copy(spread_bytes[:], x_bytes[:].indirect(offs_t[:]))
+        for q in range(QUADS):
+            nc.scalar.dma_start(
+                picked_bytes[32 * q : 32 * q + 4, :].bitcast(I32),
+                spread_bytes[SPREAD + 4 * q : SPREAD + 4 * q + 4, :].bitcast(I32),
+            )
 
         w1_codes = sb.tile([P, H], U32, name="w1_codes", align_bytes=64)
         w1_scale = sb.tile([P, H], U8, name="w1_scale", align_bytes=64)
         w1_cols = w1_raw[:].rearrange("p j (m t) -> p m j t", t=PACK)
         w1_bf = [sb.tile([P, PAIR * M * PACK], BF16, name=f"w1_bf{u}", align_bytes=64) for u in range(2)]
-        for u, copy in enumerate((nc.vector.tensor_copy, nc.scalar.copy)):
-            copy(
+        for u in range(2):
+            nc.vector.tensor_copy(
                 w1_bf[u][:].rearrange("p (t m j) -> p m j t", t=PAIR, j=PACK),
                 w1_cols[:, :, :, PAIR * u : PAIR * (u + 1)],
             )
-        for t0, t1 in ((0, 1), (1, 2), (2, 4)):
-            u, inner = divmod(t0, PAIR)
-            nc.vector.quantize_mx(
-                out=w1_codes[:, t0 * M : t1 * M].bitcast(FP8X4),
-                scales=w1_scale[:, t0 * M : t1 * M],
-                in_=w1_bf[u][:, inner * M * PACK : (inner + t1 - t0) * M * PACK],
+        for u in range(2):
+            cols = slice(u * PAIR * M, (u + 1) * PAIR * M)
+            nc.vector.quantize_mx(out=w1_codes[:, cols].bitcast(FP8X4), scales=w1_scale[:, cols], in_=w1_bf[u][:])
+
+        picked_codes = sb.tile([P, S], U32, name="picked_codes", align_bytes=64)
+        for h in range(2):
+            nc.vector.tensor_copy(
+                picked_codes[:, h * HALF : (h + 1) * HALF],
+                x_codes[:].bitcast(U32).indirect(offs_t[:, h * HALF // GROUP : (h + 1) * HALF // GROUP]),
             )
 
         y = [sb.tile([P, S], F32, name=f"y{t}", tag=f"y{t}", align_bytes=64) for t in range(PACK)]
         first = ORDER[0]
-        pieces = [(first, 0, HALF), (first, HALF, S)] + [(t, 0, S) for t in ORDER[1:]]
+        pieces = [(first, 0, HALF), (ORDER[1], 0, HALF), (first, HALF, S), (ORDER[1], HALF, S)] + [(t, 0, S) for t in ORDER[2:]]
         for b, (t, c0, c1) in enumerate(pieces):
             y_acc = ps.tile([M, c1 - c0], F32, name=f"y_acc{b}", tag=f"bank{b}")
             cols = slice(t * M, (t + 1) * M)
@@ -104,14 +110,15 @@ def tile_picked_bellman_none_po_kernel(
                 start=True,
                 stop=True,
             )
-            nc.scalar.copy(y[t][:, c0:c1], y_acc[:])
+            copy = nc.vector.tensor_copy if b == 1 else nc.scalar.copy
+            copy(y[t][:, c0:c1], y_acc[:])
 
         w2_codes = sb.tile([P, 2 * N], U8, name="w2_codes", align_bytes=64)
         nc.vector.tensor_copy(
             w2_codes[:].bitcast(U16).rearrange("p (t m) -> p m t", t=PACK),
             w2_raw[:].bitcast(U16).rearrange("p (m t) -> p m t", t=PACK),
         )
-        w2_scale_head = sb.tile([P, (PACK - 1) * M], U8, name="w2_scale_head", align_bytes=64)
+        w2_scale_head = sb.tile([P, (PACK - 1) * M], U8, name="w2_scale_head", tag="x_codes", align_bytes=64)
         w2_byte_cols = w2_bytes[:].rearrange("p (m t) -> p m t", t=PACK)
         nc.vector.tensor_copy(w2_scale_head[:].rearrange("p (t m) -> p m t", m=M), w2_byte_cols[:, :, : PACK - 1])
 

@@ -43,18 +43,21 @@ def tile_picked_bellman_none_po_kernel(
         src_t = lists.tile([P, V // GROUP], U16, name="src_t")
         dst_t = lists.tile([P, V // GROUP], U16, name="dst_t")
 
-        x_codes = sb.tile([P, T], I32, name="x_codes", tag="x_codes", align_bytes=64)
+        x_codes = sb.tile([P, T], I32, name="x_codes", align_bytes=64)
         x_bytes = sb.tile([P, T], U8, name="x_bytes", align_bytes=64)
         w1_raw = sb.tile([P, PACK, H], F32, name="w1_raw", align_bytes=64)
         ln_t = sb.tile([P, PACK, V], F32, name="ln_t", align_bytes=64)
         w2_bytes = sb.tile([P, N], U8, name="w2_bytes", align_bytes=64)
 
-        nc.gpsimd.memset(w2_bytes[:].bitcast(I32), 0)
         nc.gpsimd.memset(x_bytes[:SPREAD, :].bitcast(I32), 0)
+        nc.gpsimd.memset(w2_bytes[:SPREAD, :].bitcast(I32), 0)
         picked_bytes = sb.tile([P, S], U8, name="picked_bytes", align_bytes=64)
         nc.gpsimd.memset(picked_bytes[:].bitcast(I32), 0)
+        w2_scale = sb.tile([P, N], U8, name="w2_scale", align_bytes=64)
+        nc.gpsimd.memset(w2_scale[:].bitcast(I32), 0)
         nc.sync.dma_start(offs_t[:], offs)
         nc.scalar.dma_start(x_bytes[SPREAD:, :].bitcast(I32), x_scales[0].bitcast(I32))
+        nc.scalar.dma_start(w2_bytes[SPREAD:, :].bitcast(I32), w2_scales[0].bitcast(I32))
         nc.sync.dma_start(dst_t[:], dst)
         nc.sync.dma_start(w1_raw[:], w1.rearrange("(p j) c -> p j c", j=PACK))
         nc.sync.dma_start(x_codes[:], x_words[0].rearrange("p n t -> p (n t)").bitcast(I32))
@@ -62,10 +65,6 @@ def tile_picked_bellman_none_po_kernel(
         nc.sync.dma_start(w2_raw[:].bitcast(I32), w2_words[0].bitcast(I32))
         nc.sync.dma_start(src_t[:], src)
         nc.sync.dma_start(ln_t[:], ln.rearrange("(p t) v -> p t v", t=PACK))
-        for q in range(QUADS):
-            nc.gpsimd.dma_start(
-                w2_bytes[32 * q : 32 * q + 4, :].bitcast(I32), w2_scales[0, 4 * q : 4 * q + 4, :].bitcast(I32)
-            )
 
         spread_bytes = sb.tile([P, S], U8, name="spread_bytes", align_bytes=64)
         nc.vector.tensor_copy(spread_bytes[:], x_bytes[:].indirect(offs_t[:]))
@@ -73,6 +72,16 @@ def tile_picked_bellman_none_po_kernel(
             nc.scalar.dma_start(
                 picked_bytes[32 * q : 32 * q + 4, :].bitcast(I32),
                 spread_bytes[SPREAD + 4 * q : SPREAD + 4 * q + 4, :].bitcast(I32),
+            )
+
+        w2_dealt = sb.tile([P, N], U8, name="w2_dealt", align_bytes=64)
+        nc.vector.tensor_copy(
+            w2_dealt[:].rearrange("p (t m) -> p m t", t=PACK), w2_bytes[:].rearrange("p (m t) -> p m t", t=PACK)
+        )
+        for q in range(QUADS):
+            nc.sync.dma_start(
+                w2_scale[32 * q : 32 * q + 4, :].bitcast(I32),
+                w2_dealt[SPREAD + 4 * q : SPREAD + 4 * q + 4, :].bitcast(I32),
             )
 
         w1_codes = sb.tile([P, H], U32, name="w1_codes", align_bytes=64)
@@ -113,14 +122,11 @@ def tile_picked_bellman_none_po_kernel(
             copy = nc.vector.tensor_copy if b == 1 else nc.scalar.copy
             copy(y[t][:, c0:c1], y_acc[:])
 
-        w2_codes = sb.tile([P, 2 * N], U8, name="w2_codes", align_bytes=64)
+        w2_head = sb.tile([P, 2 * (PACK - 1) * M], U8, name="w2_head", align_bytes=64)
+        w2_word_cols = w2_raw[:].bitcast(U16).rearrange("p (m t) -> p m t", t=PACK)
         nc.vector.tensor_copy(
-            w2_codes[:].bitcast(U16).rearrange("p (t m) -> p m t", t=PACK),
-            w2_raw[:].bitcast(U16).rearrange("p (m t) -> p m t", t=PACK),
+            w2_head[:].bitcast(U16).rearrange("p (t m) -> p m t", m=M), w2_word_cols[:, :, : PACK - 1]
         )
-        w2_scale_head = sb.tile([P, (PACK - 1) * M], U8, name="w2_scale_head", tag="x_codes", align_bytes=64)
-        w2_byte_cols = w2_bytes[:].rearrange("p (m t) -> p m t", t=PACK)
-        nc.vector.tensor_copy(w2_scale_head[:].rearrange("p (t m) -> p m t", m=M), w2_byte_cols[:, :, : PACK - 1])
 
         old = sb.tile([P, PACK, V], F32, name="old", tag="old", align_bytes=64)
         new = sb.tile([P, PACK, V], F32, name="new", align_bytes=64)
@@ -158,16 +164,16 @@ def tile_picked_bellman_none_po_kernel(
         nc.vector.tensor_tensor(new[:, 3, :], old[:, 3, :], new[:, 3, :], MIN)
         put_back(2)
 
-        w2_scale_tail = sb.tile([P, M], U8, name="w2_scale_tail", tag="old", align_bytes=64)
-        nc.vector.tensor_copy(w2_scale_tail[:], w2_byte_cols[:, :, PACK - 1])
-        w2_scale = [w2_scale_head[:, t * M : (t + 1) * M] for t in range(PACK - 1)] + [w2_scale_tail[:]]
+        w2_tail = sb.tile([P, 2 * M], U8, name="w2_tail", tag="old", align_bytes=64)
+        nc.vector.tensor_copy(w2_tail[:].bitcast(U16), w2_word_cols[:, :, PACK - 1])
+        w2_codes = [w2_head[:, 2 * M * t : 2 * M * (t + 1)] for t in range(PACK - 1)] + [w2_tail[:]]
 
         warm = ps.tile([M, S], F32, name="warm", tag="bank7")
         for rep in range(WARM_PASSES):
             nc.tensor.matmul_mx(
                 out=warm[:],
-                lhsT=w2_codes[:, 2 * M * (PACK - 1) :].bitcast(FP4X4),
-                lhsT_scale=w2_scale[PACK - 1],
+                lhsT=w2_codes[PACK - 1].bitcast(FP4X4),
+                lhsT_scale=w2_scale[:, (PACK - 1) * M :],
                 rhs=picked_codes[:].bitcast(FP8X4),
                 rhs_scale=picked_bytes[:],
                 start=True,
@@ -214,8 +220,8 @@ def tile_picked_bellman_none_po_kernel(
                     t = PAIR * u + inner
                     nc.tensor.matmul_mx(
                         out=out_acc[:, inner, :],
-                        lhsT=w2_codes[:, 2 * M * t : 2 * M * (t + 1)].bitcast(FP4X4),
-                        lhsT_scale=w2_scale[t],
+                        lhsT=w2_codes[t].bitcast(FP4X4),
+                        lhsT_scale=w2_scale[:, t * M : (t + 1) * M],
                         rhs=z_codes[:, cols].bitcast(FP8X4),
                         rhs_scale=z_scale[:, cols],
                         start=True,

@@ -26,7 +26,7 @@ SPREAD = P - 16
 QUARTER = S // 4
 PAIR = 2
 ORDER = (0, 2, 3, 1)
-VECTOR_BANKS = ((0, 1), (3, 1))
+VECTOR_BANKS = ((0, 1), (1, 1))
 WARM_PASSES = 2
 
 
@@ -37,16 +37,16 @@ def tile_picked_bellman_none_po_kernel(
     with ExitStack() as ctx:
         lists = ctx.enter_context(tc.tile_pool(name="lists", bufs=1))
         sb = ctx.enter_context(tc.tile_pool(name="sb", bufs=1))
+        reuse = ctx.enter_context(tc.tile_pool(name="reuse", bufs=1))
         ps = ctx.enter_context(tc.psum_pool(name="ps", bufs=1))
 
         offs_t = lists.tile([P, S // GROUP], U16, name="offs_t")
         src_t = lists.tile([P, V // GROUP], U16, name="src_t")
         dst_t = lists.tile([P, V // GROUP], U16, name="dst_t")
 
-        x_codes = sb.tile([P, T], I32, name="x_codes", align_bytes=64)
-        x_bytes = sb.tile([P, T], U8, name="x_bytes", align_bytes=64)
+        x_codes = sb.tile([P, T], I32, name="x_codes", tag="x_codes", align_bytes=64)
+        x_bytes = reuse.tile([P, T], U8, name="x_bytes", offset=0)
         w1_raw = sb.tile([P, PACK, H], F32, name="w1_raw", align_bytes=64)
-        ln_t = sb.tile([P, PACK, V], F32, name="ln_t", align_bytes=64)
         w2_bytes = sb.tile([P, N], U8, name="w2_bytes", align_bytes=64)
 
         nc.gpsimd.memset(x_bytes[:SPREAD, :].bitcast(I32), 0)
@@ -61,18 +61,19 @@ def tile_picked_bellman_none_po_kernel(
         nc.sync.dma_start(dst_t[:], dst)
         nc.sync.dma_start(w1_raw[:], w1.rearrange("(p j) c -> p j c", j=PACK))
         nc.sync.dma_start(x_codes[:], x_words[0].rearrange("p n t -> p (n t)").bitcast(I32))
-        w2_raw = sb.tile([P, 2 * N], U8, name="w2_raw", align_bytes=64)
-        nc.sync.dma_start(w2_raw[:].bitcast(I32), w2_words[0].bitcast(I32))
         nc.sync.dma_start(src_t[:], src)
-        nc.sync.dma_start(ln_t[:], ln.rearrange("(p t) v -> p t v", t=PACK))
 
         spread_bytes = sb.tile([P, S], U8, name="spread_bytes", align_bytes=64)
         nc.vector.tensor_copy(spread_bytes[:], x_bytes[:].indirect(offs_t[:]))
         for q in range(QUADS):
-            nc.scalar.dma_start(
+            nc.sync.dma_start(
                 picked_bytes[32 * q : 32 * q + 4, :].bitcast(I32),
                 spread_bytes[SPREAD + 4 * q : SPREAD + 4 * q + 4, :].bitcast(I32),
             )
+        w2_raw = reuse.tile([P, 2 * N], U8, name="w2_raw", offset=0)
+        nc.sync.dma_start(w2_raw[:].bitcast(I32), w2_words[0].bitcast(I32))
+        ln_t = reuse.tile([P, PACK, V], F32, name="ln_t", offset=2 * N)
+        nc.sync.dma_start(ln_t[:], ln.rearrange("(p t) v -> p t v", t=PACK))
 
         w2_dealt = sb.tile([P, N], U8, name="w2_dealt", align_bytes=64)
         nc.vector.tensor_copy(
@@ -106,7 +107,8 @@ def tile_picked_bellman_none_po_kernel(
 
         y = [sb.tile([P, S], F32, name=f"y{t}", tag=f"y{t}", align_bytes=64) for t in range(PACK)]
         first = ORDER[0]
-        pieces = [(first, 0, HALF), (ORDER[1], 0, HALF), (first, HALF, S), (ORDER[1], HALF, S)] + [(t, 0, S) for t in ORDER[2:]]
+        pieces = [(first, 0, HALF), (ORDER[1], 0, HALF), (first, HALF, S - QUARTER), (first, S - QUARTER, S), (ORDER[1], HALF, S)]
+        pieces = pieces + [(t, 0, S) for t in ORDER[2:]]
         for b, (t, c0, c1) in enumerate(pieces):
             y_acc = ps.tile([M, c1 - c0], F32, name=f"y_acc{b}", tag=f"bank{b}")
             cols = slice(t * M, (t + 1) * M)
@@ -119,10 +121,10 @@ def tile_picked_bellman_none_po_kernel(
                 start=True,
                 stop=True,
             )
-            copy = nc.vector.tensor_copy if b == 1 else nc.scalar.copy
+            copy = nc.vector.tensor_copy if b == 2 else nc.scalar.copy
             copy(y[t][:, c0:c1], y_acc[:])
 
-        w2_head = sb.tile([P, 2 * (PACK - 1) * M], U8, name="w2_head", align_bytes=64)
+        w2_head = sb.tile([P, 2 * (PACK - 1) * M], U8, name="w2_head", tag="x_codes", align_bytes=64)
         w2_word_cols = w2_raw[:].bitcast(U16).rearrange("p (m t) -> p m t", t=PACK)
         nc.vector.tensor_copy(
             w2_head[:].bitcast(U16).rearrange("p (t m) -> p m t", m=M), w2_word_cols[:, :, : PACK - 1]
@@ -210,7 +212,7 @@ def tile_picked_bellman_none_po_kernel(
                 res[q][:].rearrange("p t (c i) -> p c t i", i=4),
             )
 
-        for q in range(S // QUARTER):
+        for q in range(S // QUARTER - 1):
             cols = slice(q * QUARTER, (q + 1) * QUARTER)
             res.append(sb.tile([P, PACK, QUARTER], F32, name=f"res{q}", align_bytes=64))
             for u in range(PACK // PAIR):
@@ -236,13 +238,27 @@ def tile_picked_bellman_none_po_kernel(
             if q == 1:
                 interleave(nc.vector.tensor_copy, 0)
                 interleave(nc.vector.tensor_copy, 1)
+        cols = slice(S - QUARTER, S)
+        last_acc = ps.tile([M, PACK, QUARTER], F32, name="last_acc", tag="bank6")
+        for t in range(PACK):
+            nc.tensor.matmul_mx(
+                out=last_acc[:, t, :],
+                lhsT=w2_codes[t].bitcast(FP4X4),
+                lhsT_scale=w2_scale[:, t * M : (t + 1) * M],
+                rhs=z_codes[:, cols].bitcast(FP8X4),
+                rhs_scale=z_scale[:, cols],
+                start=True,
+                stop=True,
+            )
+        res_last = sb.tile([P, PACK, QUARTER], F32, name="res_last", align_bytes=64)
+        nc.scalar.copy(res_last[:], last_acc[:])
+        nc.sync.dma_start(out_rows[:, :, cols], res_last[:])
+        nc.scalar.copy(res_bf[:, cols, :], last_acc[:].rearrange("p t c -> p c t"))
         interleave(nc.vector.tensor_copy, 2)
-        interleave(nc.scalar.copy, 3)
         quantize(out_codes, out_scale, res_flat, 0, HALF)
         quantize(out_codes, out_scale, res_flat, HALF, S - QUARTER)
-        nc.sync.dma_start(out_words[:, : S - QUARTER], out_codes[:, : S - QUARTER])
         quantize(out_codes, out_scale, res_flat, S - QUARTER, S)
-        nc.sync.dma_start(out_words[:, S - QUARTER :], out_codes[:, S - QUARTER :])
+        nc.sync.dma_start(out_words, out_codes[:])
         for q in range(QUADS):
             queue = nc.sync if q % 2 else nc.scalar
             queue.dma_start(

@@ -130,7 +130,7 @@ def tile_picked_bellman_none_po_kernel(
             w2_head[:].bitcast(U16).rearrange("p (t m) -> p m t", m=M), w2_word_cols[:, :, : PACK - 1]
         )
 
-        old = sb.tile([P, PACK, V], F32, name="old", tag="old", align_bytes=64)
+        old = sb.tile([P, PACK, V], F32, name="old", align_bytes=64)
         new = sb.tile([P, PACK, V], F32, name="new", align_bytes=64)
 
         def fetch_old(i):
@@ -141,7 +141,8 @@ def tile_picked_bellman_none_po_kernel(
 
         z_bf = sb.tile([P, S, PACK], BF16, name="z_bf", align_bytes=64)
         last = ORDER[PACK - 1]
-        relaxed = [ln_t[:, 0, :], ln_t[:, 3, :], new[:, 2, :], new[:, 3, :]]
+        relaxed2 = sb.tile([P, V], F32, name="relaxed2", tag="relaxed2", align_bytes=64)
+        relaxed = [ln_t[:, 0, :], ln_t[:, 3, :], relaxed2[:], new[:, 3, :]]
 
         def put_back(i):
             t = ORDER[i]
@@ -161,13 +162,16 @@ def tile_picked_bellman_none_po_kernel(
         nc.scalar.copy(z_last[:], y[last][:])
         fetch_old(3)
         fetch_new(3)
-        nc.vector.tensor_tensor(new[:, 2, :], old[:, 2, :], new[:, 2, :], MIN)
+        nc.vector.tensor_tensor(relaxed[2], old[:, 2, :], new[:, 2, :], MIN)
         put_back(1)
         nc.vector.tensor_tensor(new[:, 3, :], old[:, 3, :], new[:, 3, :], MIN)
         put_back(2)
 
-        w2_tail = sb.tile([P, 2 * M], U8, name="w2_tail", tag="old", align_bytes=64)
-        nc.vector.tensor_copy(w2_tail[:].bitcast(U16), w2_word_cols[:, :, PACK - 1])
+        w2_tail = sb.tile([P, 2 * M], U8, name="w2_tail", tag="relaxed2", align_bytes=64)
+        nc.gpsimd.tensor_copy(
+            w2_tail[:].rearrange("p (m b) -> p m b", b=2),
+            w2_raw[:].rearrange("p (m t b) -> p m t b", t=PACK, b=2)[:, :, PACK - 1, :],
+        )
         w2_codes = [w2_head[:, 2 * M * t : 2 * M * (t + 1)] for t in range(PACK - 1)] + [w2_tail[:]]
 
         warm = ps.tile([M, S], F32, name="warm", tag="bank7")

@@ -47,17 +47,12 @@ def tile_picked_bellman_none_po_kernel(
         x_codes = sb.tile([P, T], I32, name="x_codes", tag="x_codes", align_bytes=64)
         x_bytes = reuse.tile([P, T], U8, name="x_bytes", offset=0)
         w1_raw = sb.tile([P, PACK, H], F32, name="w1_raw", align_bytes=64)
-        w2_bytes = sb.tile([P, N], U8, name="w2_bytes", align_bytes=64)
 
         nc.gpsimd.memset(x_bytes[:SPREAD, :].bitcast(I32), 0)
-        nc.gpsimd.memset(w2_bytes[:SPREAD, :].bitcast(I32), 0)
         picked_bytes = sb.tile([P, S], U8, name="picked_bytes", align_bytes=64)
         nc.gpsimd.memset(picked_bytes[:].bitcast(I32), 0)
-        w2_scale = sb.tile([P, N], U8, name="w2_scale", align_bytes=64)
-        nc.gpsimd.memset(w2_scale[:].bitcast(I32), 0)
         nc.sync.dma_start(offs_t[:], offs)
         nc.scalar.dma_start(x_bytes[SPREAD:, :].bitcast(I32), x_scales[0].bitcast(I32))
-        nc.scalar.dma_start(w2_bytes[SPREAD:, :].bitcast(I32), w2_scales[0].bitcast(I32))
         nc.sync.dma_start(dst_t[:], dst)
         nc.sync.dma_start(w1_raw[:], w1.rearrange("(p j) c -> p j c", j=PACK))
         nc.sync.dma_start(x_codes[:], x_words[0].rearrange("p n t -> p (n t)").bitcast(I32))
@@ -72,17 +67,14 @@ def tile_picked_bellman_none_po_kernel(
             )
         w2_raw = reuse.tile([P, 2 * N], U8, name="w2_raw", offset=0)
         nc.sync.dma_start(w2_raw[:].bitcast(I32), w2_words[0].bitcast(I32))
-        ln_t = reuse.tile([P, PACK, V], F32, name="ln_t", offset=2 * N)
+        ln_t = reuse.tile([P, PACK, V], F32, name="ln_t", offset=3 * N)
         nc.sync.dma_start(ln_t[:], ln.rearrange("(p t) v -> p t v", t=PACK))
 
-        w2_dealt = sb.tile([P, N], U8, name="w2_dealt", align_bytes=64)
-        nc.vector.tensor_copy(
-            w2_dealt[:].rearrange("p (t m) -> p m t", t=PACK), w2_bytes[:].rearrange("p (m t) -> p m t", t=PACK)
-        )
+        w2_bytes = reuse.tile([P, N], U8, name="w2_bytes", offset=2 * N)
+        nc.gpsimd.memset(w2_bytes[:].bitcast(I32), 0)
         for q in range(QUADS):
             nc.sync.dma_start(
-                w2_scale[32 * q : 32 * q + 4, :].bitcast(I32),
-                w2_dealt[SPREAD + 4 * q : SPREAD + 4 * q + 4, :].bitcast(I32),
+                w2_bytes[32 * q : 32 * q + 4, :].bitcast(I32), w2_scales[0, 4 * q : 4 * q + 4, :].bitcast(I32)
             )
 
         w1_codes = sb.tile([P, H], U32, name="w1_codes", align_bytes=64)
@@ -124,17 +116,21 @@ def tile_picked_bellman_none_po_kernel(
             copy = nc.vector.tensor_copy if b == 2 else nc.scalar.copy
             copy(y[t][:, c0:c1], y_acc[:])
 
-        w2_head = sb.tile([P, 2 * (PACK - 1) * M], U8, name="w2_head", tag="x_codes", align_bytes=64)
-        w2_word_cols = w2_raw[:].bitcast(U16).rearrange("p (m t) -> p m t", t=PACK)
+        w2_dealt = sb.tile([P, 2 * N], U8, name="w2_dealt", tag="x_codes", align_bytes=64)
         nc.vector.tensor_copy(
-            w2_head[:].bitcast(U16).rearrange("p (t m) -> p m t", m=M), w2_word_cols[:, :, : PACK - 1]
+            w2_dealt[:].bitcast(U16).rearrange("p (t m) -> p m t", t=PACK),
+            w2_raw[:].bitcast(U16).rearrange("p (m t) -> p m t", t=PACK),
         )
+        w2_codes = [w2_dealt[:, 2 * M * t : 2 * M * (t + 1)] for t in range(PACK)]
 
-        old = sb.tile([P, PACK, V], F32, name="old", align_bytes=64)
+        old = sb.tile([P, PACK - 1, V], F32, name="old", align_bytes=64)
         new = sb.tile([P, PACK, V], F32, name="new", align_bytes=64)
 
+        old2 = sb.tile([P, V], F32, name="old2", tag="old2", align_bytes=64)
+        olds = [old[:, 0, :], old[:, 1, :], old2[:], old[:, 2, :]]
+
         def fetch_old(i):
-            nc.vector.tensor_copy(old[:, i, :], y[ORDER[i]][:].indirect(dst_t[:]))
+            nc.vector.tensor_copy(olds[i], y[ORDER[i]][:].indirect(dst_t[:]))
 
         def fetch_new(i):
             nc.vector.tensor_tensor(new[:, i, :], y[ORDER[i]][:].indirect(src_t[:]), ln_t[:, ORDER[i], :], ADD)
@@ -162,24 +158,24 @@ def tile_picked_bellman_none_po_kernel(
         nc.scalar.copy(z_last[:], y[last][:])
         fetch_old(3)
         fetch_new(3)
-        nc.vector.tensor_tensor(relaxed[2], old[:, 2, :], new[:, 2, :], MIN)
+        nc.vector.tensor_tensor(relaxed[2], olds[2], new[:, 2, :], MIN)
+        w2_byte_cols = w2_bytes[:].rearrange("p (m t) -> p t m", t=PACK)
+        w2_scale_head = sb.tile([P, PACK - 1, M], U8, name="w2_scale_head", tag="old2", align_bytes=64)
+        nc.gpsimd.tensor_copy(w2_scale_head[:], w2_byte_cols[:, : PACK - 1, :])
         put_back(1)
-        nc.vector.tensor_tensor(new[:, 3, :], old[:, 3, :], new[:, 3, :], MIN)
+        nc.vector.tensor_tensor(new[:, 3, :], olds[3], new[:, 3, :], MIN)
         put_back(2)
 
-        w2_tail = sb.tile([P, 2 * M], U8, name="w2_tail", tag="relaxed2", align_bytes=64)
-        nc.gpsimd.tensor_copy(
-            w2_tail[:].rearrange("p (m b) -> p m b", b=2),
-            w2_raw[:].rearrange("p (m t b) -> p m t b", t=PACK, b=2)[:, :, PACK - 1, :],
-        )
-        w2_codes = [w2_head[:, 2 * M * t : 2 * M * (t + 1)] for t in range(PACK - 1)] + [w2_tail[:]]
+        w2_scale_tail = sb.tile([P, M], U8, name="w2_scale_tail", tag="relaxed2", align_bytes=64)
+        nc.gpsimd.tensor_copy(w2_scale_tail[:], w2_byte_cols[:, PACK - 1, :])
+        w2_scale = [w2_scale_head[:, t, :] for t in range(PACK - 1)] + [w2_scale_tail[:]]
 
         warm = ps.tile([M, S], F32, name="warm", tag="bank7")
         for rep in range(WARM_PASSES):
             nc.tensor.matmul_mx(
                 out=warm[:],
                 lhsT=w2_codes[PACK - 1].bitcast(FP4X4),
-                lhsT_scale=w2_scale[:, (PACK - 1) * M :],
+                lhsT_scale=w2_scale[PACK - 1],
                 rhs=picked_codes[:].bitcast(FP8X4),
                 rhs_scale=picked_bytes[:],
                 start=True,
@@ -227,7 +223,7 @@ def tile_picked_bellman_none_po_kernel(
                     nc.tensor.matmul_mx(
                         out=out_acc[:, inner, :],
                         lhsT=w2_codes[t].bitcast(FP4X4),
-                        lhsT_scale=w2_scale[:, t * M : (t + 1) * M],
+                        lhsT_scale=w2_scale[t],
                         rhs=z_codes[:, cols].bitcast(FP8X4),
                         rhs_scale=z_scale[:, cols],
                         start=True,
@@ -248,7 +244,7 @@ def tile_picked_bellman_none_po_kernel(
             nc.tensor.matmul_mx(
                 out=last_acc[:, t, :],
                 lhsT=w2_codes[t].bitcast(FP4X4),
-                lhsT_scale=w2_scale[:, t * M : (t + 1) * M],
+                lhsT_scale=w2_scale[t],
                 rhs=z_codes[:, cols].bitcast(FP8X4),
                 rhs_scale=z_scale[:, cols],
                 start=True,

@@ -45,25 +45,35 @@ def tile_picked_bellman_none_po_kernel(
         dst_t = lists.tile([P, V // GROUP], U16, name="dst_t")
 
         x_codes = sb.tile([P, T], I32, name="x_codes", tag="x_codes", align_bytes=64)
-        x_bytes = reuse.tile([P, T], U8, name="x_bytes", offset=0)
-        w1_raw = sb.tile([P, PACK, H], F32, name="w1_raw", align_bytes=64)
+        x_bytes = sb.tile([P, T], U8, name="x_bytes", align_bytes=64)
+        w1_raw = reuse.tile([P, PACK, H], F32, name="w1_raw", offset=0)
 
         nc.gpsimd.memset(x_bytes[:SPREAD, :].bitcast(I32), 0)
         picked_bytes = sb.tile([P, S], U8, name="picked_bytes", align_bytes=64)
         nc.gpsimd.memset(picked_bytes[:].bitcast(I32), 0)
         nc.sync.dma_start(offs_t[:], offs)
         nc.scalar.dma_start(x_bytes[SPREAD:, :].bitcast(I32), x_scales[0].bitcast(I32))
-        nc.sync.dma_start(dst_t[:], dst)
         nc.sync.dma_start(w1_raw[:], w1.rearrange("(p j) c -> p j c", j=PACK))
+        nc.sync.dma_start(dst_t[:], dst)
         nc.sync.dma_start(x_codes[:], x_words[0].rearrange("p n t -> p (n t)").bitcast(I32))
         nc.sync.dma_start(src_t[:], src)
 
         spread_bytes = sb.tile([P, S], U8, name="spread_bytes", align_bytes=64)
         nc.vector.tensor_copy(spread_bytes[:], x_bytes[:].indirect(offs_t[:]))
         for q in range(QUADS):
-            nc.sync.dma_start(
+            nc.scalar.dma_start(
                 picked_bytes[32 * q : 32 * q + 4, :].bitcast(I32),
                 spread_bytes[SPREAD + 4 * q : SPREAD + 4 * q + 4, :].bitcast(I32),
+            )
+
+        w1_codes = sb.tile([P, H], U32, name="w1_codes", align_bytes=64)
+        w1_scale = sb.tile([P, H], U8, name="w1_scale", align_bytes=64)
+        w1_cols = w1_raw[:].rearrange("p j (m t) -> p m j t", t=PACK)
+        w1_bf = [sb.tile([P, PAIR * M * PACK], BF16, name=f"w1_bf{u}", align_bytes=64) for u in range(2)]
+        for u in range(2):
+            nc.vector.tensor_copy(
+                w1_bf[u][:].rearrange("p (t m j) -> p m j t", t=PAIR, j=PACK),
+                w1_cols[:, :, :, PAIR * u : PAIR * (u + 1)],
             )
         w2_raw = reuse.tile([P, 2 * N], U8, name="w2_raw", offset=0)
         nc.sync.dma_start(w2_raw[:].bitcast(I32), w2_words[0].bitcast(I32))
@@ -77,15 +87,6 @@ def tile_picked_bellman_none_po_kernel(
                 w2_bytes[32 * q : 32 * q + 4, :].bitcast(I32), w2_scales[0, 4 * q : 4 * q + 4, :].bitcast(I32)
             )
 
-        w1_codes = sb.tile([P, H], U32, name="w1_codes", align_bytes=64)
-        w1_scale = sb.tile([P, H], U8, name="w1_scale", align_bytes=64)
-        w1_cols = w1_raw[:].rearrange("p j (m t) -> p m j t", t=PACK)
-        w1_bf = [sb.tile([P, PAIR * M * PACK], BF16, name=f"w1_bf{u}", align_bytes=64) for u in range(2)]
-        for u in range(2):
-            nc.vector.tensor_copy(
-                w1_bf[u][:].rearrange("p (t m j) -> p m j t", t=PAIR, j=PACK),
-                w1_cols[:, :, :, PAIR * u : PAIR * (u + 1)],
-            )
         for u in range(2):
             cols = slice(u * PAIR * M, (u + 1) * PAIR * M)
             nc.vector.quantize_mx(out=w1_codes[:, cols].bitcast(FP8X4), scales=w1_scale[:, cols], in_=w1_bf[u][:])

@@ -26,7 +26,6 @@ SPREAD = P - 16
 QUARTER = S // 4
 PAIR = 2
 ORDER = (0, 2, 3, 1)
-VECTOR_BANKS = ((0, 1), (1, 1))
 WARM_PASSES = 2
 
 
@@ -205,45 +204,17 @@ def tile_picked_bellman_none_po_kernel(
 
         res_bf = sb.tile([P, S, PACK], BF16, name="res_bf", align_bytes=64)
         res_flat = res_bf[:].rearrange("p c t -> p (c t)")
-        res = []
+        res = sb.tile([P, PACK, S], F32, name="res", align_bytes=64)
 
-        def interleave(copy, q):
-            copy(
-                res_bf[:, q * QUARTER : (q + 1) * QUARTER, :].rearrange("p (c i) t -> p c t i", i=4),
-                res[q][:].rearrange("p t (c i) -> p c t i", i=4),
+        def interleave(c0, c1):
+            nc.vector.tensor_copy(
+                res_bf[:, c0:c1, :].rearrange("p (c i) t -> p c t i", i=4),
+                res[:, :, c0:c1].rearrange("p t (c i) -> p c t i", i=4),
             )
 
-        for q in range(S // QUARTER - 1):
-            cols = slice(q * QUARTER, (q + 1) * QUARTER)
-            res.append(sb.tile([P, PACK, QUARTER], F32, name=f"res{q}", align_bytes=64))
-            for u in range(PACK // PAIR):
-                planes = slice(PAIR * u, PAIR * (u + 1))
-                out_acc = ps.tile([M, PAIR, QUARTER], F32, name=f"out_acc{q}{u}", tag=f"bank{PAIR * q + u}")
-                for inner in range(PAIR):
-                    t = PAIR * u + inner
-                    nc.tensor.matmul_mx(
-                        out=out_acc[:, inner, :],
-                        lhsT=w2_codes[t].bitcast(FP4X4),
-                        lhsT_scale=w2_scale[t],
-                        rhs=z_codes[:, cols].bitcast(FP8X4),
-                        rhs_scale=z_scale[:, cols],
-                        start=True,
-                        stop=True,
-                    )
-                copy = nc.vector.tensor_copy if (q, u) in VECTOR_BANKS else nc.scalar.copy
-                copy(res[q][:, planes, :], out_acc[:])
-                if q == 0:
-                    nc.sync.dma_start(out_rows[:, planes, cols], res[q][:, planes, :])
-            if q > 0:
-                nc.sync.dma_start(out_rows[:, :, cols], res[q][:])
-            if q == 1:
-                interleave(nc.vector.tensor_copy, 0)
-                interleave(nc.vector.tensor_copy, 1)
-        cols = slice(S - QUARTER, S)
-        last_acc = ps.tile([M, PACK, QUARTER], F32, name="last_acc", tag="bank6")
-        for t in range(PACK):
+        def multiply(acc, t, cols):
             nc.tensor.matmul_mx(
-                out=last_acc[:, t, :],
+                out=acc,
                 lhsT=w2_codes[t].bitcast(FP4X4),
                 lhsT_scale=w2_scale[t],
                 rhs=z_codes[:, cols].bitcast(FP8X4),
@@ -251,11 +222,36 @@ def tile_picked_bellman_none_po_kernel(
                 start=True,
                 stop=True,
             )
-        res_last = sb.tile([P, PACK, QUARTER], F32, name="res_last", align_bytes=64)
-        nc.scalar.copy(res_last[:], last_acc[:])
-        nc.sync.dma_start(out_rows[:, :, cols], res_last[:])
-        nc.scalar.copy(res_bf[:, cols, :], last_acc[:].rearrange("p t c -> p c t"))
-        interleave(nc.vector.tensor_copy, 2)
+
+        def store(u, q0, q1):
+            planes = slice(PAIR * u, PAIR * (u + 1))
+            cols = slice(q0 * QUARTER, q1 * QUARTER)
+            nc.sync.dma_start(out_rows[:, planes, cols], res[:, planes, cols])
+
+        for b, (q, u) in enumerate(((0, 0), (0, 1), (1, 1), (1, 0), (2, 0), (2, 1))):
+            cols = slice(q * QUARTER, (q + 1) * QUARTER)
+            out_acc = ps.tile([M, PAIR, QUARTER], F32, name=f"out_acc{b}", tag=f"bank{b}")
+            for inner in range(PAIR):
+                multiply(out_acc[:, inner, :], PAIR * u + inner, cols)
+            copy = nc.vector.tensor_copy if b in (1, 3) else nc.scalar.copy
+            copy(res[:, PAIR * u : PAIR * (u + 1), cols], out_acc[:])
+            if b % 2 == 0:
+                store(u, max(q - 1, 0), q + 1)
+            if b == 3:
+                interleave(0, QUARTER)
+                interleave(QUARTER, HALF)
+        cols = slice(S - QUARTER, S)
+        last_acc = ps.tile([M, PACK, QUARTER], F32, name="last_acc", tag="bank6")
+        for t in range(PACK):
+            multiply(last_acc[:, t, :], t, cols)
+        for u in (1, 0):
+            planes = slice(PAIR * u, PAIR * (u + 1))
+            nc.scalar.copy(res[:, planes, cols], last_acc[:, planes, :])
+            store(u, 3 - u, 4)
+        share = 96
+        nc.scalar.copy(res_bf[:, S - QUARTER : S - QUARTER + share, :], last_acc[:, :, :share].rearrange("p t c -> p c t"))
+        interleave(HALF, S - QUARTER)
+        interleave(S - QUARTER + share, S)
         quantize(out_codes, out_scale, res_flat, 0, HALF)
         quantize(out_codes, out_scale, res_flat, HALF, S - QUARTER)
         quantize(out_codes, out_scale, res_flat, S - QUARTER, S)

@@ -26,7 +26,7 @@ SPREAD = P - 16
 QUARTER = S // 4
 PAIR = 2
 ORDER = (0, 2, 3, 1)
-WARM_PASSES = 2
+NARROW = 64
 
 
 def tile_picked_bellman_none_po_kernel(
@@ -74,17 +74,10 @@ def tile_picked_bellman_none_po_kernel(
                 w1_bf[u][:].rearrange("p (t m j) -> p m j t", t=PAIR, j=PACK),
                 w1_cols[:, :, :, PAIR * u : PAIR * (u + 1)],
             )
+        ln_t = reuse.tile([P, PACK, V], F32, name="ln_t", offset=2 * N)
+        nc.sync.dma_start(ln_t[:], ln.rearrange("(p t) v -> p t v", t=PACK))
         w2_raw = reuse.tile([P, 2 * N], U8, name="w2_raw", offset=0)
         nc.sync.dma_start(w2_raw[:].bitcast(I32), w2_words[0].bitcast(I32))
-        ln_t = reuse.tile([P, PACK, V], F32, name="ln_t", offset=3 * N)
-        nc.sync.dma_start(ln_t[:], ln.rearrange("(p t) v -> p t v", t=PACK))
-
-        w2_bytes = reuse.tile([P, N], U8, name="w2_bytes", offset=2 * N)
-        nc.gpsimd.memset(w2_bytes[:].bitcast(I32), 0)
-        for q in range(QUADS):
-            nc.sync.dma_start(
-                w2_bytes[32 * q : 32 * q + 4, :].bitcast(I32), w2_scales[0, 4 * q : 4 * q + 4, :].bitcast(I32)
-            )
 
         for u in range(2):
             cols = slice(u * PAIR * M, (u + 1) * PAIR * M)
@@ -97,6 +90,13 @@ def tile_picked_bellman_none_po_kernel(
                 x_codes[:].bitcast(U32).indirect(offs_t[:, h * HALF // GROUP : (h + 1) * HALF // GROUP]),
             )
 
+        w2_bytes = sb.tile([P, N], U8, name="w2_bytes", tag="x_codes", align_bytes=64)
+        nc.gpsimd.memset(w2_bytes[:].bitcast(I32), 0)
+        for q in range(QUADS):
+            nc.sync.dma_start(
+                w2_bytes[32 * q : 32 * q + 4, :].bitcast(I32), w2_scales[0, 4 * q : 4 * q + 4, :].bitcast(I32)
+            )
+
         y = [sb.tile([P, S], F32, name=f"y{t}", tag=f"y{t}", align_bytes=64) for t in range(PACK)]
         first = ORDER[0]
         pieces = [(first, 0, HALF), (ORDER[1], 0, HALF), (first, HALF, S - QUARTER), (first, S - QUARTER, S), (ORDER[1], HALF, S)]
@@ -104,26 +104,20 @@ def tile_picked_bellman_none_po_kernel(
         for b, (t, c0, c1) in enumerate(pieces):
             y_acc = ps.tile([M, c1 - c0], F32, name=f"y_acc{b}", tag=f"bank{b}")
             cols = slice(t * M, (t + 1) * M)
-            nc.tensor.matmul_mx(
-                out=y_acc[:],
-                lhsT=w1_codes[:, cols].bitcast(FP8X4),
-                lhsT_scale=w1_scale[:, cols],
-                rhs=picked_codes[:, c0:c1].bitcast(FP8X4),
-                rhs_scale=picked_bytes[:, c0:c1],
-                start=True,
-                stop=True,
-            )
+            for c in range(c0, c1, QUARTER):
+                nc.tensor.matmul_mx(
+                    out=y_acc[:, c - c0 : c - c0 + QUARTER],
+                    lhsT=w1_codes[:, cols].bitcast(FP8X4),
+                    lhsT_scale=w1_scale[:, cols],
+                    rhs=picked_codes[:, c : c + QUARTER].bitcast(FP8X4),
+                    rhs_scale=picked_bytes[:, c : c + QUARTER],
+                    start=True,
+                    stop=True,
+                )
             copy = nc.vector.tensor_copy if b == 2 else nc.scalar.copy
             copy(y[t][:, c0:c1], y_acc[:])
 
-        w2_dealt = sb.tile([P, 2 * N], U8, name="w2_dealt", tag="x_codes", align_bytes=64)
-        nc.vector.tensor_copy(
-            w2_dealt[:].bitcast(U16).rearrange("p (t m) -> p m t", t=PACK),
-            w2_raw[:].bitcast(U16).rearrange("p (m t) -> p m t", t=PACK),
-        )
-        w2_codes = [w2_dealt[:, 2 * M * t : 2 * M * (t + 1)] for t in range(PACK)]
-
-        old = sb.tile([P, PACK - 1, V], F32, name="old", align_bytes=64)
+        old = sb.tile([P, PACK - 1, V], F32, name="old", tag="old", align_bytes=64)
         new = sb.tile([P, PACK, V], F32, name="new", align_bytes=64)
 
         old2 = sb.tile([P, V], F32, name="old2", tag="old2", align_bytes=64)
@@ -137,7 +131,7 @@ def tile_picked_bellman_none_po_kernel(
 
         z_bf = sb.tile([P, S, PACK], BF16, name="z_bf", align_bytes=64)
         last = ORDER[PACK - 1]
-        relaxed2 = sb.tile([P, V], F32, name="relaxed2", tag="relaxed2", align_bytes=64)
+        relaxed2 = sb.tile([P, V], F32, name="relaxed2", align_bytes=64)
         relaxed = [ln_t[:, 0, :], ln_t[:, 3, :], relaxed2[:], new[:, 3, :]]
 
         def put_back(i):
@@ -159,23 +153,27 @@ def tile_picked_bellman_none_po_kernel(
         fetch_old(3)
         fetch_new(3)
         nc.vector.tensor_tensor(relaxed[2], olds[2], new[:, 2, :], MIN)
-        w2_byte_cols = w2_bytes[:].rearrange("p (m t) -> p t m", t=PACK)
-        w2_scale_head = sb.tile([P, PACK - 1, M], U8, name="w2_scale_head", tag="old2", align_bytes=64)
-        nc.gpsimd.tensor_copy(w2_scale_head[:], w2_byte_cols[:, : PACK - 1, :])
+        w2_scale_dealt = sb.tile([P, PACK, M], U8, name="w2_scale_dealt", tag="old2", align_bytes=64)
+        nc.gpsimd.tensor_copy(w2_scale_dealt[:], w2_bytes[:].rearrange("p (m t) -> p t m", t=PACK))
+        w2_scale = [w2_scale_dealt[:, t, :] for t in range(PACK)]
         put_back(1)
         nc.vector.tensor_tensor(new[:, 3, :], olds[3], new[:, 3, :], MIN)
+        w2_dealt = sb.tile([P, PACK, 2 * M], U8, name="w2_dealt", tag="old", align_bytes=64)
+        nc.gpsimd.tensor_copy(
+            w2_dealt[:].rearrange("p t (m e) -> p t m e", e=2),
+            w2_raw[:].rearrange("p (m t e) -> p t m e", t=PACK, e=2),
+        )
+        w2_codes = [w2_dealt[:, t, :] for t in range(PACK)]
         put_back(2)
 
-        w2_scale_tail = sb.tile([P, M], U8, name="w2_scale_tail", tag="relaxed2", align_bytes=64)
-        nc.gpsimd.tensor_copy(w2_scale_tail[:], w2_byte_cols[:, PACK - 1, :])
-        w2_scale = [w2_scale_head[:, t, :] for t in range(PACK - 1)] + [w2_scale_tail[:]]
-
         warm = ps.tile([M, S], F32, name="warm", tag="bank7")
-        for rep in range(WARM_PASSES):
+        stationary = [(w2_codes[0].bitcast(FP4X4), w2_scale[0], M)]
+        stationary = stationary + 2 * [(w1_codes[:, :NARROW].bitcast(FP8X4), w1_scale[:, :NARROW], NARROW)]
+        for codes, scale, rows in stationary:
             nc.tensor.matmul_mx(
-                out=warm[:],
-                lhsT=w2_codes[PACK - 1].bitcast(FP4X4),
-                lhsT_scale=w2_scale[PACK - 1],
+                out=warm[:rows, :],
+                lhsT=codes,
+                lhsT_scale=scale,
                 rhs=picked_codes[:].bitcast(FP8X4),
                 rhs_scale=picked_bytes[:],
                 start=True,

@@ -74,10 +74,10 @@ def tile_picked_bellman_none_po_kernel(
                 w1_bf[u][:].rearrange("p (t m j) -> p m j t", t=PAIR, j=PACK),
                 w1_cols[:, :, :, PAIR * u : PAIR * (u + 1)],
             )
-        ln_t = reuse.tile([P, PACK, V], F32, name="ln_t", offset=2 * N)
-        nc.sync.dma_start(ln_t[:], ln.rearrange("(p t) v -> p t v", t=PACK))
         w2_raw = reuse.tile([P, 2 * N], U8, name="w2_raw", offset=0)
         nc.sync.dma_start(w2_raw[:].bitcast(I32), w2_words[0].bitcast(I32))
+        ln_t = reuse.tile([P, PACK, V], F32, name="ln_t", offset=2 * N)
+        nc.sync.dma_start(ln_t[:], ln.rearrange("(p t) v -> p t v", t=PACK))
 
         for u in range(2):
             cols = slice(u * PAIR * M, (u + 1) * PAIR * M)
@@ -88,13 +88,6 @@ def tile_picked_bellman_none_po_kernel(
             nc.vector.tensor_copy(
                 picked_codes[:, h * HALF : (h + 1) * HALF],
                 x_codes[:].bitcast(U32).indirect(offs_t[:, h * HALF // GROUP : (h + 1) * HALF // GROUP]),
-            )
-
-        w2_bytes = sb.tile([P, N], U8, name="w2_bytes", tag="x_codes", align_bytes=64)
-        nc.gpsimd.memset(w2_bytes[:].bitcast(I32), 0)
-        for q in range(QUADS):
-            nc.sync.dma_start(
-                w2_bytes[32 * q : 32 * q + 4, :].bitcast(I32), w2_scales[0, 4 * q : 4 * q + 4, :].bitcast(I32)
             )
 
         y = [sb.tile([P, S], F32, name=f"y{t}", tag=f"y{t}", align_bytes=64) for t in range(PACK)]
@@ -116,6 +109,20 @@ def tile_picked_bellman_none_po_kernel(
                 )
             copy = nc.vector.tensor_copy if b == 2 else nc.scalar.copy
             copy(y[t][:, c0:c1], y_acc[:])
+
+        w2_dealt = sb.tile([P, 2 * N], U8, name="w2_dealt", tag="x_codes", align_bytes=64)
+        nc.vector.tensor_copy(
+            w2_dealt[:].bitcast(U16).rearrange("p (t m) -> p m t", t=PACK),
+            w2_raw[:].bitcast(U16).rearrange("p (m t) -> p m t", t=PACK),
+        )
+        w2_codes = [w2_dealt[:, 2 * M * t : 2 * M * (t + 1)] for t in range(PACK)]
+
+        w2_bytes = reuse.tile([P, N], U8, name="w2_bytes", offset=0)
+        nc.gpsimd.memset(w2_bytes[:].bitcast(I32), 0)
+        for q in range(QUADS):
+            nc.sync.dma_start(
+                w2_bytes[32 * q : 32 * q + 4, :].bitcast(I32), w2_scales[0, 4 * q : 4 * q + 4, :].bitcast(I32)
+            )
 
         old = sb.tile([P, PACK - 1, V], F32, name="old", tag="old", align_bytes=64)
         new = sb.tile([P, PACK, V], F32, name="new", align_bytes=64)
@@ -153,18 +160,15 @@ def tile_picked_bellman_none_po_kernel(
         fetch_old(3)
         fetch_new(3)
         nc.vector.tensor_tensor(relaxed[2], olds[2], new[:, 2, :], MIN)
-        w2_scale_dealt = sb.tile([P, PACK, M], U8, name="w2_scale_dealt", tag="old2", align_bytes=64)
-        nc.gpsimd.tensor_copy(w2_scale_dealt[:], w2_bytes[:].rearrange("p (m t) -> p t m", t=PACK))
-        w2_scale = [w2_scale_dealt[:, t, :] for t in range(PACK)]
+        w2_byte_cols = w2_bytes[:].rearrange("p (m t) -> p t m", t=PACK)
+        w2_scale_rest = sb.tile([P, PACK - 1, M], U8, name="w2_scale_rest", tag="old2", align_bytes=64)
+        nc.gpsimd.tensor_copy(w2_scale_rest[:], w2_byte_cols[:, 1:, :])
         put_back(1)
         nc.vector.tensor_tensor(new[:, 3, :], olds[3], new[:, 3, :], MIN)
-        w2_dealt = sb.tile([P, PACK, 2 * M], U8, name="w2_dealt", tag="old", align_bytes=64)
-        nc.gpsimd.tensor_copy(
-            w2_dealt[:].rearrange("p t (m e) -> p t m e", e=2),
-            w2_raw[:].rearrange("p (m t e) -> p t m e", t=PACK, e=2),
-        )
-        w2_codes = [w2_dealt[:, t, :] for t in range(PACK)]
         put_back(2)
+        w2_scale_first = sb.tile([P, M], U8, name="w2_scale_first", tag="old", align_bytes=64)
+        nc.vector.tensor_copy(w2_scale_first[:], w2_byte_cols[:, 0, :])
+        w2_scale = [w2_scale_first[:]] + [w2_scale_rest[:, t, :] for t in range(PACK - 1)]
 
         warm = ps.tile([M, S], F32, name="warm", tag="bank7")
         stationary = [(w2_codes[0].bitcast(FP4X4), w2_scale[0], M)]

@@ -208,8 +208,8 @@ def tile_picked_bellman_none_po_kernel(
         res_flat = res_bf[:].rearrange("p c t -> p (c t)")
         res = sb.tile([P, PACK, S], F32, name="res", align_bytes=64)
 
-        def interleave(c0, c1):
-            nc.vector.tensor_copy(
+        def interleave(copy, c0, c1):
+            copy(
                 res_bf[:, c0:c1, :].rearrange("p (c i) t -> p c t i", i=4),
                 res[:, :, c0:c1].rearrange("p t (c i) -> p c t i", i=4),
             )
@@ -225,35 +225,26 @@ def tile_picked_bellman_none_po_kernel(
                 stop=True,
             )
 
-        def store(u, q0, q1):
+        def store(u, c0, c1):
             planes = slice(PAIR * u, PAIR * (u + 1))
-            cols = slice(q0 * QUARTER, q1 * QUARTER)
-            nc.sync.dma_start(out_rows[:, planes, cols], res[:, planes, cols])
+            nc.sync.dma_start(out_rows[:, planes, c0:c1], res[:, planes, c0:c1])
 
-        for b, (q, u) in enumerate(((0, 0), (0, 1), (1, 1), (1, 0), (2, 0), (2, 1))):
+        for b, (u, q) in enumerate(((0, 0), (0, 1), (1, 0), (0, 2), (1, 1), (0, 3), (1, 2), (1, 3))):
             cols = slice(q * QUARTER, (q + 1) * QUARTER)
             out_acc = ps.tile([M, PAIR, QUARTER], F32, name=f"out_acc{b}", tag=f"bank{b}")
             for inner in range(PAIR):
                 multiply(out_acc[:, inner, :], PAIR * u + inner, cols)
-            copy = nc.vector.tensor_copy if b in (1, 3) else nc.scalar.copy
+            copy = nc.vector.tensor_copy if u == 0 and q > 0 else nc.scalar.copy
             copy(res[:, PAIR * u : PAIR * (u + 1), cols], out_acc[:])
-            if b % 2 == 0:
-                store(u, max(q - 1, 0), q + 1)
-            if b == 3:
-                interleave(0, QUARTER)
-                interleave(QUARTER, HALF)
-        cols = slice(S - QUARTER, S)
-        last_acc = ps.tile([M, PACK, QUARTER], F32, name="last_acc", tag="bank6")
-        for t in range(PACK):
-            multiply(last_acc[:, t, :], t, cols)
-        for u in (1, 0):
-            planes = slice(PAIR * u, PAIR * (u + 1))
-            nc.scalar.copy(res[:, planes, cols], last_acc[:, planes, :])
-            store(u, 3 - u, 4)
-        share = 96
-        nc.scalar.copy(res_bf[:, S - QUARTER : S - QUARTER + share, :], last_acc[:, :, :share].rearrange("p t c -> p c t"))
-        interleave(HALF, S - QUARTER)
-        interleave(S - QUARTER + share, S)
+            if u == 0 and q % 2:
+                store(0, (q - 1) * QUARTER, (q + 1) * QUARTER)
+        store(1, 0, S)
+        share = 32
+        for q in range(2):
+            interleave(nc.vector.tensor_copy, q * QUARTER, (q + 1) * QUARTER)
+        interleave(nc.scalar.copy, HALF, S - QUARTER)
+        interleave(nc.scalar.copy, S - QUARTER, S - QUARTER + share)
+        interleave(nc.vector.tensor_copy, S - QUARTER + share, S)
         quantize(out_codes, out_scale, res_flat, 0, HALF)
         quantize(out_codes, out_scale, res_flat, HALF, S - QUARTER)
         quantize(out_codes, out_scale, res_flat, S - QUARTER, S)

@@ -198,9 +198,11 @@ def tile_picked_bellman_none_po_kernel(
                 out=codes[:, c0:c1].bitcast(FP8X4), scales=scale[:, c0:c1], in_=values[:, c0 * PACK : c1 * PACK]
             )
 
-        for c0 in range(0, S, QUARTER):
-            copy = nc.vector.tensor_copy if c0 < HALF else nc.scalar.copy
-            copy(z_bf[:, c0 : c0 + QUARTER, last], z_last[:, c0 : c0 + QUARTER])
+        eighth = QUARTER // 2
+        for c0, c1 in ((0, QUARTER), (QUARTER, HALF), (S - eighth, S)):
+            nc.vector.tensor_copy(z_bf[:, c0:c1, last], z_last[:, c0:c1])
+        for c0, c1 in ((HALF, S - QUARTER), (S - QUARTER, S - eighth)):
+            nc.scalar.copy(z_bf[:, c0:c1, last], z_last[:, c0:c1])
         for c0 in range(0, S, QUARTER):
             quantize(z_codes, z_scale, z_flat, c0, c0 + QUARTER)
 
@@ -229,14 +231,15 @@ def tile_picked_bellman_none_po_kernel(
             planes = slice(PAIR * u, PAIR * (u + 1))
             nc.sync.dma_start(out_rows[:, planes, c0:c1], res[:, planes, c0:c1])
 
-        for b, (u, q) in enumerate(((0, 0), (0, 1), (1, 0), (0, 2), (1, 1), (0, 3), (1, 2), (1, 3))):
+        pieces = [(0, 1, 0), (1, 2, 0), (0, 1, 1), (1, 2, 1), (2, 4, 0), (0, 2, 2), (2, 4, 1), (0, 2, 3), (2, 4, 2), (2, 4, 3)]
+        for b, (t0, t1, q) in enumerate(pieces):
             cols = slice(q * QUARTER, (q + 1) * QUARTER)
-            out_acc = ps.tile([M, PAIR, QUARTER], F32, name=f"out_acc{b}", tag=f"bank{b}")
-            for inner in range(PAIR):
-                multiply(out_acc[:, inner, :], PAIR * u + inner, cols)
-            copy = nc.vector.tensor_copy if u == 0 and q > 0 else nc.scalar.copy
-            copy(res[:, PAIR * u : PAIR * (u + 1), cols], out_acc[:])
-            if u == 0 and q % 2:
+            out_acc = ps.tile([M, t1 - t0, QUARTER], F32, name=f"out_acc{b}", tag=f"bank{b % 8}")
+            for t in range(t0, t1):
+                multiply(out_acc[:, t - t0, :], t, cols)
+            copy = nc.vector.tensor_copy if t0 == 0 and q > 0 else nc.scalar.copy
+            copy(res[:, t0:t1, cols], out_acc[:])
+            if t1 == PAIR and q % 2:
                 store(0, (q - 1) * QUARTER, (q + 1) * QUARTER)
         store(1, 0, S)
         share = 32

@@ -44,8 +44,8 @@ def tile_picked_bellman_none_po_kernel(
         dst_t = lists.tile([P, V // GROUP], U16, name="dst_t")
 
         x_codes = sb.tile([P, T], I32, name="x_codes", tag="x_codes", align_bytes=64)
-        x_bytes = sb.tile([P, T], U8, name="x_bytes", align_bytes=64)
-        w1_raw = reuse.tile([P, PACK, H], F32, name="w1_raw", offset=0)
+        x_bytes = reuse.tile([P, T], U8, name="x_bytes", offset=0)
+        w1_raw = sb.tile([P, PACK, H], F32, name="w1_raw", align_bytes=64)
 
         nc.gpsimd.memset(x_bytes[:SPREAD, :].bitcast(I32), 0)
         picked_bytes = sb.tile([P, S], U8, name="picked_bytes", align_bytes=64)
@@ -60,7 +60,7 @@ def tile_picked_bellman_none_po_kernel(
         spread_bytes = sb.tile([P, S], U8, name="spread_bytes", align_bytes=64)
         nc.vector.tensor_copy(spread_bytes[:], x_bytes[:].indirect(offs_t[:]))
         for q in range(QUADS):
-            nc.scalar.dma_start(
+            nc.sync.dma_start(
                 picked_bytes[32 * q : 32 * q + 4, :].bitcast(I32),
                 spread_bytes[SPREAD + 4 * q : SPREAD + 4 * q + 4, :].bitcast(I32),
             )
@@ -69,14 +69,18 @@ def tile_picked_bellman_none_po_kernel(
         w1_scale = sb.tile([P, H], U8, name="w1_scale", align_bytes=64)
         w1_cols = w1_raw[:].rearrange("p j (m t) -> p m j t", t=PACK)
         w1_bf = [sb.tile([P, PAIR * M * PACK], BF16, name=f"w1_bf{u}", align_bytes=64) for u in range(2)]
-        for u in range(2):
-            nc.vector.tensor_copy(
-                w1_bf[u][:].rearrange("p (t m j) -> p m j t", t=PAIR, j=PACK),
-                w1_cols[:, :, :, PAIR * u : PAIR * (u + 1)],
+        for copy, u, m0, m1 in (
+            (nc.vector.tensor_copy, 0, 0, M),
+            (nc.scalar.copy, 1, M // 2, M),
+            (nc.vector.tensor_copy, 1, 0, M // 2),
+        ):
+            copy(
+                w1_bf[u][:].rearrange("p (t m j) -> p m j t", t=PAIR, j=PACK)[:, m0:m1],
+                w1_cols[:, m0:m1, :, PAIR * u : PAIR * (u + 1)],
             )
         w2_raw = reuse.tile([P, 2 * N], U8, name="w2_raw", offset=0)
         nc.sync.dma_start(w2_raw[:].bitcast(I32), w2_words[0].bitcast(I32))
-        ln_t = reuse.tile([P, PACK, V], F32, name="ln_t", offset=2 * N)
+        ln_t = reuse.tile([P, PACK, V], F32, name="ln_t", offset=3 * N)
         nc.sync.dma_start(ln_t[:], ln.rearrange("(p t) v -> p t v", t=PACK))
 
         for u in range(2):
@@ -92,7 +96,7 @@ def tile_picked_bellman_none_po_kernel(
 
         y = [sb.tile([P, S], F32, name=f"y{t}", tag=f"y{t}", align_bytes=64) for t in range(PACK)]
         first = ORDER[0]
-        pieces = [(first, 0, HALF), (ORDER[1], 0, HALF), (first, HALF, S - QUARTER), (first, S - QUARTER, S), (ORDER[1], HALF, S)]
+        pieces = [(first, 0, HALF), (first, HALF, S - QUARTER), (first, S - QUARTER, S), (ORDER[1], 0, HALF), (ORDER[1], HALF, S)]
         pieces = pieces + [(t, 0, S) for t in ORDER[2:]]
         for b, (t, c0, c1) in enumerate(pieces):
             y_acc = ps.tile([M, c1 - c0], F32, name=f"y_acc{b}", tag=f"bank{b}")
@@ -107,7 +111,7 @@ def tile_picked_bellman_none_po_kernel(
                     start=True,
                     stop=True,
                 )
-            copy = nc.vector.tensor_copy if b == 2 else nc.scalar.copy
+            copy = nc.vector.tensor_copy if b == 1 else nc.scalar.copy
             copy(y[t][:, c0:c1], y_acc[:])
 
         w2_dealt = sb.tile([P, 2 * N], U8, name="w2_dealt", tag="x_codes", align_bytes=64)
@@ -117,7 +121,7 @@ def tile_picked_bellman_none_po_kernel(
         )
         w2_codes = [w2_dealt[:, 2 * M * t : 2 * M * (t + 1)] for t in range(PACK)]
 
-        w2_bytes = reuse.tile([P, N], U8, name="w2_bytes", offset=0)
+        w2_bytes = reuse.tile([P, N], U8, name="w2_bytes", offset=2 * N)
         nc.gpsimd.memset(w2_bytes[:].bitcast(I32), 0)
         for q in range(QUADS):
             nc.sync.dma_start(
@@ -128,7 +132,8 @@ def tile_picked_bellman_none_po_kernel(
         new = sb.tile([P, PACK, V], F32, name="new", align_bytes=64)
 
         old2 = sb.tile([P, V], F32, name="old2", tag="old2", align_bytes=64)
-        olds = [old[:, 0, :], old[:, 1, :], old2[:], old[:, 2, :]]
+        old0 = sb.tile([P, V], F32, name="old0", tag="old0", align_bytes=64)
+        olds = [old0[:], old[:, 1, :], old2[:], old[:, 2, :]]
 
         def fetch_old(i):
             nc.vector.tensor_copy(olds[i], y[ORDER[i]][:].indirect(dst_t[:]))
@@ -139,7 +144,7 @@ def tile_picked_bellman_none_po_kernel(
         z_bf = sb.tile([P, S, PACK], BF16, name="z_bf", align_bytes=64)
         last = ORDER[PACK - 1]
         relaxed2 = sb.tile([P, V], F32, name="relaxed2", align_bytes=64)
-        relaxed = [ln_t[:, 0, :], ln_t[:, 3, :], relaxed2[:], new[:, 3, :]]
+        relaxed = [old0[:], ln_t[:, 3, :], relaxed2[:], new[:, 3, :]]
 
         def put_back(i):
             t = ORDER[i]
@@ -151,11 +156,12 @@ def tile_picked_bellman_none_po_kernel(
         for i in range(2):
             fetch_old(i)
             fetch_new(i)
+        nc.vector.tensor_tensor(relaxed[0], olds[0], new[:, 0, :], MIN)
         fetch_new(2)
-        nc.vector.tensor_tensor(ln_t[:, 0::3, :], old[:, 0:2, :], new[:, 0:2, :], MIN)
+        nc.vector.tensor_tensor(relaxed[1], olds[1], new[:, 1, :], MIN)
         fetch_old(2)
         put_back(0)
-        z_last = sb.tile([P, S], F32, name="z_last", tag=f"y{first}", align_bytes=64)
+        z_last = sb.tile([P, S], F32, name="z_last", tag="old0", align_bytes=64)
         nc.scalar.copy(z_last[:], y[last][:])
         fetch_old(3)
         fetch_new(3)

@@ -15,6 +15,7 @@ FP8X4 = mybir.dt.float8_e4m3fn_x4
 FP4X4 = mybir.dt.float4_e2m1fn_x4
 ADD = mybir.AluOpType.add
 MIN = mybir.AluOpType.min
+COPY = mybir.ActivationFunctionType.Copy
 
 P = 128
 PACK = 4
@@ -25,8 +26,8 @@ HALF = S // 2
 SPREAD = P - 16
 QUARTER = S // 4
 PAIR = 2
-ORDER = (0, 2, 3, 1)
-NARROW = 64
+ORDER = (1, 3, 0, 2)
+NARROW = 32
 
 
 def tile_picked_bellman_none_po_kernel(
@@ -55,10 +56,11 @@ def tile_picked_bellman_none_po_kernel(
         nc.sync.dma_start(w1_raw[:], w1.rearrange("(p j) c -> p j c", j=PACK))
         nc.sync.dma_start(dst_t[:], dst)
         nc.sync.dma_start(x_codes[:], x_words[0].rearrange("p n t -> p (n t)").bitcast(I32))
-        nc.sync.dma_start(src_t[:], src)
 
         spread_bytes = sb.tile([P, S], U8, name="spread_bytes", align_bytes=64)
         nc.vector.tensor_copy(spread_bytes[:], x_bytes[:].indirect(offs_t[:]))
+        w2_raw = reuse.tile([P, 2 * N], U8, name="w2_raw", offset=0)
+        nc.sync.dma_start(w2_raw[:].bitcast(I32), w2_words[0].bitcast(I32))
         for q in range(QUADS):
             nc.sync.dma_start(
                 picked_bytes[32 * q : 32 * q + 4, :].bitcast(I32),
@@ -78,8 +80,7 @@ def tile_picked_bellman_none_po_kernel(
                 w1_bf[u][:].rearrange("p (t m j) -> p m j t", t=PAIR, j=PACK)[:, m0:m1],
                 w1_cols[:, m0:m1, :, PAIR * u : PAIR * (u + 1)],
             )
-        w2_raw = reuse.tile([P, 2 * N], U8, name="w2_raw", offset=0)
-        nc.sync.dma_start(w2_raw[:].bitcast(I32), w2_words[0].bitcast(I32))
+        nc.sync.dma_start(src_t[:], src)
         ln_t = reuse.tile([P, PACK, V], F32, name="ln_t", offset=3 * N)
         nc.sync.dma_start(ln_t[:], ln.rearrange("(p t) v -> p t v", t=PACK))
 
@@ -94,25 +95,34 @@ def tile_picked_bellman_none_po_kernel(
                 x_codes[:].bitcast(U32).indirect(offs_t[:, h * HALF // GROUP : (h + 1) * HALF // GROUP]),
             )
 
-        y = [sb.tile([P, S], F32, name=f"y{t}", tag=f"y{t}", align_bytes=64) for t in range(PACK)]
-        first = ORDER[0]
-        pieces = [(first, 0, HALF), (first, HALF, S - QUARTER), (first, S - QUARTER, S), (ORDER[1], 0, HALF), (ORDER[1], HALF, S)]
-        pieces = pieces + [(t, 0, S) for t in ORDER[2:]]
-        for b, (t, c0, c1) in enumerate(pieces):
-            y_acc = ps.tile([M, c1 - c0], F32, name=f"y_acc{b}", tag=f"bank{b}")
+        y = [sb.tile([P, (PAIR - t % PAIR) * S], F32, name=f"y{t}", align_bytes=64) for t in range(PACK)]
+        a, b, c, d = ORDER
+        pieces = [
+            (a, 0, HALF, 0, nc.scalar.copy),
+            (a, HALF, S - QUARTER, 1, nc.vector.tensor_copy),
+            (a, S - QUARTER, S, 2, nc.scalar.copy),
+            (b, 0, S, 0, nc.scalar.copy),
+            (c, 0, S, 2, nc.scalar.copy),
+            (d, 0, S, 0, nc.scalar.copy),
+        ]
+
+        def first_product(t, c0, c1, bank, copy):
+            y_acc = ps.tile([M, c1 - c0], F32, name=f"y_acc{t}_{c0}", tag=f"bank{bank}")
             cols = slice(t * M, (t + 1) * M)
-            for c in range(c0, c1, QUARTER):
+            for n0 in range(c0, c1, QUARTER):
                 nc.tensor.matmul_mx(
-                    out=y_acc[:, c - c0 : c - c0 + QUARTER],
+                    out=y_acc[:, n0 - c0 : n0 - c0 + QUARTER],
                     lhsT=w1_codes[:, cols].bitcast(FP8X4),
                     lhsT_scale=w1_scale[:, cols],
-                    rhs=picked_codes[:, c : c + QUARTER].bitcast(FP8X4),
-                    rhs_scale=picked_bytes[:, c : c + QUARTER],
+                    rhs=picked_codes[:, n0 : n0 + QUARTER].bitcast(FP8X4),
+                    rhs_scale=picked_bytes[:, n0 : n0 + QUARTER],
                     start=True,
                     stop=True,
                 )
-            copy = nc.vector.tensor_copy if b == 1 else nc.scalar.copy
             copy(y[t][:, c0:c1], y_acc[:])
+
+        for piece in pieces[:3]:
+            first_product(*piece)
 
         w2_dealt = sb.tile([P, 2 * N], U8, name="w2_dealt", tag="x_codes", align_bytes=64)
         nc.vector.tensor_copy(
@@ -128,68 +138,90 @@ def tile_picked_bellman_none_po_kernel(
                 w2_bytes[32 * q : 32 * q + 4, :].bitcast(I32), w2_scales[0, 4 * q : 4 * q + 4, :].bitcast(I32)
             )
 
-        old = sb.tile([P, PACK - 1, V], F32, name="old", tag="old", align_bytes=64)
-        new = sb.tile([P, PACK, V], F32, name="new", align_bytes=64)
+        def values(name, tag=None, width=V):
+            return sb.tile([P, width], F32, name=name, tag=tag or name, align_bytes=64)
 
-        old2 = sb.tile([P, V], F32, name="old2", tag="old2", align_bytes=64)
-        old0 = sb.tile([P, V], F32, name="old0", tag="old0", align_bytes=64)
-        olds = [old0[:], old[:, 1, :], old2[:], old[:, 2, :]]
-
-        def fetch_old(i):
-            nc.vector.tensor_copy(olds[i], y[ORDER[i]][:].indirect(dst_t[:]))
-
-        def fetch_new(i):
-            nc.vector.tensor_tensor(new[:, i, :], y[ORDER[i]][:].indirect(src_t[:]), ln_t[:, ORDER[i], :], ADD)
-
+        old = {t: values(f"old{t}") for t in (b, c, d)}
+        old_halves = [values(f"old_half{h}", width=V // 2) for h in range(2)]
+        far = {t: values(f"far{t}") for t in (c, d)}
+        new = {a: values(f"new{a}")}
+        relaxed = [values(f"relaxed{t}") for t in range(PACK)]
         z_bf = sb.tile([P, S, PACK], BF16, name="z_bf", align_bytes=64)
-        last = ORDER[PACK - 1]
-        relaxed2 = sb.tile([P, V], F32, name="relaxed2", align_bytes=64)
-        relaxed = [old0[:], ln_t[:, 3, :], relaxed2[:], new[:, 3, :]]
+        whole, halves = slice(0, V), (slice(0, V // 2), slice(V // 2, V))
 
-        def put_back(i):
-            t = ORDER[i]
-            nc.vector.tensor_copy(y[t][:].indirect(dst_t[:]), relaxed[i])
-            for h in range(2):
-                cols = slice(h * HALF, (h + 1) * HALF)
-                nc.scalar.copy(z_bf[:, cols, t], y[t][:, cols])
+        def window(t, offsets, v):
+            return y[t][:].indirect(offsets[:, v.start // GROUP : v.stop // GROUP])
 
-        for i in range(2):
-            fetch_old(i)
-            fetch_new(i)
-        nc.vector.tensor_tensor(relaxed[0], olds[0], new[:, 0, :], MIN)
-        fetch_new(2)
-        nc.vector.tensor_tensor(relaxed[1], olds[1], new[:, 1, :], MIN)
-        fetch_old(2)
-        put_back(0)
-        z_last = sb.tile([P, S], F32, name="z_last", tag="old0", align_bytes=64)
-        nc.scalar.copy(z_last[:], y[last][:])
-        fetch_old(3)
-        fetch_new(3)
-        nc.vector.tensor_tensor(relaxed[2], olds[2], new[:, 2, :], MIN)
+        def fetch_old(t):
+            nc.scalar.activation(old[t][:], window(t, dst_t, whole), COPY)
+
+        def fetch_far(t):
+            nc.scalar.activation(far[t][:], window(t, src_t, whole), COPY)
+
+        def fetch_new(t, v=whole):
+            nc.vector.tensor_tensor(new[t][:, v], window(t, src_t, v), ln_t[:, t, v], ADD)
+
+        def add_length(t):
+            nc.vector.tensor_tensor(new[t][:], far[t][:], ln_t[:, t, :], ADD)
+
+        def relax(t):
+            nc.vector.tensor_tensor(relaxed[t][:], old[t][:], new[t][:], MIN)
+
+        def put_back(t, v=whole):
+            nc.vector.tensor_copy(window(t, dst_t, v), relaxed[t][:, v])
+
+        def round_pair(copy, t, c0, c1):
+            copy(z_bf[:, c0:c1, t : t + PAIR], y[t][:].rearrange("p (e c) -> p c e", e=PAIR)[:, c0:c1, :])
+
+        for v in halves:
+            fetch_new(a, v)
+        for v, old_half in zip(halves, old_halves):
+            nc.scalar.activation(old_half[:], window(a, dst_t, v), COPY)
+            nc.vector.tensor_tensor(relaxed[a][:, v], old_half[:], new[a][:, v], MIN)
+        put_back(a, halves[0])
+        first_product(*pieces[3])
+        new[b] = values(f"new{b}", "old_half0")
+        fetch_new(b)
+        put_back(a, halves[1])
+        first_product(*pieces[4])
+        fetch_old(b)
+        relax(b)
+        fetch_far(c)
+        new[c] = values(f"new{c}", f"relaxed{a}")
+        add_length(c)
+        put_back(b)
+        first_product(*pieces[5])
+        fetch_old(c)
+        relax(c)
+        fetch_far(d)
+        new[d] = values(f"new{d}", f"old{b}")
+        add_length(d)
         w2_byte_cols = w2_bytes[:].rearrange("p (m t) -> p t m", t=PACK)
-        w2_scale_rest = sb.tile([P, PACK - 1, M], U8, name="w2_scale_rest", tag="old2", align_bytes=64)
+        w2_scale_rest = sb.tile([P, PACK - 1, M], U8, name="w2_scale_rest", tag=f"far{d}", align_bytes=64)
         nc.gpsimd.tensor_copy(w2_scale_rest[:], w2_byte_cols[:, 1:, :])
-        put_back(1)
-        nc.vector.tensor_tensor(new[:, 3, :], olds[3], new[:, 3, :], MIN)
-        put_back(2)
-        w2_scale_first = sb.tile([P, M], U8, name="w2_scale_first", tag="old", align_bytes=64)
+        nc.scalar.copy(y[c][:, S:], y[a][:])
+        put_back(c)
+        fetch_old(d)
+        relax(d)
+        nc.scalar.copy(y[d][:, S:], y[b][:])
+        for h in range(2):
+            round_pair(nc.scalar.copy, c, h * HALF, (h + 1) * HALF)
+        w2_scale_first = sb.tile([P, M], U8, name="w2_scale_first", tag=f"relaxed{c}", align_bytes=64)
         nc.vector.tensor_copy(w2_scale_first[:], w2_byte_cols[:, 0, :])
         w2_scale = [w2_scale_first[:]] + [w2_scale_rest[:, t, :] for t in range(PACK - 1)]
 
         warm = ps.tile([M, S], F32, name="warm", tag="bank7")
-        stationary = [(w2_codes[0].bitcast(FP4X4), w2_scale[0], M)]
-        stationary = stationary + 2 * [(w1_codes[:, :NARROW].bitcast(FP8X4), w1_scale[:, :NARROW], NARROW)]
-        for codes, scale, rows in stationary:
+        for i in range(3):
             nc.tensor.matmul_mx(
-                out=warm[:rows, :],
-                lhsT=codes,
-                lhsT_scale=scale,
-                rhs=picked_codes[:].bitcast(FP8X4),
-                rhs_scale=picked_bytes[:],
+                out=warm[:NARROW, :],
+                lhsT=w1_codes[:, :NARROW].bitcast(FP8X4),
+                lhsT_scale=w2_scale_first[:, :NARROW],
+                rhs=w1_codes[:].bitcast(FP8X4),
+                rhs_scale=w1_scale[:],
                 start=True,
                 stop=True,
             )
-        nc.vector.tensor_copy(z_last[:].indirect(dst_t[:]), relaxed[PACK - 1])
+        put_back(d)
 
         z_codes = sb.tile([P, S], U32, name="z_codes", align_bytes=64)
         z_scale = sb.tile([P, S], U8, name="z_scale", align_bytes=64)
@@ -206,9 +238,9 @@ def tile_picked_bellman_none_po_kernel(
 
         eighth = QUARTER // 2
         for c0, c1 in ((0, QUARTER), (QUARTER, HALF), (S - eighth, S)):
-            nc.vector.tensor_copy(z_bf[:, c0:c1, last], z_last[:, c0:c1])
+            round_pair(nc.vector.tensor_copy, d, c0, c1)
         for c0, c1 in ((HALF, S - QUARTER), (S - QUARTER, S - eighth)):
-            nc.scalar.copy(z_bf[:, c0:c1, last], z_last[:, c0:c1])
+            round_pair(nc.scalar.copy, d, c0, c1)
         for c0 in range(0, S, QUARTER):
             quantize(z_codes, z_scale, z_flat, c0, c0 + QUARTER)
 
@@ -238,9 +270,9 @@ def tile_picked_bellman_none_po_kernel(
             nc.sync.dma_start(out_rows[:, planes, c0:c1], res[:, planes, c0:c1])
 
         pieces = [(0, 1, 0), (1, 2, 0), (0, 1, 1), (1, 2, 1), (2, 4, 0), (0, 2, 2), (2, 4, 1), (0, 2, 3), (2, 4, 2), (2, 4, 3)]
-        for b, (t0, t1, q) in enumerate(pieces):
+        for bank, (t0, t1, q) in enumerate(pieces):
             cols = slice(q * QUARTER, (q + 1) * QUARTER)
-            out_acc = ps.tile([M, t1 - t0, QUARTER], F32, name=f"out_acc{b}", tag=f"bank{b % 8}")
+            out_acc = ps.tile([M, t1 - t0, QUARTER], F32, name=f"out_acc{bank}", tag=f"bank{bank % 8}")
             for t in range(t0, t1):
                 multiply(out_acc[:, t - t0, :], t, cols)
             copy = nc.vector.tensor_copy if t0 == 0 and q > 0 else nc.scalar.copy

@@ -45,24 +45,25 @@ def tile_picked_bellman_none_po_kernel(
         dst_t = lists.tile([P, V // GROUP], U16, name="dst_t")
 
         x_codes = sb.tile([P, T], I32, name="x_codes", tag="x_codes", align_bytes=64)
-        x_bytes = reuse.tile([P, T], U8, name="x_bytes", offset=0)
-        w1_raw = sb.tile([P, PACK, H], F32, name="w1_raw", align_bytes=64)
+        x_bytes = sb.tile([P, T], U8, name="x_bytes", align_bytes=64)
+        w1_raw = reuse.tile([P, PACK, H], F32, name="w1_raw", offset=0)
 
         nc.gpsimd.memset(x_bytes[:SPREAD, :].bitcast(I32), 0)
         picked_bytes = sb.tile([P, S], U8, name="picked_bytes", align_bytes=64)
         nc.gpsimd.memset(picked_bytes[:].bitcast(I32), 0)
+        w2_bytes = sb.tile([P, N], U8, name="w2_bytes", align_bytes=64)
+        nc.gpsimd.memset(w2_bytes[:].bitcast(I32), 0)
         nc.sync.dma_start(offs_t[:], offs)
         nc.scalar.dma_start(x_bytes[SPREAD:, :].bitcast(I32), x_scales[0].bitcast(I32))
         nc.sync.dma_start(w1_raw[:], w1.rearrange("(p j) c -> p j c", j=PACK))
         nc.sync.dma_start(dst_t[:], dst)
+        nc.sync.dma_start(src_t[:], src)
         nc.sync.dma_start(x_codes[:], x_words[0].rearrange("p n t -> p (n t)").bitcast(I32))
 
         spread_bytes = sb.tile([P, S], U8, name="spread_bytes", align_bytes=64)
         nc.vector.tensor_copy(spread_bytes[:], x_bytes[:].indirect(offs_t[:]))
-        w2_raw = reuse.tile([P, 2 * N], U8, name="w2_raw", offset=0)
-        nc.sync.dma_start(w2_raw[:].bitcast(I32), w2_words[0].bitcast(I32))
         for q in range(QUADS):
-            nc.sync.dma_start(
+            nc.scalar.dma_start(
                 picked_bytes[32 * q : 32 * q + 4, :].bitcast(I32),
                 spread_bytes[SPREAD + 4 * q : SPREAD + 4 * q + 4, :].bitcast(I32),
             )
@@ -71,58 +72,56 @@ def tile_picked_bellman_none_po_kernel(
         w1_scale = sb.tile([P, H], U8, name="w1_scale", align_bytes=64)
         w1_cols = w1_raw[:].rearrange("p j (m t) -> p m j t", t=PACK)
         w1_bf = [sb.tile([P, PAIR * M * PACK], BF16, name=f"w1_bf{u}", align_bytes=64) for u in range(2)]
-        for copy, u, m0, m1 in (
-            (nc.vector.tensor_copy, 0, 0, M),
-            (nc.scalar.copy, 1, M // 2, M),
-            (nc.vector.tensor_copy, 1, 0, M // 2),
-        ):
-            copy(
-                w1_bf[u][:].rearrange("p (t m j) -> p m j t", t=PAIR, j=PACK)[:, m0:m1],
-                w1_cols[:, m0:m1, :, PAIR * u : PAIR * (u + 1)],
+        for u in range(2):
+            nc.vector.tensor_copy(
+                w1_bf[u][:].rearrange("p (t m j) -> p m j t", t=PAIR, j=PACK),
+                w1_cols[:, :, :, PAIR * u : PAIR * (u + 1)],
             )
-        nc.sync.dma_start(src_t[:], src)
-        ln_t = reuse.tile([P, PACK, V], F32, name="ln_t", offset=3 * N)
+        ln_t = reuse.tile([P, PACK, V], F32, name="ln_t", offset=0)
         nc.sync.dma_start(ln_t[:], ln.rearrange("(p t) v -> p t v", t=PACK))
+        w2_raw = reuse.tile([P, 2 * N], U8, name="w2_raw", offset=PACK * V * 4)
+        nc.sync.dma_start(w2_raw[:].bitcast(I32), w2_words[0].bitcast(I32))
 
         for u in range(2):
             cols = slice(u * PAIR * M, (u + 1) * PAIR * M)
             nc.vector.quantize_mx(out=w1_codes[:, cols].bitcast(FP8X4), scales=w1_scale[:, cols], in_=w1_bf[u][:])
 
         picked_codes = sb.tile([P, S], U32, name="picked_codes", align_bytes=64)
-        for h in range(2):
+        for c0 in range(0, S, QUARTER):
             nc.vector.tensor_copy(
-                picked_codes[:, h * HALF : (h + 1) * HALF],
-                x_codes[:].bitcast(U32).indirect(offs_t[:, h * HALF // GROUP : (h + 1) * HALF // GROUP]),
+                picked_codes[:, c0 : c0 + QUARTER],
+                x_codes[:].bitcast(U32).indirect(offs_t[:, c0 // GROUP : (c0 + QUARTER) // GROUP]),
             )
 
-        y = [sb.tile([P, (PAIR - t % PAIR) * S], F32, name=f"y{t}", align_bytes=64) for t in range(PACK)]
         a, b, c, d = ORDER
-        pieces = [
-            (a, 0, HALF, 0, nc.scalar.copy),
-            (a, HALF, S - QUARTER, 1, nc.vector.tensor_copy),
-            (a, S - QUARTER, S, 2, nc.scalar.copy),
-            (b, 0, S, 0, nc.scalar.copy),
-            (c, 0, S, 2, nc.scalar.copy),
-            (d, 0, S, 0, nc.scalar.copy),
-        ]
+        y = [sb.tile([P, PAIR * S if t == c else S], F32, name=f"y{t}", tag=f"y{t}", align_bytes=64) for t in range(PACK)]
 
-        def first_product(t, c0, c1, bank, copy):
-            y_acc = ps.tile([M, c1 - c0], F32, name=f"y_acc{t}_{c0}", tag=f"bank{bank}")
+        def first_product(t, c0, c1, acc):
             cols = slice(t * M, (t + 1) * M)
+            nc.tensor.matmul_mx(
+                out=acc,
+                lhsT=w1_codes[:, cols].bitcast(FP8X4),
+                lhsT_scale=w1_scale[:, cols],
+                rhs=picked_codes[:, c0:c1].bitcast(FP8X4),
+                rhs_scale=picked_bytes[:, c0:c1],
+                start=True,
+                stop=True,
+            )
+
+        def make_y(t, c0, c1, bank, copy):
+            y_acc = ps.tile([M, c1 - c0], F32, name=f"y_acc{bank}", tag=f"bank{bank}")
             for n0 in range(c0, c1, QUARTER):
-                nc.tensor.matmul_mx(
-                    out=y_acc[:, n0 - c0 : n0 - c0 + QUARTER],
-                    lhsT=w1_codes[:, cols].bitcast(FP8X4),
-                    lhsT_scale=w1_scale[:, cols],
-                    rhs=picked_codes[:, n0 : n0 + QUARTER].bitcast(FP8X4),
-                    rhs_scale=picked_bytes[:, n0 : n0 + QUARTER],
-                    start=True,
-                    stop=True,
-                )
+                first_product(t, n0, n0 + QUARTER, y_acc[:, n0 - c0 : n0 - c0 + QUARTER])
             copy(y[t][:, c0:c1], y_acc[:])
 
-        for piece in pieces[:3]:
-            first_product(*piece)
+        lead = ps.tile([M, HALF], F32, name="lead", tag="bank0")
+        first_product(a, 0, QUARTER, lead[:, :QUARTER])
+        make_y(b, 0, QUARTER, 1, nc.vector.tensor_copy)
+        first_product(a, QUARTER, HALF, lead[:, QUARTER:])
+        nc.scalar.copy(y[a][:, :HALF], lead[:])
+        make_y(a, HALF, S - QUARTER, 2, nc.vector.tensor_copy)
+        make_y(a, S - QUARTER, S, 3, nc.scalar.copy)
+        make_y(b, QUARTER, S, 4, nc.scalar.copy)
 
         w2_dealt = sb.tile([P, 2 * N], U8, name="w2_dealt", tag="x_codes", align_bytes=64)
         nc.vector.tensor_copy(
@@ -131,35 +130,28 @@ def tile_picked_bellman_none_po_kernel(
         )
         w2_codes = [w2_dealt[:, 2 * M * t : 2 * M * (t + 1)] for t in range(PACK)]
 
-        w2_bytes = reuse.tile([P, N], U8, name="w2_bytes", offset=2 * N)
-        nc.gpsimd.memset(w2_bytes[:].bitcast(I32), 0)
         for q in range(QUADS):
             nc.sync.dma_start(
                 w2_bytes[32 * q : 32 * q + 4, :].bitcast(I32), w2_scales[0, 4 * q : 4 * q + 4, :].bitcast(I32)
             )
 
-        def values(name, tag=None, width=V):
-            return sb.tile([P, width], F32, name=name, tag=tag or name, align_bytes=64)
+        def values(name):
+            return sb.tile([P, V], F32, name=name, tag=name, align_bytes=64)
 
-        old = {t: values(f"old{t}") for t in (b, c, d)}
-        old_halves = [values(f"old_half{h}", width=V // 2) for h in range(2)]
+        old = [values(f"old{t}") for t in range(PACK)]
         far = {t: values(f"far{t}") for t in (c, d)}
-        new = {a: values(f"new{a}")}
+        new = [values(f"new{t}") for t in range(PACK)]
         relaxed = [values(f"relaxed{t}") for t in range(PACK)]
         z_bf = sb.tile([P, S, PACK], BF16, name="z_bf", align_bytes=64)
-        whole, halves = slice(0, V), (slice(0, V // 2), slice(V // 2, V))
-
-        def window(t, offsets, v):
-            return y[t][:].indirect(offsets[:, v.start // GROUP : v.stop // GROUP])
 
         def fetch_old(t):
-            nc.scalar.activation(old[t][:], window(t, dst_t, whole), COPY)
+            nc.scalar.activation(old[t][:], y[t][:].indirect(dst_t[:]), COPY)
 
         def fetch_far(t):
-            nc.scalar.activation(far[t][:], window(t, src_t, whole), COPY)
+            nc.scalar.activation(far[t][:], y[t][:].indirect(src_t[:]), COPY)
 
-        def fetch_new(t, v=whole):
-            nc.vector.tensor_tensor(new[t][:, v], window(t, src_t, v), ln_t[:, t, v], ADD)
+        def fetch_new(t):
+            nc.vector.tensor_tensor(new[t][:], y[t][:].indirect(src_t[:]), ln_t[:, t, :], ADD)
 
         def add_length(t):
             nc.vector.tensor_tensor(new[t][:], far[t][:], ln_t[:, t, :], ADD)
@@ -167,34 +159,30 @@ def tile_picked_bellman_none_po_kernel(
         def relax(t):
             nc.vector.tensor_tensor(relaxed[t][:], old[t][:], new[t][:], MIN)
 
-        def put_back(t, v=whole):
-            nc.vector.tensor_copy(window(t, dst_t, v), relaxed[t][:, v])
+        def put_back(t):
+            nc.vector.tensor_copy(y[t][:].indirect(dst_t[:]), relaxed[t][:])
 
         def round_pair(copy, t, c0, c1):
             copy(z_bf[:, c0:c1, t : t + PAIR], y[t][:].rearrange("p (e c) -> p c e", e=PAIR)[:, c0:c1, :])
 
-        for v in halves:
-            fetch_new(a, v)
-        for v, old_half in zip(halves, old_halves):
-            nc.scalar.activation(old_half[:], window(a, dst_t, v), COPY)
-            nc.vector.tensor_tensor(relaxed[a][:, v], old_half[:], new[a][:, v], MIN)
-        put_back(a, halves[0])
-        first_product(*pieces[3])
-        new[b] = values(f"new{b}", "old_half0")
+        def round_plane(copy, t, c0, c1):
+            copy(z_bf[:, c0:c1, t], y[t][:, c0:c1])
+
+        fetch_new(a)
         fetch_new(b)
-        put_back(a, halves[1])
-        first_product(*pieces[4])
+        fetch_old(a)
+        relax(a)
+        put_back(a)
+        make_y(c, 0, S, 5, nc.scalar.copy)
         fetch_old(b)
         relax(b)
         fetch_far(c)
-        new[c] = values(f"new{c}", f"relaxed{a}")
         add_length(c)
         put_back(b)
-        first_product(*pieces[5])
+        make_y(d, 0, S, 6, nc.scalar.copy)
         fetch_old(c)
         relax(c)
         fetch_far(d)
-        new[d] = values(f"new{d}", f"old{b}")
         add_length(d)
         w2_byte_cols = w2_bytes[:].rearrange("p (m t) -> p t m", t=PACK)
         w2_scale_rest = sb.tile([P, PACK - 1, M], U8, name="w2_scale_rest", tag=f"far{d}", align_bytes=64)
@@ -202,10 +190,15 @@ def tile_picked_bellman_none_po_kernel(
         nc.scalar.copy(y[c][:, S:], y[a][:])
         put_back(c)
         fetch_old(d)
-        relax(d)
-        nc.scalar.copy(y[d][:, S:], y[b][:])
         for h in range(2):
-            round_pair(nc.scalar.copy, c, h * HALF, (h + 1) * HALF)
+            round_plane(nc.scalar.copy, b, h * HALF, (h + 1) * HALF)
+        relax(d)
+        z_last = sb.tile([P, S], F32, name="z_last", align_bytes=64)
+        nc.scalar.copy(z_last[:], y[d][:])
+        y[d] = z_last
+        for c0, c1 in ((0, HALF), (HALF, S - QUARTER // 2)):
+            round_pair(nc.scalar.copy, c, c0, c1)
+        round_pair(nc.vector.tensor_copy, c, S - QUARTER // 2, S)
         w2_scale_first = sb.tile([P, M], U8, name="w2_scale_first", tag=f"relaxed{c}", align_bytes=64)
         nc.vector.tensor_copy(w2_scale_first[:], w2_byte_cols[:, 0, :])
         w2_scale = [w2_scale_first[:]] + [w2_scale_rest[:, t, :] for t in range(PACK - 1)]
@@ -238,9 +231,9 @@ def tile_picked_bellman_none_po_kernel(
 
         eighth = QUARTER // 2
         for c0, c1 in ((0, QUARTER), (QUARTER, HALF), (S - eighth, S)):
-            round_pair(nc.vector.tensor_copy, d, c0, c1)
+            round_plane(nc.vector.tensor_copy, d, c0, c1)
         for c0, c1 in ((HALF, S - QUARTER), (S - QUARTER, S - eighth)):
-            round_pair(nc.scalar.copy, d, c0, c1)
+            round_plane(nc.scalar.copy, d, c0, c1)
         for c0 in range(0, S, QUARTER):
             quantize(z_codes, z_scale, z_flat, c0, c0 + QUARTER)
 

@@ -45,8 +45,8 @@ def tile_picked_bellman_none_po_kernel(
         dst_t = lists.tile([P, V // GROUP], U16, name="dst_t")
 
         x_codes = sb.tile([P, T], I32, name="x_codes", tag="x_codes", align_bytes=64)
-        x_bytes = sb.tile([P, T], U8, name="x_bytes", align_bytes=64)
-        w1_raw = reuse.tile([P, PACK, H], F32, name="w1_raw", offset=0)
+        x_bytes = reuse.tile([P, T], U8, name="x_bytes", offset=0)
+        w1_raw = sb.tile([P, PACK, H], F32, name="w1_raw", align_bytes=64)
 
         nc.gpsimd.memset(x_bytes[:SPREAD, :].bitcast(I32), 0)
         picked_bytes = sb.tile([P, S], U8, name="picked_bytes", align_bytes=64)
@@ -77,9 +77,9 @@ def tile_picked_bellman_none_po_kernel(
                 w1_bf[u][:].rearrange("p (t m j) -> p m j t", t=PAIR, j=PACK),
                 w1_cols[:, :, :, PAIR * u : PAIR * (u + 1)],
             )
-        ln_t = reuse.tile([P, PACK, V], F32, name="ln_t", offset=0)
+        ln_t = reuse.tile([P, PACK, V], F32, name="ln_t", offset=2 * N)
         nc.sync.dma_start(ln_t[:], ln.rearrange("(p t) v -> p t v", t=PACK))
-        w2_raw = reuse.tile([P, 2 * N], U8, name="w2_raw", offset=PACK * V * 4)
+        w2_raw = reuse.tile([P, 2 * N], U8, name="w2_raw", offset=0)
         nc.sync.dma_start(w2_raw[:].bitcast(I32), w2_words[0].bitcast(I32))
 
         for u in range(2):
@@ -94,7 +94,7 @@ def tile_picked_bellman_none_po_kernel(
             )
 
         a, b, c, d = ORDER
-        y = [sb.tile([P, PAIR * S if t == c else S], F32, name=f"y{t}", tag=f"y{t}", align_bytes=64) for t in range(PACK)]
+        y = [sb.tile([P, PAIR * S if t in (c, d) else S], F32, name=f"y{t}", tag=f"y{t}", align_bytes=64) for t in range(PACK)]
 
         def first_product(t, c0, c1, acc):
             cols = slice(t * M, (t + 1) * M)
@@ -165,9 +165,6 @@ def tile_picked_bellman_none_po_kernel(
         def round_pair(copy, t, c0, c1):
             copy(z_bf[:, c0:c1, t : t + PAIR], y[t][:].rearrange("p (e c) -> p c e", e=PAIR)[:, c0:c1, :])
 
-        def round_plane(copy, t, c0, c1):
-            copy(z_bf[:, c0:c1, t], y[t][:, c0:c1])
-
         fetch_new(a)
         fetch_new(b)
         fetch_old(a)
@@ -190,12 +187,8 @@ def tile_picked_bellman_none_po_kernel(
         nc.scalar.copy(y[c][:, S:], y[a][:])
         put_back(c)
         fetch_old(d)
-        for h in range(2):
-            round_plane(nc.scalar.copy, b, h * HALF, (h + 1) * HALF)
         relax(d)
-        z_last = sb.tile([P, S], F32, name="z_last", align_bytes=64)
-        nc.scalar.copy(z_last[:], y[d][:])
-        y[d] = z_last
+        nc.scalar.copy(y[d][:, S:], y[b][:])
         for c0, c1 in ((0, HALF), (HALF, S - QUARTER // 2)):
             round_pair(nc.scalar.copy, c, c0, c1)
         round_pair(nc.vector.tensor_copy, c, S - QUARTER // 2, S)
@@ -231,9 +224,9 @@ def tile_picked_bellman_none_po_kernel(
 
         eighth = QUARTER // 2
         for c0, c1 in ((0, QUARTER), (QUARTER, HALF), (S - eighth, S)):
-            round_plane(nc.vector.tensor_copy, d, c0, c1)
+            round_pair(nc.vector.tensor_copy, d, c0, c1)
         for c0, c1 in ((HALF, S - QUARTER), (S - QUARTER, S - eighth)):
-            round_plane(nc.scalar.copy, d, c0, c1)
+            round_pair(nc.scalar.copy, d, c0, c1)
         for c0 in range(0, S, QUARTER):
             quantize(z_codes, z_scale, z_flat, c0, c0 + QUARTER)
 

@@ -51,19 +51,19 @@ def tile_picked_bellman_none_po_kernel(
         nc.gpsimd.memset(x_bytes[:SPREAD, :].bitcast(I32), 0)
         picked_bytes = sb.tile([P, S], U8, name="picked_bytes", align_bytes=64)
         nc.gpsimd.memset(picked_bytes[:].bitcast(I32), 0)
-        w2_bytes = sb.tile([P, N], U8, name="w2_bytes", align_bytes=64)
-        nc.gpsimd.memset(w2_bytes[:].bitcast(I32), 0)
         nc.sync.dma_start(offs_t[:], offs)
         nc.scalar.dma_start(x_bytes[SPREAD:, :].bitcast(I32), x_scales[0].bitcast(I32))
         nc.sync.dma_start(w1_raw[:], w1.rearrange("(p j) c -> p j c", j=PACK))
         nc.sync.dma_start(dst_t[:], dst)
-        nc.sync.dma_start(src_t[:], src)
         nc.sync.dma_start(x_codes[:], x_words[0].rearrange("p n t -> p (n t)").bitcast(I32))
+        nc.sync.dma_start(src_t[:], src)
 
         spread_bytes = sb.tile([P, S], U8, name="spread_bytes", align_bytes=64)
         nc.vector.tensor_copy(spread_bytes[:], x_bytes[:].indirect(offs_t[:]))
+        w2_raw = reuse.tile([P, 2 * N], U8, name="w2_raw", offset=0)
+        nc.sync.dma_start(w2_raw[:].bitcast(I32), w2_words[0].bitcast(I32))
         for q in range(QUADS):
-            nc.scalar.dma_start(
+            nc.sync.dma_start(
                 picked_bytes[32 * q : 32 * q + 4, :].bitcast(I32),
                 spread_bytes[SPREAD + 4 * q : SPREAD + 4 * q + 4, :].bitcast(I32),
             )
@@ -72,34 +72,37 @@ def tile_picked_bellman_none_po_kernel(
         w1_scale = sb.tile([P, H], U8, name="w1_scale", align_bytes=64)
         w1_cols = w1_raw[:].rearrange("p j (m t) -> p m j t", t=PACK)
         w1_bf = [sb.tile([P, PAIR * M * PACK], BF16, name=f"w1_bf{u}", align_bytes=64) for u in range(2)]
-        for u in range(2):
-            nc.vector.tensor_copy(
-                w1_bf[u][:].rearrange("p (t m j) -> p m j t", t=PAIR, j=PACK),
-                w1_cols[:, :, :, PAIR * u : PAIR * (u + 1)],
+        for copy, u, m0, m1 in (
+            (nc.vector.tensor_copy, 0, 0, M),
+            (nc.scalar.copy, 1, M // 2, M),
+            (nc.vector.tensor_copy, 1, 0, M // 2),
+        ):
+            copy(
+                w1_bf[u][:].rearrange("p (t m j) -> p m j t", t=PAIR, j=PACK)[:, m0:m1],
+                w1_cols[:, m0:m1, :, PAIR * u : PAIR * (u + 1)],
             )
-        ln_t = reuse.tile([P, PACK, V], F32, name="ln_t", offset=2 * N)
+        ln_t = reuse.tile([P, PACK, V], F32, name="ln_t", offset=3 * N)
         nc.sync.dma_start(ln_t[:], ln.rearrange("(p t) v -> p t v", t=PACK))
-        w2_raw = reuse.tile([P, 2 * N], U8, name="w2_raw", offset=0)
-        nc.sync.dma_start(w2_raw[:].bitcast(I32), w2_words[0].bitcast(I32))
 
         for u in range(2):
             cols = slice(u * PAIR * M, (u + 1) * PAIR * M)
             nc.vector.quantize_mx(out=w1_codes[:, cols].bitcast(FP8X4), scales=w1_scale[:, cols], in_=w1_bf[u][:])
 
         picked_codes = sb.tile([P, S], U32, name="picked_codes", align_bytes=64)
-        for c0 in range(0, S, QUARTER):
+        for h in range(2):
             nc.vector.tensor_copy(
-                picked_codes[:, c0 : c0 + QUARTER],
-                x_codes[:].bitcast(U32).indirect(offs_t[:, c0 // GROUP : (c0 + QUARTER) // GROUP]),
+                picked_codes[:, h * HALF : (h + 1) * HALF],
+                x_codes[:].bitcast(U32).indirect(offs_t[:, h * HALF // GROUP : (h + 1) * HALF // GROUP]),
             )
 
         a, b, c, d = ORDER
         y = [sb.tile([P, PAIR * S if t in (c, d) else S], F32, name=f"y{t}", tag=f"y{t}", align_bytes=64) for t in range(PACK)]
 
-        def first_product(t, c0, c1, acc):
+        def make_y(t, c0, c1, bank, copy):
+            y_acc = ps.tile([M, c1 - c0], F32, name=f"y_acc{bank}", tag=f"bank{bank}")
             cols = slice(t * M, (t + 1) * M)
             nc.tensor.matmul_mx(
-                out=acc,
+                out=y_acc[:],
                 lhsT=w1_codes[:, cols].bitcast(FP8X4),
                 lhsT_scale=w1_scale[:, cols],
                 rhs=picked_codes[:, c0:c1].bitcast(FP8X4),
@@ -107,21 +110,12 @@ def tile_picked_bellman_none_po_kernel(
                 start=True,
                 stop=True,
             )
-
-        def make_y(t, c0, c1, bank, copy):
-            y_acc = ps.tile([M, c1 - c0], F32, name=f"y_acc{bank}", tag=f"bank{bank}")
-            for n0 in range(c0, c1, QUARTER):
-                first_product(t, n0, n0 + QUARTER, y_acc[:, n0 - c0 : n0 - c0 + QUARTER])
             copy(y[t][:, c0:c1], y_acc[:])
 
-        lead = ps.tile([M, HALF], F32, name="lead", tag="bank0")
-        first_product(a, 0, QUARTER, lead[:, :QUARTER])
-        make_y(b, 0, QUARTER, 1, nc.vector.tensor_copy)
-        first_product(a, QUARTER, HALF, lead[:, QUARTER:])
-        nc.scalar.copy(y[a][:, :HALF], lead[:])
-        make_y(a, HALF, S - QUARTER, 2, nc.vector.tensor_copy)
-        make_y(a, S - QUARTER, S, 3, nc.scalar.copy)
-        make_y(b, QUARTER, S, 4, nc.scalar.copy)
+        make_y(a, 0, HALF, 0, nc.scalar.copy)
+        make_y(a, HALF, S - QUARTER, 1, nc.vector.tensor_copy)
+        make_y(a, S - QUARTER, S, 2, nc.scalar.copy)
+        make_y(b, 0, S, 3, nc.scalar.copy)
 
         w2_dealt = sb.tile([P, 2 * N], U8, name="w2_dealt", tag="x_codes", align_bytes=64)
         nc.vector.tensor_copy(
@@ -130,6 +124,8 @@ def tile_picked_bellman_none_po_kernel(
         )
         w2_codes = [w2_dealt[:, 2 * M * t : 2 * M * (t + 1)] for t in range(PACK)]
 
+        w2_bytes = reuse.tile([P, N], U8, name="w2_bytes", offset=2 * N)
+        nc.gpsimd.memset(w2_bytes[:].bitcast(I32), 0)
         for q in range(QUADS):
             nc.sync.dma_start(
                 w2_bytes[32 * q : 32 * q + 4, :].bitcast(I32), w2_scales[0, 4 * q : 4 * q + 4, :].bitcast(I32)

@@ -72,14 +72,10 @@ def tile_picked_bellman_none_po_kernel(
         w1_scale = sb.tile([P, H], U8, name="w1_scale", align_bytes=64)
         w1_cols = w1_raw[:].rearrange("p j (m t) -> p m j t", t=PACK)
         w1_bf = [sb.tile([P, PAIR * M * PACK], BF16, name=f"w1_bf{u}", align_bytes=64) for u in range(2)]
-        for copy, u, m0, m1 in (
-            (nc.vector.tensor_copy, 0, 0, M),
-            (nc.scalar.copy, 1, M // 2, M),
-            (nc.vector.tensor_copy, 1, 0, M // 2),
-        ):
-            copy(
-                w1_bf[u][:].rearrange("p (t m j) -> p m j t", t=PAIR, j=PACK)[:, m0:m1],
-                w1_cols[:, m0:m1, :, PAIR * u : PAIR * (u + 1)],
+        for u in range(2):
+            nc.vector.tensor_copy(
+                w1_bf[u][:].rearrange("p (t m j) -> p m j t", t=PAIR, j=PACK),
+                w1_cols[:, :, :, PAIR * u : PAIR * (u + 1)],
             )
         ln_t = reuse.tile([P, PACK, V], F32, name="ln_t", offset=3 * N)
         nc.sync.dma_start(ln_t[:], ln.rearrange("(p t) v -> p t v", t=PACK))
@@ -263,14 +259,12 @@ def tile_picked_bellman_none_po_kernel(
                 store(0, (q - 1) * QUARTER, (q + 1) * QUARTER)
         store(1, 0, S)
         share = 32
-        for q in range(2):
-            interleave(nc.vector.tensor_copy, q * QUARTER, (q + 1) * QUARTER)
+        interleave(nc.vector.tensor_copy, 0, HALF)
         interleave(nc.scalar.copy, HALF, S - QUARTER)
         interleave(nc.scalar.copy, S - QUARTER, S - QUARTER + share)
         interleave(nc.vector.tensor_copy, S - QUARTER + share, S)
         quantize(out_codes, out_scale, res_flat, 0, HALF)
-        quantize(out_codes, out_scale, res_flat, HALF, S - QUARTER)
-        quantize(out_codes, out_scale, res_flat, S - QUARTER, S)
+        quantize(out_codes, out_scale, res_flat, HALF, S)
         nc.sync.dma_start(out_words, out_codes[:])
         for q in range(QUADS):
             queue = nc.sync if q % 2 else nc.scalar

@@ -181,11 +181,10 @@ def tile_picked_bellman_none_po_kernel(
         fetch_old(d)
         relax(d)
         nc.scalar.copy(y[d][:, S:], y[b][:])
-        for c0, c1 in ((0, HALF), (HALF, S - QUARTER // 2)):
-            round_pair(nc.scalar.copy, c, c0, c1)
+        round_pair(nc.scalar.copy, c, 0, S - QUARTER // 2)
         round_pair(nc.vector.tensor_copy, c, S - QUARTER // 2, S)
-        w2_scale_first = sb.tile([P, M], U8, name="w2_scale_first", tag=f"relaxed{c}", align_bytes=64)
-        nc.vector.tensor_copy(w2_scale_first[:], w2_byte_cols[:, 0, :])
+        w2_scale_first = sb.tile([P, M], U8, name="w2_scale_first", tag=f"old{d}", align_bytes=64)
+        nc.gpsimd.tensor_copy(w2_scale_first[:], w2_byte_cols[:, 0, :])
         w2_scale = [w2_scale_first[:]] + [w2_scale_rest[:, t, :] for t in range(PACK - 1)]
 
         warm = ps.tile([M, S], F32, name="warm", tag="bank7")
@@ -258,16 +257,13 @@ def tile_picked_bellman_none_po_kernel(
             if t1 == PAIR and q % 2:
                 store(0, (q - 1) * QUARTER, (q + 1) * QUARTER)
         store(1, 0, S)
-        share = 32
         interleave(nc.vector.tensor_copy, 0, HALF)
         interleave(nc.scalar.copy, HALF, S - QUARTER)
-        interleave(nc.scalar.copy, S - QUARTER, S - QUARTER + share)
-        interleave(nc.vector.tensor_copy, S - QUARTER + share, S)
+        interleave(nc.vector.tensor_copy, S - QUARTER, S)
         quantize(out_codes, out_scale, res_flat, 0, HALF)
         quantize(out_codes, out_scale, res_flat, HALF, S)
         nc.sync.dma_start(out_words, out_codes[:])
         for q in range(QUADS):
-            queue = nc.sync if q % 2 else nc.scalar
-            queue.dma_start(
+            nc.sync.dma_start(
                 out_2[0, 4 * q : 4 * q + 4, :].bitcast(I32), out_scale[32 * q : 32 * q + 4, :].bitcast(I32)
             )

@@ -26,7 +26,6 @@ HALF = S // 2
 SPREAD = P - 16
 QUARTER = S // 4
 PAIR = 2
-ORDER = (1, 3, 0, 2)
 NARROW = 32
 
 
@@ -91,11 +90,11 @@ def tile_picked_bellman_none_po_kernel(
                 x_codes[:].bitcast(U32).indirect(offs_t[:, h * HALF // GROUP : (h + 1) * HALF // GROUP]),
             )
 
-        a, b, c, d = ORDER
-        y = [sb.tile([P, PAIR * S if t in (c, d) else S], F32, name=f"y{t}", tag=f"y{t}", align_bytes=64) for t in range(PACK)]
+        a, b, c, d = range(PACK)
+        y = [sb.tile([P, S], F32, name=f"y{t}", align_bytes=64) for t in range(PACK)]
 
         def make_y(t, c0, c1, bank, copy):
-            y_acc = ps.tile([M, c1 - c0], F32, name=f"y_acc{bank}", tag=f"bank{bank}")
+            y_acc = ps.tile([M, c1 - c0], F32, name=f"y_acc{t}_{c0}", tag=f"bank{bank}")
             cols = slice(t * M, (t + 1) * M)
             nc.tensor.matmul_mx(
                 out=y_acc[:],
@@ -109,9 +108,9 @@ def tile_picked_bellman_none_po_kernel(
             copy(y[t][:, c0:c1], y_acc[:])
 
         make_y(a, 0, HALF, 0, nc.scalar.copy)
-        make_y(a, HALF, S - QUARTER, 1, nc.vector.tensor_copy)
-        make_y(a, S - QUARTER, S, 2, nc.scalar.copy)
-        make_y(b, 0, S, 3, nc.scalar.copy)
+        make_y(b, 0, HALF, 1, nc.scalar.copy)
+        make_y(a, HALF, S, 2, nc.scalar.copy)
+        make_y(b, HALF, S, 3, nc.vector.tensor_copy)
 
         w2_dealt = sb.tile([P, 2 * N], U8, name="w2_dealt", tag="x_codes", align_bytes=64)
         nc.vector.tensor_copy(
@@ -127,63 +126,59 @@ def tile_picked_bellman_none_po_kernel(
                 w2_bytes[32 * q : 32 * q + 4, :].bitcast(I32), w2_scales[0, 4 * q : 4 * q + 4, :].bitcast(I32)
             )
 
-        def values(name):
-            return sb.tile([P, V], F32, name=name, tag=name, align_bytes=64)
+        def values(name, tag=None):
+            return sb.tile([P, V], F32, name=name, tag=tag or name, align_bytes=64)
 
         old = [values(f"old{t}") for t in range(PACK)]
-        far = {t: values(f"far{t}") for t in (c, d)}
-        new = [values(f"new{t}") for t in range(PACK)]
+        far = values("far")
+        new = {t: values(f"new{t}") for t in (a, b)}
         relaxed = [values(f"relaxed{t}") for t in range(PACK)]
+        z = sb.tile([P, PACK, S], F32, name="z", align_bytes=64)
         z_bf = sb.tile([P, S, PACK], BF16, name="z_bf", align_bytes=64)
 
         def fetch_old(t):
             nc.scalar.activation(old[t][:], y[t][:].indirect(dst_t[:]), COPY)
 
-        def fetch_far(t):
-            nc.scalar.activation(far[t][:], y[t][:].indirect(src_t[:]), COPY)
-
         def fetch_new(t):
             nc.vector.tensor_tensor(new[t][:], y[t][:].indirect(src_t[:]), ln_t[:, t, :], ADD)
-
-        def add_length(t):
-            nc.vector.tensor_tensor(new[t][:], far[t][:], ln_t[:, t, :], ADD)
 
         def relax(t):
             nc.vector.tensor_tensor(relaxed[t][:], old[t][:], new[t][:], MIN)
 
-        def put_back(t):
+        def put_back_vector(t):
             nc.vector.tensor_copy(y[t][:].indirect(dst_t[:]), relaxed[t][:])
 
-        def round_pair(copy, t, c0, c1):
-            copy(z_bf[:, c0:c1, t : t + PAIR], y[t][:].rearrange("p (e c) -> p c e", e=PAIR)[:, c0:c1, :])
+        def put_back_scalar(t):
+            nc.scalar.activation(y[t][:].indirect(dst_t[:]), relaxed[t][:], COPY)
 
         fetch_new(a)
         fetch_new(b)
         fetch_old(a)
-        relax(a)
-        put_back(a)
-        make_y(c, 0, S, 5, nc.scalar.copy)
         fetch_old(b)
+        relax(a)
         relax(b)
-        fetch_far(c)
-        add_length(c)
-        put_back(b)
-        make_y(d, 0, S, 6, nc.scalar.copy)
+        put_back_vector(a)
+        make_y(c, 0, S, 3, nc.scalar.copy)
+        make_y(d, 0, S, 2, nc.scalar.copy)
         fetch_old(c)
-        relax(c)
-        fetch_far(d)
-        add_length(d)
-        w2_byte_cols = w2_bytes[:].rearrange("p (m t) -> p t m", t=PACK)
-        w2_scale_rest = sb.tile([P, PACK - 1, M], U8, name="w2_scale_rest", tag=f"far{d}", align_bytes=64)
-        nc.gpsimd.tensor_copy(w2_scale_rest[:], w2_byte_cols[:, 1:, :])
-        nc.scalar.copy(y[c][:, S:], y[a][:])
-        put_back(c)
+        nc.scalar.activation(far[:], y[c][:].indirect(src_t[:]), COPY)
         fetch_old(d)
+        put_back_scalar(b)
+        nc.sync.dma_start(z[:, a, :], y[a][:])
+        nc.sync.dma_start(z[:, b, :], y[b][:])
+        new[d] = values(f"new{d}", f"new{b}")
+        new[c] = values(f"new{c}", f"relaxed{a}")
+        fetch_new(d)
+        nc.vector.tensor_tensor(new[c][:], far[:], ln_t[:, c, :], ADD)
         relax(d)
-        nc.scalar.copy(y[d][:, S:], y[b][:])
-        round_pair(nc.scalar.copy, c, 0, S - QUARTER // 2)
-        round_pair(nc.vector.tensor_copy, c, S - QUARTER // 2, S)
-        w2_scale_first = sb.tile([P, M], U8, name="w2_scale_first", tag=f"old{d}", align_bytes=64)
+        relax(c)
+        put_back_vector(d)
+        put_back_scalar(c)
+
+        w2_byte_cols = w2_bytes[:].rearrange("p (m t) -> p t m", t=PACK)
+        w2_scale_rest = sb.tile([P, PACK - 1, M], U8, name="w2_scale_rest", tag=f"old{c}", align_bytes=64)
+        nc.gpsimd.tensor_copy(w2_scale_rest[:], w2_byte_cols[:, 1:, :])
+        w2_scale_first = sb.tile([P, M], U8, name="w2_scale_first", tag=f"relaxed{a}", align_bytes=64)
         nc.gpsimd.tensor_copy(w2_scale_first[:], w2_byte_cols[:, 0, :])
         w2_scale = [w2_scale_first[:]] + [w2_scale_rest[:, t, :] for t in range(PACK - 1)]
 
@@ -198,7 +193,6 @@ def tile_picked_bellman_none_po_kernel(
                 start=True,
                 stop=True,
             )
-        put_back(d)
 
         z_codes = sb.tile([P, S], U32, name="z_codes", align_bytes=64)
         z_scale = sb.tile([P, S], U8, name="z_scale", align_bytes=64)
@@ -213,23 +207,29 @@ def tile_picked_bellman_none_po_kernel(
                 out=codes[:, c0:c1].bitcast(FP8X4), scales=scale[:, c0:c1], in_=values[:, c0 * PACK : c1 * PACK]
             )
 
+        def interleave(copy, words, planes, c0, c1):
+            copy(
+                words[:, c0:c1, :].rearrange("p (c i) t -> p c t i", i=4),
+                planes[:, :, c0:c1].rearrange("p t (c i) -> p c t i", i=4),
+            )
+
         eighth = QUARTER // 2
-        for c0, c1 in ((0, QUARTER), (QUARTER, HALF), (S - eighth, S)):
-            round_pair(nc.vector.tensor_copy, d, c0, c1)
-        for c0, c1 in ((HALF, S - QUARTER), (S - QUARTER, S - eighth)):
-            round_pair(nc.scalar.copy, d, c0, c1)
-        for c0 in range(0, S, QUARTER):
-            quantize(z_codes, z_scale, z_flat, c0, c0 + QUARTER)
+        nc.vector.tensor_copy(z[:, d, :HALF], y[d][:, :HALF])
+        nc.vector.tensor_copy(z[:, c, :HALF], y[c][:, :HALF])
+        nc.vector.tensor_copy(z[:, d, HALF:], y[d][:, HALF:])
+        nc.scalar.copy(z[:, c, HALF:], y[c][:, HALF:])
+        interleave(nc.vector.tensor_copy, z_bf, z, 0, QUARTER)
+        interleave(nc.vector.tensor_copy, z_bf, z, QUARTER, HALF)
+        interleave(nc.scalar.copy, z_bf, z, HALF + eighth, S)
+        quantize(z_codes, z_scale, z_flat, 0, QUARTER)
+        quantize(z_codes, z_scale, z_flat, QUARTER, HALF)
+        interleave(nc.vector.tensor_copy, z_bf, z, HALF, HALF + eighth)
+        quantize(z_codes, z_scale, z_flat, HALF, S - QUARTER)
+        quantize(z_codes, z_scale, z_flat, S - QUARTER, S)
 
         res_bf = sb.tile([P, S, PACK], BF16, name="res_bf", align_bytes=64)
         res_flat = res_bf[:].rearrange("p c t -> p (c t)")
         res = sb.tile([P, PACK, S], F32, name="res", align_bytes=64)
-
-        def interleave(copy, c0, c1):
-            copy(
-                res_bf[:, c0:c1, :].rearrange("p (c i) t -> p c t i", i=4),
-                res[:, :, c0:c1].rearrange("p t (c i) -> p c t i", i=4),
-            )
 
         def multiply(acc, t, cols):
             nc.tensor.matmul_mx(
@@ -257,9 +257,9 @@ def tile_picked_bellman_none_po_kernel(
             if t1 == PAIR and q % 2:
                 store(0, (q - 1) * QUARTER, (q + 1) * QUARTER)
         store(1, 0, S)
-        interleave(nc.vector.tensor_copy, 0, HALF)
-        interleave(nc.scalar.copy, HALF, S - QUARTER)
-        interleave(nc.vector.tensor_copy, S - QUARTER, S)
+        interleave(nc.vector.tensor_copy, res_bf, res, 0, HALF)
+        interleave(nc.scalar.copy, res_bf, res, HALF, S - QUARTER)
+        interleave(nc.vector.tensor_copy, res_bf, res, S - QUARTER, S)
         quantize(out_codes, out_scale, res_flat, 0, HALF)
         quantize(out_codes, out_scale, res_flat, HALF, S)
         nc.sync.dma_start(out_words, out_codes[:])

@@ -84,20 +84,19 @@ def tile_picked_bellman_none_po_kernel(
             nc.vector.quantize_mx(out=w1_codes[:, cols].bitcast(FP8X4), scales=w1_scale[:, cols], in_=w1_bf[u][:])
 
         picked_codes = sb.tile([P, S], U32, name="picked_codes", align_bytes=64)
-        for h in range(2):
+        for c0 in range(0, S, QUARTER):
             nc.vector.tensor_copy(
-                picked_codes[:, h * HALF : (h + 1) * HALF],
-                x_codes[:].bitcast(U32).indirect(offs_t[:, h * HALF // GROUP : (h + 1) * HALF // GROUP]),
+                picked_codes[:, c0 : c0 + QUARTER],
+                x_codes[:].bitcast(U32).indirect(offs_t[:, c0 // GROUP : (c0 + QUARTER) // GROUP]),
             )
 
         a, b, c, d = range(PACK)
         y = [sb.tile([P, S], F32, name=f"y{t}", align_bytes=64) for t in range(PACK)]
 
-        def make_y(t, c0, c1, bank, copy):
-            y_acc = ps.tile([M, c1 - c0], F32, name=f"y_acc{t}_{c0}", tag=f"bank{bank}")
+        def project(acc, t, c0, c1):
             cols = slice(t * M, (t + 1) * M)
             nc.tensor.matmul_mx(
-                out=y_acc[:],
+                out=acc,
                 lhsT=w1_codes[:, cols].bitcast(FP8X4),
                 lhsT_scale=w1_scale[:, cols],
                 rhs=picked_codes[:, c0:c1].bitcast(FP8X4),
@@ -105,12 +104,20 @@ def tile_picked_bellman_none_po_kernel(
                 start=True,
                 stop=True,
             )
+
+        def make_y(t, c0, c1, bank, copy):
+            y_acc = ps.tile([M, c1 - c0], F32, name=f"y_acc{t}_{c0}", tag=f"bank{bank}")
+            project(y_acc[:], t, c0, c1)
             copy(y[t][:, c0:c1], y_acc[:])
 
-        make_y(a, 0, HALF, 0, nc.scalar.copy)
-        make_y(b, 0, HALF, 1, nc.scalar.copy)
-        make_y(a, HALF, S, 2, nc.scalar.copy)
-        make_y(b, HALF, S, 3, nc.vector.tensor_copy)
+        early = {t: ps.tile([M, S - QUARTER], F32, name=f"early{t}", tag=f"bank{t}") for t in (a, b)}
+        for c0 in range(0, S - QUARTER, QUARTER):
+            for t in (a, b):
+                project(early[t][:, c0 : c0 + QUARTER], t, c0, c0 + QUARTER)
+        nc.scalar.copy(y[a][:, : S - QUARTER], early[a][:])
+        nc.vector.tensor_copy(y[b][:, : S - QUARTER], early[b][:])
+        make_y(a, S - QUARTER, S, 2, nc.scalar.copy)
+        make_y(b, S - QUARTER, S, 3, nc.vector.tensor_copy)
 
         w2_dealt = sb.tile([P, 2 * N], U8, name="w2_dealt", tag="x_codes", align_bytes=64)
         nc.vector.tensor_copy(
@@ -129,21 +136,21 @@ def tile_picked_bellman_none_po_kernel(
         def values(name, tag=None):
             return sb.tile([P, V], F32, name=name, tag=tag or name, align_bytes=64)
 
-        old = [values(f"old{t}") for t in range(PACK)]
+        z = sb.tile([P, PACK, S], F32, name="z", align_bytes=64)
+        old = {t: values(f"old{t}")[:] for t in range(PACK)}
         far = values("far")
         new = {t: values(f"new{t}") for t in (a, b)}
         relaxed = [values(f"relaxed{t}") for t in range(PACK)]
-        z = sb.tile([P, PACK, S], F32, name="z", align_bytes=64)
         z_bf = sb.tile([P, S, PACK], BF16, name="z_bf", align_bytes=64)
 
         def fetch_old(t):
-            nc.scalar.activation(old[t][:], y[t][:].indirect(dst_t[:]), COPY)
+            nc.scalar.activation(old[t], y[t][:].indirect(dst_t[:]), COPY)
 
         def fetch_new(t):
             nc.vector.tensor_tensor(new[t][:], y[t][:].indirect(src_t[:]), ln_t[:, t, :], ADD)
 
         def relax(t):
-            nc.vector.tensor_tensor(relaxed[t][:], old[t][:], new[t][:], MIN)
+            nc.vector.tensor_tensor(relaxed[t][:], old[t], new[t][:], MIN)
 
         def put_back_vector(t):
             nc.vector.tensor_copy(y[t][:].indirect(dst_t[:]), relaxed[t][:])
@@ -213,19 +220,16 @@ def tile_picked_bellman_none_po_kernel(
                 planes[:, :, c0:c1].rearrange("p t (c i) -> p c t i", i=4),
             )
 
-        eighth = QUARTER // 2
         nc.vector.tensor_copy(z[:, d, :HALF], y[d][:, :HALF])
         nc.vector.tensor_copy(z[:, c, :HALF], y[c][:, :HALF])
         nc.vector.tensor_copy(z[:, d, HALF:], y[d][:, HALF:])
         nc.scalar.copy(z[:, c, HALF:], y[c][:, HALF:])
         interleave(nc.vector.tensor_copy, z_bf, z, 0, QUARTER)
         interleave(nc.vector.tensor_copy, z_bf, z, QUARTER, HALF)
-        interleave(nc.scalar.copy, z_bf, z, HALF + eighth, S)
-        quantize(z_codes, z_scale, z_flat, 0, QUARTER)
-        quantize(z_codes, z_scale, z_flat, QUARTER, HALF)
-        interleave(nc.vector.tensor_copy, z_bf, z, HALF, HALF + eighth)
-        quantize(z_codes, z_scale, z_flat, HALF, S - QUARTER)
-        quantize(z_codes, z_scale, z_flat, S - QUARTER, S)
+        interleave(nc.scalar.copy, z_bf, z, HALF, S - QUARTER)
+        interleave(nc.scalar.copy, z_bf, z, S - QUARTER, S)
+        for c0 in range(0, S, QUARTER):
+            quantize(z_codes, z_scale, z_flat, c0, c0 + QUARTER)
 
         res_bf = sb.tile([P, S, PACK], BF16, name="res_bf", align_bytes=64)
         res_flat = res_bf[:].rearrange("p c t -> p (c t)")

@@ -59,13 +59,13 @@ def tile_picked_bellman_none_po_kernel(
 
         spread_bytes = sb.tile([P, S], U8, name="spread_bytes", align_bytes=64)
         nc.vector.tensor_copy(spread_bytes[:], x_bytes[:].indirect(offs_t[:]))
-        w2_raw = reuse.tile([P, 2 * N], U8, name="w2_raw", offset=0)
-        nc.sync.dma_start(w2_raw[:].bitcast(I32), w2_words[0].bitcast(I32))
         for q in range(QUADS):
             nc.sync.dma_start(
                 picked_bytes[32 * q : 32 * q + 4, :].bitcast(I32),
                 spread_bytes[SPREAD + 4 * q : SPREAD + 4 * q + 4, :].bitcast(I32),
             )
+        w2_raw = reuse.tile([P, 2 * N], U8, name="w2_raw", offset=0)
+        nc.sync.dma_start(w2_raw[:].bitcast(I32), w2_words[0].bitcast(I32))
 
         w1_codes = sb.tile([P, H], U32, name="w1_codes", align_bytes=64)
         w1_scale = sb.tile([P, H], U8, name="w1_scale", align_bytes=64)

@@ -25,6 +25,7 @@ GROUP = 16
 HALF = S // 2
 SPREAD = P - 16
 QUARTER = S // 4
+X_FIRST = T - T // 8
 PAIR = 2
 NARROW = 32
 
@@ -54,7 +55,8 @@ def tile_picked_bellman_none_po_kernel(
         nc.scalar.dma_start(x_bytes[SPREAD:, :].bitcast(I32), x_scales[0].bitcast(I32))
         nc.sync.dma_start(w1_raw[:], w1.rearrange("(p j) c -> p j c", j=PACK))
         nc.sync.dma_start(dst_t[:], dst)
-        nc.sync.dma_start(x_codes[:], x_words[0].rearrange("p n t -> p (n t)").bitcast(I32))
+        x_rows = x_words[0].rearrange("p n t -> p (n t)").bitcast(I32)
+        nc.sync.dma_start(x_codes[:, :X_FIRST], x_rows[:, :X_FIRST])
         nc.sync.dma_start(src_t[:], src)
 
         spread_bytes = sb.tile([P, S], U8, name="spread_bytes", align_bytes=64)
@@ -64,6 +66,7 @@ def tile_picked_bellman_none_po_kernel(
                 picked_bytes[32 * q : 32 * q + 4, :].bitcast(I32),
                 spread_bytes[SPREAD + 4 * q : SPREAD + 4 * q + 4, :].bitcast(I32),
             )
+        nc.sync.dma_start(x_codes[:, X_FIRST:], x_rows[:, X_FIRST:])
         w2_raw = reuse.tile([P, 2 * N], U8, name="w2_raw", offset=0)
         nc.sync.dma_start(w2_raw[:].bitcast(I32), w2_words[0].bitcast(I32))
 
@@ -71,8 +74,8 @@ def tile_picked_bellman_none_po_kernel(
         w1_scale = sb.tile([P, H], U8, name="w1_scale", align_bytes=64)
         w1_cols = w1_raw[:].rearrange("p j (m t) -> p m j t", t=PACK)
         w1_bf = [sb.tile([P, PAIR * M * PACK], BF16, name=f"w1_bf{u}", align_bytes=64) for u in range(2)]
-        for u in range(2):
-            nc.vector.tensor_copy(
+        for u, copy in enumerate((nc.vector.tensor_copy, nc.scalar.copy)):
+            copy(
                 w1_bf[u][:].rearrange("p (t m j) -> p m j t", t=PAIR, j=PACK),
                 w1_cols[:, :, :, PAIR * u : PAIR * (u + 1)],
             )
@@ -165,7 +168,7 @@ def tile_picked_bellman_none_po_kernel(
         relax(a)
         relax(b)
         put_back_vector(a)
-        make_y(c, 0, S, 3, nc.scalar.copy)
+        make_y(c, 0, S, 0, nc.scalar.copy)
         make_y(d, 0, S, 2, nc.scalar.copy)
         fetch_old(c)
         nc.scalar.activation(far[:], y[c][:].indirect(src_t[:]), COPY)

from contextlib import ExitStack

import concourse.mybir as mybir

K, T, S, V, H, N = 512, 2048, 512, 256, 512, 512
FLOPS = 2 * K * H * S + 2 * H * N * S

F32 = mybir.dt.float32
BF16 = mybir.dt.bfloat16
I32 = mybir.dt.int32
U32 = mybir.dt.uint32
U16 = mybir.dt.uint16
U8 = mybir.dt.uint8
FP8X4 = mybir.dt.float8_e4m3fn_x4
FP4X4 = mybir.dt.float4_e2m1fn_x4
ADD = mybir.AluOpType.add
MIN = mybir.AluOpType.min
COPY = mybir.ActivationFunctionType.Copy

P = 128
PACK = 4
QUADS = 4
M = 128
GROUP = 16
HALF = S // 2
SPREAD = P - 16
QUARTER = S // 4
X_FIRST = T - T // 8
PAIR = 2
NARROW = 32


def tile_picked_bellman_none_po_kernel(
    tc, x_words, x_scales, w1, ln, w2_words, w2_scales, offs, src, dst, out_0, out_1, out_2
):
    nc = tc.nc
    with ExitStack() as ctx:
        lists = ctx.enter_context(tc.tile_pool(name="lists", bufs=1))
        sb = ctx.enter_context(tc.tile_pool(name="sb", bufs=1))
        reuse = ctx.enter_context(tc.tile_pool(name="reuse", bufs=1))
        ps = ctx.enter_context(tc.psum_pool(name="ps", bufs=1))

        offs_t = lists.tile([P, S // GROUP], U16, name="offs_t")
        src_t = lists.tile([P, V // GROUP], U16, name="src_t")
        dst_t = lists.tile([P, V // GROUP], U16, name="dst_t")

        x_codes = sb.tile([P, T], I32, name="x_codes", tag="x_codes", align_bytes=64)
        x_bytes = reuse.tile([P, T], U8, name="x_bytes", offset=0)
        w1_raw = sb.tile([P, PACK, H], F32, name="w1_raw", align_bytes=64)

        nc.gpsimd.memset(x_bytes[:SPREAD, :].bitcast(I32), 0)
        picked_bytes = sb.tile([P, S], U8, name="picked_bytes", align_bytes=64)
        nc.gpsimd.memset(picked_bytes[:].bitcast(I32), 0)
        nc.sync.dma_start(offs_t[:], offs)
        nc.scalar.dma_start(x_bytes[SPREAD:, :].bitcast(I32), x_scales[0].bitcast(I32))
        nc.sync.dma_start(w1_raw[:], w1.rearrange("(p j) c -> p j c", j=PACK))
        nc.sync.dma_start(dst_t[:], dst)
        x_rows = x_words[0].rearrange("p n t -> p (n t)").bitcast(I32)
        nc.sync.dma_start(x_codes[:, :X_FIRST], x_rows[:, :X_FIRST])
        nc.sync.dma_start(src_t[:], src)

        spread_bytes = sb.tile([P, S], U8, name="spread_bytes", align_bytes=64)
        nc.vector.tensor_copy(spread_bytes[:], x_bytes[:].indirect(offs_t[:]))
        for q in range(QUADS):
            nc.sync.dma_start(
                picked_bytes[32 * q : 32 * q + 4, :].bitcast(I32),
                spread_bytes[SPREAD + 4 * q : SPREAD + 4 * q + 4, :].bitcast(I32),
            )
        nc.sync.dma_start(x_codes[:, X_FIRST:], x_rows[:, X_FIRST:])
        w2_raw = reuse.tile([P, 2 * N], U8, name="w2_raw", offset=0)
        nc.sync.dma_start(w2_raw[:].bitcast(I32), w2_words[0].bitcast(I32))

        w1_codes = sb.tile([P, H], U32, name="w1_codes", align_bytes=64)
        w1_scale = sb.tile([P, H], U8, name="w1_scale", align_bytes=64)
        w1_cols = w1_raw[:].rearrange("p j (m t) -> p m j t", t=PACK)
        w1_bf = [sb.tile([P, PAIR * M * PACK], BF16, name=f"w1_bf{u}", align_bytes=64) for u in range(2)]
        for u, copy in enumerate((nc.vector.tensor_copy, nc.scalar.copy)):
            copy(
                w1_bf[u][:].rearrange("p (t m j) -> p m j t", t=PAIR, j=PACK),
                w1_cols[:, :, :, PAIR * u : PAIR * (u + 1)],
            )
        ln_t = reuse.tile([P, PACK, V], F32, name="ln_t", offset=3 * N)
        nc.sync.dma_start(ln_t[:], ln.rearrange("(p t) v -> p t v", t=PACK))

        for u in range(2):
            cols = slice(u * PAIR * M, (u + 1) * PAIR * M)
            nc.vector.quantize_mx(out=w1_codes[:, cols].bitcast(FP8X4), scales=w1_scale[:, cols], in_=w1_bf[u][:])

        picked_codes = sb.tile([P, S], U32, name="picked_codes", align_bytes=64)
        for c0 in range(0, S, QUARTER):
            nc.vector.tensor_copy(
                picked_codes[:, c0 : c0 + QUARTER],
                x_codes[:].bitcast(U32).indirect(offs_t[:, c0 // GROUP : (c0 + QUARTER) // GROUP]),
            )

        a, b, c, d = range(PACK)
        y = [sb.tile([P, S], F32, name=f"y{t}", align_bytes=64) for t in range(PACK)]

        def project(acc, t, c0, c1):
            cols = slice(t * M, (t + 1) * M)
            nc.tensor.matmul_mx(
                out=acc,
                lhsT=w1_codes[:, cols].bitcast(FP8X4),
                lhsT_scale=w1_scale[:, cols],
                rhs=picked_codes[:, c0:c1].bitcast(FP8X4),
                rhs_scale=picked_bytes[:, c0:c1],
                start=True,
                stop=True,
            )

        def make_y(t, c0, c1, bank, copy):
            y_acc = ps.tile([M, c1 - c0], F32, name=f"y_acc{t}_{c0}", tag=f"bank{bank}")
            project(y_acc[:], t, c0, c1)
            copy(y[t][:, c0:c1], y_acc[:])

        early = {t: ps.tile([M, S - QUARTER], F32, name=f"early{t}", tag=f"bank{t}") for t in (a, b)}
        for c0 in range(0, S - QUARTER, QUARTER):
            for t in (a, b):
                project(early[t][:, c0 : c0 + QUARTER], t, c0, c0 + QUARTER)
        nc.scalar.copy(y[a][:, : S - QUARTER], early[a][:])
        nc.vector.tensor_copy(y[b][:, : S - QUARTER], early[b][:])
        make_y(a, S - QUARTER, S, 2, nc.scalar.copy)
        make_y(b, S - QUARTER, S, 3, nc.vector.tensor_copy)

        w2_dealt = sb.tile([P, 2 * N], U8, name="w2_dealt", tag="x_codes", align_bytes=64)
        nc.vector.tensor_copy(
            w2_dealt[:].bitcast(U16).rearrange("p (t m) -> p m t", t=PACK),
            w2_raw[:].bitcast(U16).rearrange("p (m t) -> p m t", t=PACK),
        )
        w2_codes = [w2_dealt[:, 2 * M * t : 2 * M * (t + 1)] for t in range(PACK)]

        w2_bytes = reuse.tile([P, N], U8, name="w2_bytes", offset=2 * N)
        nc.gpsimd.memset(w2_bytes[:].bitcast(I32), 0)
        for q in range(QUADS):
            nc.sync.dma_start(
                w2_bytes[32 * q : 32 * q + 4, :].bitcast(I32), w2_scales[0, 4 * q : 4 * q + 4, :].bitcast(I32)
            )

        def values(name, tag=None):
            return sb.tile([P, V], F32, name=name, tag=tag or name, align_bytes=64)

        z = sb.tile([P, PACK, S], F32, name="z", align_bytes=64)
        old = {t: values(f"old{t}")[:] for t in range(PACK)}
        far = values("far")
        new = {t: values(f"new{t}") for t in (a, b)}
        relaxed = [values(f"relaxed{t}") for t in range(PACK)]
        z_bf = sb.tile([P, S, PACK], BF16, name="z_bf", align_bytes=64)

        def fetch_old(t):
            nc.scalar.activation(old[t], y[t][:].indirect(dst_t[:]), COPY)

        def fetch_new(t):
            nc.vector.tensor_tensor(new[t][:], y[t][:].indirect(src_t[:]), ln_t[:, t, :], ADD)

        def relax(t):
            nc.vector.tensor_tensor(relaxed[t][:], old[t], new[t][:], MIN)

        def put_back_vector(t):
            nc.vector.tensor_copy(y[t][:].indirect(dst_t[:]), relaxed[t][:])

        def put_back_scalar(t):
            nc.scalar.activation(y[t][:].indirect(dst_t[:]), relaxed[t][:], COPY)

        fetch_new(a)
        fetch_new(b)
        fetch_old(a)
        fetch_old(b)
        relax(a)
        relax(b)
        put_back_vector(a)
        make_y(c, 0, S, 0, nc.scalar.copy)
        make_y(d, 0, S, 2, nc.scalar.copy)
        fetch_old(c)
        nc.scalar.activation(far[:], y[c][:].indirect(src_t[:]), COPY)
        fetch_old(d)
        put_back_scalar(b)
        nc.sync.dma_start(z[:, a, :], y[a][:])
        nc.sync.dma_start(z[:, b, :], y[b][:])
        new[d] = values(f"new{d}", f"new{b}")
        new[c] = values(f"new{c}", f"relaxed{a}")
        fetch_new(d)
        nc.vector.tensor_tensor(new[c][:], far[:], ln_t[:, c, :], ADD)
        relax(d)
        relax(c)
        put_back_vector(d)
        put_back_scalar(c)

        w2_byte_cols = w2_bytes[:].rearrange("p (m t) -> p t m", t=PACK)
        w2_scale_rest = sb.tile([P, PACK - 1, M], U8, name="w2_scale_rest", tag=f"old{c}", align_bytes=64)
        nc.gpsimd.tensor_copy(w2_scale_rest[:], w2_byte_cols[:, 1:, :])
        w2_scale_first = sb.tile([P, M], U8, name="w2_scale_first", tag=f"relaxed{a}", align_bytes=64)
        nc.gpsimd.tensor_copy(w2_scale_first[:], w2_byte_cols[:, 0, :])
        w2_scale = [w2_scale_first[:]] + [w2_scale_rest[:, t, :] for t in range(PACK - 1)]

        warm = ps.tile([M, S], F32, name="warm", tag="bank7")
        for i in range(3):
            nc.tensor.matmul_mx(
                out=warm[:NARROW, :],
                lhsT=w1_codes[:, :NARROW].bitcast(FP8X4),
                lhsT_scale=w2_scale_first[:, :NARROW],
                rhs=w1_codes[:].bitcast(FP8X4),
                rhs_scale=w1_scale[:],
                start=True,
                stop=True,
            )

        z_codes = sb.tile([P, S], U32, name="z_codes", align_bytes=64)
        z_scale = sb.tile([P, S], U8, name="z_scale", align_bytes=64)
        out_codes = sb.tile([P, S], I32, name="out_codes", align_bytes=64)
        out_scale = sb.tile([P, S], U8, name="out_scale", align_bytes=64)
        z_flat = z_bf[:].rearrange("p c t -> p (c t)")
        out_rows = out_0.rearrange("(p t) c -> p t c", t=PACK)
        out_words = out_1[0].rearrange("p n t -> p (n t)").bitcast(I32)

        def quantize(codes, scale, values, c0, c1):
            nc.vector.quantize_mx(
                out=codes[:, c0:c1].bitcast(FP8X4), scales=scale[:, c0:c1], in_=values[:, c0 * PACK : c1 * PACK]
            )

        def interleave(copy, words, planes, c0, c1):
            copy(
                words[:, c0:c1, :].rearrange("p (c i) t -> p c t i", i=4),
                planes[:, :, c0:c1].rearrange("p t (c i) -> p c t i", i=4),
            )

        nc.vector.tensor_copy(z[:, d, :HALF], y[d][:, :HALF])
        nc.vector.tensor_copy(z[:, c, :HALF], y[c][:, :HALF])
        nc.vector.tensor_copy(z[:, d, HALF:], y[d][:, HALF:])
        nc.scalar.copy(z[:, c, HALF:], y[c][:, HALF:])
        interleave(nc.vector.tensor_copy, z_bf, z, 0, QUARTER)
        interleave(nc.vector.tensor_copy, z_bf, z, QUARTER, HALF)
        interleave(nc.scalar.copy, z_bf, z, HALF, S - QUARTER)
        interleave(nc.scalar.copy, z_bf, z, S - QUARTER, S)
        for c0 in range(0, S, QUARTER):
            quantize(z_codes, z_scale, z_flat, c0, c0 + QUARTER)

        res_bf = sb.tile([P, S, PACK], BF16, name="res_bf", align_bytes=64)
        res_flat = res_bf[:].rearrange("p c t -> p (c t)")
        res = sb.tile([P, PACK, S], F32, name="res", align_bytes=64)

        def multiply(acc, t, cols):
            nc.tensor.matmul_mx(
                out=acc,
                lhsT=w2_codes[t].bitcast(FP4X4),
                lhsT_scale=w2_scale[t],
                rhs=z_codes[:, cols].bitcast(FP8X4),
                rhs_scale=z_scale[:, cols],
                start=True,
                stop=True,
            )

        def store(u, c0, c1):
            planes = slice(PAIR * u, PAIR * (u + 1))
            nc.sync.dma_start(out_rows[:, planes, c0:c1], res[:, planes, c0:c1])

        pieces = [(0, 1, 0), (1, 2, 0), (0, 1, 1), (1, 2, 1), (2, 4, 0), (0, 2, 2), (2, 4, 1), (0, 2, 3), (2, 4, 2), (2, 4, 3)]
        for bank, (t0, t1, q) in enumerate(pieces):
            cols = slice(q * QUARTER, (q + 1) * QUARTER)
            out_acc = ps.tile([M, t1 - t0, QUARTER], F32, name=f"out_acc{bank}", tag=f"bank{bank % 8}")
            for t in range(t0, t1):
                multiply(out_acc[:, t - t0, :], t, cols)
            copy = nc.vector.tensor_copy if t0 == 0 and q > 0 else nc.scalar.copy
            copy(res[:, t0:t1, cols], out_acc[:])
            if t1 == PAIR and q % 2:
                store(0, (q - 1) * QUARTER, (q + 1) * QUARTER)
        store(1, 0, S)
        interleave(nc.vector.tensor_copy, res_bf, res, 0, HALF)
        interleave(nc.scalar.copy, res_bf, res, HALF, S - QUARTER)
        interleave(nc.vector.tensor_copy, res_bf, res, S - QUARTER, S)
        quantize(out_codes, out_scale, res_flat, 0, HALF)
        quantize(out_codes, out_scale, res_flat, HALF, S)
        nc.sync.dma_start(out_words, out_codes[:])
        for q in range(QUADS):
            nc.sync.dma_start(
                out_2[0, 4 * q : 4 * q + 4, :].bitcast(I32), out_scale[32 * q : 32 * q + 4, :].bitcast(I32)
            )
